import numpy as np, ml_dtypes
CORES = [78,86,94,102,110,118]
N = 6
BF = ml_dtypes.bfloat16
W, L, Q, RO, FU, SB, SC = 4096, 128, 2048, 3, 4, 2, 5
def pack(sect, mv, traj, amt, cap):
    return {"sect": np.ascontiguousarray(sect.reshape(N, 128, W)).astype(np.float32).astype(BF), "mv": np.ascontiguousarray(mv.reshape(N, 128, Q)).astype(np.int32),
            "traj": np.ascontiguousarray(traj.reshape(N, 128, L)).astype(np.int32), "amt": np.ascontiguousarray(amt.reshape(N, 128, L)).astype(np.float32).astype(BF),
            "cap": np.ascontiguousarray(cap.reshape(N, 128, 1)).astype(np.int32)}
def parts(rng):
    sect = (rng.random((N, 8, 16, W)) * 256 * rng.choice(np.array([0.5, 0.75, 1.0]), (N, 8, 1, W))).astype(np.int64)
    mv = rng.integers(0, W, (N, 8, 16, Q)); traj = rng.integers(0, W, (N, 8, 16, L))
    amt = (rng.random((N, 8, 16, L)) * rng.choice(np.array([8, 40, 100, 170, 256]), (N, 8, 1, L))).astype(np.int64)
    return sect, mv, traj, amt, rng.integers(230, 331, (N, 8, 16, 1))
def setup_inputs(rng):
    return pack(*parts(rng))
def setup_inputs_spread(rng):
    sect, mv, traj, amt, cap = parts(rng)
    sect = (np.exp2(3 + 5 * rng.random((N, 8, 1, W))) * rng.random((N, 8, 16, W))).astype(np.int64)
    amt = (np.exp2(4 + 4 * rng.random((N, 8, 1, L))) * rng.random((N, 8, 16, L))).astype(np.int64)
    traj = (W * rng.random((N, 8, 16, L)) ** 3).astype(np.int64); mv = (W * rng.random((N, 8, 16, Q)) ** 2).astype(np.int64)
    return pack(sect, mv, traj, amt, rng.integers(160, 401, (N, 8, 16, 1)))
def endmix(rng, n, top):
    k = rng.integers(0, 3, (N, 8, 1, n)); e = rng.integers(0, 2, (N, 8, 16, n))
    return top * np.where(k == 2, e, k)
def setup_inputs_ends(rng):
    sect = endmix(rng, W, 255); amt = endmix(rng, L, 255); mv = endmix(rng, Q, W - 1); traj = (W - 1) * rng.integers(0, 2, (N, 8, 16, L))
    cap = 160 + 240 * rng.integers(0, 2, (N, 8, 16, 1)); cap[:, 0] = 400; cap[:, 6:] = 160
    sect[:, 6, :, 0] = 255; sect[:, 6, :, W - 1] = 255; sect[:, 7, :, 0] = 0; sect[:, 7, :, W - 1] = 255
    amt[:, 6:, :, L - 2:] = 255; amt[:, 6:, :, 0] = 255; amt[:, 6:, :, 1] = 0
    traj[:, 6:, 0, L - 1] = 0; traj[:, 6:, 3, L - 1] = W - 1; traj[:, 6:, 13:, L - 1] = W - 1
    traj[:, 7, :15, L - 2] = 0; traj[:, 7, 15, L - 2] = W - 1; traj[:, 7, :, 1] = 0
    return pack(sect, mv, traj, amt, cap)
def setup_inputs_corners(rng):
    sect, mv, traj, amt, cap = parts(rng)
    c0 = rng.integers(160, 401, (1, 8, 16, 1)); c0[0, 0, 0] = 160; c0[0, 7, 15] = 400
    lo = np.maximum(c0 - 255, 0); hi = np.minimum(c0, 254)
    x0 = lo + (rng.random(c0.shape) * (hi - lo + 1)).astype(np.int64)
    cls = np.arange(W) % 4
    n1 = rng.choice(np.array([FU, FU + 1, 16]), (N, 8, 1, W)); n2 = rng.choice(np.array([0, FU - 1, FU, FU + 1, 16]), (N, 8, 1, W))
    n = np.where(cls == 0, 0, np.where(cls == 1, n1, n2))
    sh = rng.integers(0, 16, (N, 8, 1, W)) * rng.integers(0, 2, (N, 8, 1, W))
    over = (np.arange(16).reshape(1, 1, 16, 1) + sh) % 16 < n
    up = rng.integers(0, 3, (N, 8, 1, W)) * rng.integers(0, 2, (N, 8, 1, W))
    sect = np.where(over, np.minimum(x0 + 1 + up, 255), np.maximum(x0 - up, 0))
    kind = rng.integers(0, 6, (N, 8, 1, L)); kind[..., 0] = 1; kind[..., L - 1] = 2; kind[..., L - 2] = 5
    k = np.arange(16).reshape(1, 1, 16, 1); one = np.ones((N, 8, 16, L), np.int64)
    cl = np.where(kind == 0, 0 * one, np.where(kind == 1, one * (k == 0), np.where(kind == 2, one * (k == 15), np.where(kind == 3, rng.integers(2, 4, one.shape), np.where(kind == 4, rng.integers(0, 4, one.shape), one)))))
    traj = 4 * rng.integers(0, W // 4, (N, 8, 16, L)) + cl
    amt = np.where(kind == 4, amt, c0 - x0)
    mv[..., ::5] = (W - 1) * rng.integers(0, 2, mv[..., ::5].shape)
    return pack(sect, mv, traj, amt, np.broadcast_to(c0, (N, 8, 16, 1)))
def setup_inputs_crowd(rng):
    sect, mv, traj, amt, cap = parts(rng)
    for g in (0, 1, 2):
        sect[:, g] = rng.integers(200, 256, (N, 16, W)); amt[:, g] = rng.integers(170, 256, (N, 16, L))
    cap[:, 1] = rng.integers(300, 331, (N, 16, 1))
    pl = rng.integers(0, W, (N, 8, 1, 1)); pl[0, 0] = W - 1; pl[1, 0] = 0; traj[:, :4] = pl[:, :4]
    few = np.array([0, W - 1, W // 2, 3])
    traj[:, 4] = few[rng.integers(0, 4, (N, 16, L))]; mv[:, 4] = few[rng.integers(0, 4, (N, 16, Q))]
    traj[:, 5] = rng.integers(0, W, (N, 16, 1))
    for q in range(N):
        v = int(rng.integers(0, L)); amt[q, 1, :, v] = 0
        traj[q, 2:4, :, v] = (pl[q, 2:4, 0] + 1 + rng.integers(0, W - 1, (2, 16))) % W
        traj[q, 6] = rng.permutation(W)[:L][None, :]
    return pack(sect, mv, traj, amt, cap)
def setup_inputs_fine(rng):
    sect, mv, traj, amt, cap = parts(rng); o = rng.permutation(8); w4 = W >> 2
    for n, (base, e, share) in enumerate(((215, 20, 0.4), (240, 12, 0.4), (247, 6, 0.1))):
        g = int(o[n]); h = rng.integers(-e, e + 1, (N, 8, W)); x = np.concatenate([base + h, base - h], axis=1)
        x[:, 0] += rng.integers(1, 3, (N, W)) * (rng.random((N, W)) < share)
        x[:, :, :w4] = rng.integers(0, 21, (N, 16, w4))
        sect[:, g] = x; amt[:, g] = rng.integers(250, 256, (N, 16, L)); cap[:, g] = 160
        traj[:, g, 0] = rng.integers(0, w4, (N, L)); traj[:, g, 1:] = rng.integers(w4, W, (N, 15, L))
    for n in (3, 4):
        g = int(o[n]); hot = (rng.permutation(16) < FU).reshape(1, 16, 1)
        sect[:, g] = np.where(hot, rng.integers(200, 256, (N, 16, W)), rng.integers(0, 21, (N, 16, W)))
        amt[:, g] = np.where(hot, rng.integers(120, 256, (N, 16, L)), rng.integers(0, 21, (N, 16, L)))
        cap[:, g] = rng.integers(280, 311, (N, 16, 1))
        for q in range(0, N, 2): amt[q, g, :, int(rng.integers(0, L))] = 0
    for n in (5, 6):
        g = int(o[n]); x = rng.integers(80, 121, (N, 16, W)); x[:, :, 1::2] = rng.integers(0, 21, (N, 16, W >> 1)); sect[:, g] = x
        cap[:, g] = 400; cap[int(rng.integers(0, N)), g] = 160
        traj[:, g] = 2 * rng.integers(0, W >> 1, (N, 16, L))
        for q in range(N):
            traj[q, g, 0] = 2 * rng.permutation(W >> 1)[:L]
            a = rng.integers(100, 119, 16); a[0] += (int(np.sum(a)) + n + 1) & 1
            amt[q, g] = a[np.argsort(rng.random((16, L)), axis=0)]
    return pack(sect, mv, traj, amt, cap)
def check_inputs(d):
    bad = []
    for k, lo, hi in (("sect", 0, 255), ("mv", 0, W - 1), ("traj", 0, W - 1), ("amt", 0, 255), ("cap", 160, 400)):
        v = np.asarray(d[k]).astype(np.float64)
        if not (np.min(v) >= lo and np.max(v) <= hi): bad.append("range of " + k)
        elif not np.all(v == np.floor(v)): bad.append("whole numbers of " + k)
    return bad
def picks(x, ix):
    return np.take_along_axis(x, ix.reshape(8, 1, 16 * L), 2).reshape(8, 16, 16, L)
def full(x, z, c, th):
    return np.add.reduce((x + z[:, :, None, :] > c).astype(np.int64), axis=1) >= th
def reference(sect, mv, traj, amt, cap):
    X = sect.astype(np.float32).astype(np.int64).reshape(N, 8, 16, W); z = amt.astype(np.float32).astype(np.int64).reshape(N, 8, 16, L)
    t = traj.astype(np.int64).reshape(N, 8, 16, L); man = mv.astype(np.int64).reshape(N, 8, 16, Q); cp = cap.astype(np.int64).reshape(N, 8, 16, 1, 1)
    odd = np.zeros((N, 8, 1, 1), np.int64); kk = np.arange(16).reshape(1, 16, 1); shadows = []
    for rnd in range(RO):
        for c, g, s, a in shadows: X[c, g][:, s] = X[c, g][:, s] - a
        shadows = []; th = FU + odd; cut = []; verdict = []
        for r in range(N):
            b = (r + SB) % N; x = picks(X[b], t[r])
            fm = full(np.maximum.accumulate(x, axis=2), z[r], cp[b], th[r])
            j = np.where(np.any(fm, axis=1), np.argmax(fm, axis=1), 16)
            p = np.take_along_axis(t[r], np.minimum(j, 15)[:, None, :], 1)[:, 0]
            lead = np.zeros((8, L), bool)
            for g in range(8):
                i = np.unique(p[g], return_index=True)[1]; lead[g, i] = True
                X[b, g][:, p[g, i]] = np.minimum(X[b, g][:, p[g, i]] + (z[r, g][:, i] >> 2), 255)
            cut.append((j, p, lead))
        for r in range(N):
            c = (r + SC) % N; j, p, lead = cut[r]; y = picks(X[c], t[r])
            fy = full(y, z[r], cp[c], th[r]) & (kk >= j[:, None, :]); refused = np.any(fy, axis=1)
            score = np.add.reduce(np.maximum(y + z[r][:, :, None, :] - cp[c], 0), axis=1)
            m = np.argmax(np.where(fy, score, -1), axis=1)
            tm = np.take_along_axis(t[r], m[:, None, :], 1)
            nn = np.take_along_axis(man[c], tm & (Q - 1), 2)
            ym = np.take_along_axis(y, m[:, None, None, :], 2)[:, :, 0]
            ok = lead & (j < 16) & ~refused
            for g in range(8):
                i = np.flatnonzero(ok[g]); s = p[g, i]; a = z[r, g][:, i] >> 2
                X[c, g][:, s] = np.minimum(X[c, g][:, s] + a, 255); shadows.append((c, g, s, a))
            verdict.append((refused, nn, ym))
        for r in range(N):
            j = cut[r][0]; refused, nn, ym = verdict[r]; rf = refused[:, None, :]
            fw = full(picks(X[r], nn), z[r], cp[r], th[r])
            u = np.add.reduce(z[r], axis=1)[:, None, :]
            t[r] = np.where(rf, np.where((kk >= j[:, None, :]) & ~fw, nn, t[r]), (5 * t[r] + u + 1) & (W - 1))
            z[r] = np.where(rf, (z[r] + ym) >> 1, z[r])
            odd[r] = (np.add.reduce(refused.astype(np.int64), axis=1) & 1).reshape(8, 1, 1)
    return {"ysect": X.reshape(N, 128, W).astype(np.float32).astype(BF), "ytraj": t.reshape(N, 128, L).astype(np.float32), "yamt": z.reshape(N, 128, L).astype(np.float32).astype(BF)}

@@ -1,0 +1,746 @@
+import numpy as np
+from concourse.bass import DstId, RemoteDMATransfer
+from concourse.mybir import AluOpType as A, ActivationFunctionType as F
+
+N, RO, SB, SC = 6, 3, 2, 5
+W, L, Q = 4096, 128, 2048
+DUM, EXT, XW = W, W + L, W + 2 * L
+CH = [(0, 4), (4, 8)]
+CHJ = [(0, 4), (4, 8)]
+COST = {"V": 0.03, "S": 0.07, "cyc": 0.00104, "pe": 0.00052, "gather": 1.56, "link": 2.0, "hop": 0.1, "call": 0.4}
+J_UNITS = [(0, 2, 0), (2, 4, 1), (4, 6, 0), (6, 8, 1)]
+LIM_V = ()
+JB = (0, 1)
+EARLY = 0
+FIRST = 1.0
+STEPS, SLACK, NUDGE = 600, 0.3, 1.0
+LOOK = 0.03
+URGE = {}
+S_CUT, S_HOME = (2, 3, 7), (3, 7)
+ZW = 136
+MAG = 8388608.0
+bf, f32, i32, u16 = "bfloat16", "float32", "int32", "uint16"
+
+
+def sb(n, t):
+    return ("sbuf", [128] + (list(n) if isinstance(n, tuple) else [n]), t)
+
+
+SCRATCH = {
+    "X": sb(XW, bf), "MV": sb(XW, i32), "tr32": sb(128, i32), "cap32": sb(8, i32), "capf": sb(8, f32),
+    "Tuc": sb(384, u16), "Tuj": sb(384, u16), "Tuh": sb(384, u16),
+    "Tfc": sb(384, f32), "Tfj": sb((12, 32), f32), "Tfh": sb(512, f32),
+    "Zc": sb(4 * ZW, bf), "Zj": sb(4 * ZW, bf), "Zh": sb(4 * ZW, bf),
+    "ANc": sb(768, bf), "ANj": sb(768, bf), "ANh": sb(256, bf),
+    "zTc": sb(128, bf), "zTj": sb(128, bf), "zTh": sb(128, bf), "zcl": sb(128, bf), "z5": sb(128, f32),
+    "THc": sb(2048, bf), "THj": sb(2048, bf), "THh": sb(2048, bf),
+    "RAW": sb(2048, bf), "IC": sb(2048, bf), "IM": sb((8, 256), bf), "IH": sb(2048, bf),
+    "AJ": sb((8, 256), bf), "SG": sb((8, 256), bf),
+    "fms": sb(384, bf), "fmh": sb(384, bf), "sos": sb(384, bf), "soj": sb(384, bf),
+    "ocs": sb(24, f32), "ocj": sb(24, f32), "Y": sb(128, f32), "S0": sb(128, f32), "S1": sb(128, f32),
+    "EQ": sb(1024, bf), "po": sb(8, u16), "oc": sb(8, u16), "tc": sb(128, bf),
+    "Town": sb(128, f32), "DT": sb(136, f32), "KS": sb(136, f32), "KM": sb(136, f32), "RR": sb(136, f32),
+    "NU": sb(136, f32), "UU": sb(136, f32), "om": sb(8, u16), "of": sb(8, u16),
+    "Vus": sb(384, u16), "Vuh": sb(384, u16), "aps": sb(384, bf), "aph": sb(384, bf),
+    "SS": sb(128, f32), "r1": sb(128, f32), "r2": sb(128, f32), "acc": sb(8, f32),
+    "par": sb(8, f32), "ftmp": sb(8, f32), "tn": sb(128, i32),
+    "q1": sb(8, f32), "D2": sb(136, f32), "U2": sb(136, f32),
+    "osh": sb(8, u16), "ts": sb(128, bf), "ik": sb(136, i32), "half": sb(8, f32), "Ih": sb(128, f32), "nIh": sb(128, f32),
+    "FA": sb(128, bf), "Vf": sb(128, f32), "up": sb(256, f32), "tt": sb(256, f32),
+    "io": sb(160, i32), "io2": sb(512, i32), "io3": sb(512, i32), "ioc": sb(160, i32), "ioc2": sb(160, i32), "pc": sb(8, i32), "pcf": sb(8, f32),
+    "Iw": sb(160, f32), "IE": sb(160, f32), "IO": sb(160, f32), "nIf": sb(128, f32), "I5": sb(128, f32), "Dm": sb(128, f32),
+    "Ib": sb(128, bf), "n64": sb(128, bf), "n128": sb(128, bf), "p32": sb(128, bf),
+    "BOf": sb(128, f32), "BOb": sb(128, bf), "BO8": sb(128, bf), "SW": sb(144, bf), "E32": sb(512, bf),
+    "M16": sb(256, bf), "dg": sb(128, f32), "OD0": sb(128, bf), "OD1": sb(128, bf), "D0": sb(128, f32), "lf": sb(160, f32),
+    "DUM8": sb(8, f32), "CZ": sb((8, 17), bf), "CK": sb((8, 17), bf), "CE": sb((8, 17), f32), "RST": sb(136, bf),
+    "FL": sb(144, bf), "cA": sb(8, f32), "cB": sb(8, f32), "isS": sb(128, bf),
+    "P0": ("psum", [128, 512], f32), "P1": ("psum", [128, 16, 32], f32), "P2": ("psum", [128, 512], f32), "P3": ("psum", [128, 16, 32], f32),
+    "PZ": ("psum", [128, 16, 32], f32), "PK": ("psum", [128, 16, 32], f32), "PC": ("psum", [128, 512], f32), "PD": ("psum", [128, 512], f32),
+}
+SEMAPHORES = ["V", "S", "P", "G", "sent"] + ["d%d" % i for i in range(16)] + ["m%d" % i for i in range(64)]
+IO_SHAPES = {"sect": [128, W], "mv": [128, Q], "traj": [128, L], "amt": [128, L], "cap": [128, 1],
+             "ysect": [128, W], "ytraj": [128, L], "yamt": [128, L]}
+ALL = slice(None)
+
+
+def ap(name, *idx, rows=ALL):
+    if len(idx) >= 2 and all(isinstance(i, int) for i in idx):
+        idx = (slice(*idx),)
+    return (name, (rows,) + tuple(idx))
+
+
+def ind(win, off):
+    return ("*", win, off)
+
+
+def span(x):
+    shape = SCRATCH[x[0]][1] if x[0] in SCRATCH else IO_SHAPES[x[0]]
+    e = np.arange(int(np.prod(shape[1:]))).reshape(shape[1:])[x[1][1:]]
+    return int(np.min(e)), int(np.max(e)) + 1, int(np.size(e))
+
+
+def is_psum(x):
+    return x[0] in SCRATCH and SCRATCH[x[0]][0] == "psum"
+
+
+def two_bytes(x):
+    return SCRATCH[x[0]][2] in (bf, u16)
+
+
+def plan():
+    ops = []
+    last = {}
+    first = [0]
+
+    def add(eng, kind, args, reads, writes, cost, lat=0.0):
+        me = len(ops)
+        deps = set()
+        for x, wr in [(x, False) for x in reads] + [(x, True) for x in writes]:
+            lo, hi, _ = span(x)
+            if is_psum(x):
+                who, before, now = last.get(x[0], (eng, [], []))
+                if who != eng:
+                    before, now = now, []
+                deps.update(o for (_, _, _, o) in before)
+                deps.update(o for (a, b, w, o) in now if o != me and a < hi and lo < b and (w or wr))
+                if eng == "P" and now:
+                    deps.add(now[-1][3])
+                last[x[0]] = (eng, before, now + [(lo, hi, wr, me)])
+                continue
+            keep = []
+            for (a, b, w, o) in last.get(x[0], []):
+                if o != me and a < hi and lo < b and (w or wr):
+                    deps.add(o)
+                if not (wr and lo <= a and b <= hi):
+                    keep.append((a, b, w, o))
+            last[x[0]] = keep + [(lo, hi, wr, me)]
+        w0 = writes[0]
+        per = {"Tu": 128, "Tf": 128, "fm": 128, "so": 128, "Vu": 128, "ap": 128, "Zc": ZW, "Zj": ZW, "Zh": ZW, "AN": 256, "oc": 8}.get(w0[0][:2], 9999)
+        key = eng + w0[0] + str(span(w0)[0] % per) + (reads[0][0] + reads[-1][0] if eng == "P" else reads[-1][0] if reads and w0[0] in ("X", "po", "RAW") else "")
+        ops.append({"eng": eng, "kind": kind, "args": args, "deps": deps, "cost": cost, "lat": lat, "key": key, "first": first[0]})
+
+    def sides(xs):
+        r = []
+        for x in xs:
+            if isinstance(x, tuple):
+                r += [x[1], x[2]] if x[0] == "*" else [x]
+        return r
+
+    def compute(eng, kind, out, ins, args, per, extra_w=()):
+        fix = COST[eng]
+        if out[0] == "*":
+            add(eng, kind, args, sides(ins) + [out[2]], [out[1]], fix + 16 * span(out[2])[2] * 3.8 * CYC)
+            return
+        n = span(out)[2]
+        if ins and isinstance(ins[0], tuple) and ins[0][0] == "*":
+            per = GA
+        elif eng == "V" and all(two_bytes(x) for x in [out] + sides(ins[:2]) if span(x)[2] > 1):
+            per = per / 2
+        add(eng, kind, args, sides(ins), [out] + list(extra_w), fix + max(64, n * per) * CYC)
+
+    def cp(out, in_):
+        compute("V", "tensor_copy", out, [in_], (out, in_), 1)
+
+    def tt(out, a, b, op):
+        compute("V", "tensor_tensor", out, [a, b], (out, a, b, op), 1 if a[0] == "*" or is_psum(a) or is_psum(b) else 2)
+
+    def ts(out, a, s1, op0, s2=None, op1=None):
+        compute("V", "tensor_scalar", out, [a, s1, s2], (out, a, s1, s2, op0) + ((op1,) if op1 is not None else ()), 1)
+
+    def scan(out, d0, d1, init, op0, op1):
+        compute("V", "tensor_tensor_scan", out, [d0, d1], (out, d0, d1, init, op0, op1), 1)
+
+    def ms(out, v):
+        compute("V", "memset", out, [], (out, v), 1)
+
+    def act(out, in_, func=F.Identity, bias=0.0, scale=1.0, accum=None):
+        compute("S", "activation", out, [in_, bias, scale], (out, in_, func, bias, scale, accum), 1, [accum] if accum else [])
+
+    def mm(out, lhsT, rhs, start=True, stop=True):
+        n = span(rhs)[2]
+        add("P", "matmul", (out, lhsT, rhs, start, stop), [lhsT, rhs], [out], max(64, n) * PCYC * (1 if two_bytes(rhs) else 4))
+
+    def group(out_lhs_rhs):
+        for i, (o, l, r) in enumerate(out_lhs_rhs):
+            mm(o, l, r, i == 0, i == len(out_lhs_rhs) - 1)
+
+    def iota(out, pattern, base, cm):
+        add("G", "iota", (out, pattern, base, cm), [], [out], 0.16 + 2 * span(out)[2] * CYC)
+
+    def dma(queue, out, in_, lat, after=()):
+        add(queue, "dma", (out, in_), [in_], [out], 0.06, lat)
+        ops[-1]["deps"].update(after)
+
+    def send(step, dst, src):
+        add("G", "send", (step % N, dst, src), [src], [dst], COST["call"], LAT + span(src)[2] * (2 if two_bytes(src) else 4) * 0.002)
+
+    CYC, PCYC, GA, LAT = COST["cyc"], COST["pe"], COST["gather"], COST["link"]
+    sel = lambda a: ap("SW", 15 - a, 143 - a)
+    I_b, I_f = ap("Ib"), ap("Iw", 16, 144)
+    col = lambda name, c: ap(name, c, c + 1)
+    bank = lambda j, lo, hi: ap("P%d" % j, slice(lo // 32, hi // 32), ALL) if j % 2 else ap("P%d" % j, lo, hi)
+    Xm, Xw, Xe = ap("X", 0, W), ap("X", 0, EXT), ap("X", 0, XW)
+    zs = lambda who, r: ap("Z" + who, r * ZW, r * ZW + 128)
+    fc = lambda who, r, c: col("Z" + who, r * ZW + 128 + c)
+    cap, ncap, ccap = col("capf", 0), col("capf", 1), col("capf", 2)
+
+    dma("Y", ap("tr32"), ap("traj"), 1.9)
+    dma("S", zs("h", 0), ap("amt"), 1.9)
+    dma("S", col("cap32", 0), ap("cap"), 1.9)
+    dma("Y", Xm, ap("sect"), 4.5)
+    dma("Y", ap("MV", 0, Q), ap("mv"), 4.5, [3])
+    dma("Y", ap("MV", Q, W), ap("mv"), 7.0, [3])
+
+    iota(ap("io"), [[1, 160]], -16, -1)
+    iota(ap("ioc"), [[1, 160]], 0, 0)
+    iota(col("pc", 0), [[0, 1]], 0, 1)
+    iota(ap("io2"), [[1, 32], [0, 16]], 128, -1)
+    ts(col("pc", 1), col("pc", 0), 15, A.bitwise_and)
+    ts(col("pc", 2), col("pc", 0), 4, A.arith_shift_right)
+    ts(col("pc", 3), col("pc", 0), 4, A.arith_shift_right, 1, A.bitwise_and)
+    cp(ap("pcf", 0, 4), ap("pc", 0, 4))
+    ts(col("pcf", 4), col("pcf", 3), -1.0, A.mult, 1.0, A.add)
+    ts(col("pcf", 5), col("pcf", 1), 15.0, A.is_lt)
+    ts(ap("Iw"), ap("io"), 0.0, A.is_equal)
+    act(ap("Ib"), I_f)
+    ts(ap("io3"), ap("io2"), 31, A.bitwise_and)
+    ts(ap("E32"), ap("io3"), 0.0, A.is_equal)
+    ts(ap("ioc2"), ap("ioc"), 4, A.arith_shift_right)
+    ts(ap("BOf"), ap("ioc2", 0, 128), col("pcf", 2), A.is_equal)
+    ms(ap("SW"), 0.0)
+    cp(ap("SW", 15, 143, 16), ap("BOf", 0, 128, 16))
+    ms(ap("M16"), 1.0)
+    ms(ap("M16", 0, 256, 16), 0.0)
+    ms(ap("X", W, XW), 0.0)
+    ts(ap("ioc2"), ap("ioc"), 15, A.bitwise_and)
+    ts(ap("dg"), ap("ioc2", 0, 128), col("pcf", 1), A.is_equal)
+    cp(ap("lf"), ap("ioc"))
+    act(ap("OD0"), ap("dg"), bias=8192.0, scale=-8192.0)
+    act(ap("OD1"), ap("dg"), bias=8192.0, scale=-16384.0)
+    ts(ap("D0"), ap("lf", 0, 128), DUM + 1.0, A.add)
+    tt(ap("D0"), ap("D0"), ap("dg"), A.mult)
+    ts(ap("D0"), ap("D0"), -1.0, A.add)
+    ts(ap("DUM8"), ap("lf", 0, 128, 16), col("pcf", 1), A.add, float(DUM), A.add)
+    tt(ap("Dm"), I_f, ap("Iw", 17, 145), A.subtract)
+    tt(ap("Dm"), ap("Dm"), ap("BOf"), A.mult)
+    act(ap("BOb"), ap("BOf"))
+    act(ap("BO8"), ap("BOf"), scale=8192.0)
+    act(ap("IE"), ap("Iw"), scale=col("pcf", 4))
+    act(ap("IO"), ap("Iw"), scale=col("pcf", 3))
+    act(ap("nIf"), I_f, scale=-1.0)
+    act(ap("I5"), I_f, scale=5.0)
+    act(ap("n64"), I_f, scale=-64.0)
+    act(ap("n128"), I_f, scale=-128.0)
+    act(ap("p32"), I_f, scale=32.0)
+    ms(ap("CZ"), 0.0)
+    ms(ap("CZ", ALL, 0), 100.0)
+    ms(ap("CE"), 0.0)
+    ts(ap("CE", ALL, 0), ap("DUM8"), float(L), A.add)
+    iota(ap("ik"), [[0, 8], [-1, 17]], 17, 0)
+    ts(ap("CK"), ap("ik"), 1.0 / 16, A.mult)
+    ms(ap("CK", ALL, 0), 0.0)
+    act(ap("Ih"), I_f, scale=0.5)
+    act(ap("nIh"), I_f, scale=-0.5)
+    ms(ap("up"), 0.0)
+    ms(ap("D2"), 0.0)
+    cp(ap("D2", 16, 136, 17), ap("DUM8"))
+    ms(col("half", 0), 0.5)
+    ms(ap("RST"), 0.0)
+    ms(ap("RST", 0, 136, 17), -1024.0)
+    ms(ap("FL"), 1.0)
+    ms(ap("FL", 0, 1), 0.0)
+    ms(ap("MV", W, EXT), 0)
+    ms(ap("isS"), 0.0)
+    for b in S_HOME:
+        ms(ap("isS", 16 * b, 16 * b + 16), 1.0)
+    for c, (a_, b_) in enumerate([(0, 0), (-1, -3.5), (2, 23), (-1, 12), (-1, 60), (0, 0), (0, 0), (0, 0)]):
+        if 1 <= c <= 5:
+            hi = 8 if c == 5 else c + 1
+            ms(ap("cA", c, hi), float(a_))
+            ms(ap("cB", c, hi), float(b_))
+    cp(col("cA", 0), col("pcf", 5))
+    ts(col("cB", 0), col("pcf", 5), 5.0, A.mult, -1.0, A.add)
+    cp(cap, col("cap32", 0))
+    ts(ncap, cap, -1.0, A.mult, -0.5, A.add)
+    ts(ccap, cap, -255.0, A.add)
+    ts(col("capf", 3), cap, 1.0, A.add)
+    ms(col("half", 1), -0.5)
+
+    def quarters(an):
+        act(ap("r2"), ap("SS"), bias=MAG - 0.5, scale=0.125)
+        act(ap(an[0], an[1], an[1] + 128), ap("r2"), F.Relu, bias=-MAG)
+        act(ap(an[0], an[1] + 128, an[1] + 256), ap(an[0], an[1], an[1] + 128), bias=255.0, scale=-1.0)
+
+    def send_points(r, c):
+        a, b = 16 * CH[c][0], 16 * CH[c][1]
+        u, f = ap("Tuh", 128 * r + a, 128 * r + b), ap("Tfh", 128 * r + a, 128 * r + b)
+        send(SB, ap("Tuc", 128 * r + a, 128 * r + b), u)
+        send(SB, ap("Tfc", 128 * r + a, 128 * r + b), f)
+        if c == len(CH) - 1:
+            u, f = ap("Tuh", 128 * r, 128 * r + 128), ap("Tfh", 128 * r, 128 * r + 128)
+            send(SC, ap("Tfj", slice(4 * r, 4 * r + 4), ALL), f)
+            send(SC, ap("Tuj", 128 * r, 128 * r + 128), u)
+
+    def transposed(who, z):
+        p = ap("PZ", slice(8, 12), ALL)
+        mm(p, z, I_b)
+        act(ap("zT" + who), p)
+
+    def runs(on_scalar):
+        r = []
+        for j in range(4):
+            s0, s1 = 2 * j in on_scalar, 2 * j + 1 in on_scalar
+            r += [(2 * j, 2 * j + 2, s0)] if s0 == s1 else [(2 * j, 2 * j + 1, s0), (2 * j + 1, 2 * j + 2, s1)]
+        return r
+
+    def spread(who, b0, b1, banks=(0, 1, 2, 3)):
+        j = b0 // 2
+        rows = slice(32 * j, 32 * j + 32)
+        lo, hi = 256 * (b0 - 2 * j), 256 * (b1 - 2 * j)
+        return bank(banks[j % len(banks)], lo, hi), ap("zT" + who, rows=rows), ap("E32", lo, hi, rows=rows)
+
+    def limits(who, on_scalar, banks):
+        for b0, b1, s in runs(on_scalar):
+            if not s:
+                o, l, r_ = spread(who, b0, b1, banks)
+                mm(o, l, r_)
+                if (who, b0) in LIM_V:
+                    ts(ap("TH" + who, 256 * b0, 256 * b1), o, -1.0, A.mult, cap, A.add)
+                else:
+                    act(ap("TH" + who, 256 * b0, 256 * b1), o, bias=cap, scale=-1.0)
+
+    def over(who, on_scalar, offs, r, out):
+        for b0, b1, s in runs(on_scalar):
+            src = ind(Xm, ap(offs, 128 * r + 16 * b0, 128 * r + 16 * b1))
+            o = ap(out, 256 * b0, 256 * b1)
+            first[0] = int(b0 < CH[0][1])
+            if s:
+                raw = ap("RAW", 256 * b0, 256 * b1)
+                act(raw, src)
+                p, l, r_ = spread(who, b0, b1)
+                group([(p, l, r_), (p, I_b, raw)])
+                act(o, p, F.Sign, bias=ncap)
+            else:
+                tt(o, src, ap("TH" + who, 256 * b0, 256 * b1), A.is_gt)
+        first[0] = 0
+
+    cp(ap("Tuh", 0, 128), ap("tr32"))
+    cp(ap("Tfh", 0, 128), ap("tr32"))
+    cp(ap("Zh", 128, ZW), ap("cB"))
+    send(SB, ap("Zc", 0, 128), ap("Zh", 0, 128))
+    cp(ap("Zc", 128, ZW), ap("cB"))
+    send(SB, ap("Tuc", 0, 128), ap("Tuh", 0, 128))
+    send(SB, ap("Tfc", 0, 128), ap("Tfh", 0, 128))
+    send(SC, ap("Zj", 0, 128), ap("Zh", 0, 128))
+    cp(ap("Zj", 128, ZW), ap("cB"))
+    act(ap("SS"), zs("h", 0), bias=0.5, scale=2.0)
+    quarters(("ANh", 0))
+    send(SB, ap("ANc", 0, 256), ap("ANh"))
+    send(SC, ap("Tuj", 0, 128), ap("Tuh", 0, 128))
+    send(SC, ap("Tfj", slice(0, 4), ALL), ap("Tfh", 0, 128))
+    send(SC, ap("ANj", 0, 256), ap("ANh"))
+
+    def judge_points(r):
+        seg = slice(4 * r, 4 * r + 4)
+        for h, (m0, m1) in enumerate([(ap("IE", 16, 144), ap("IE", 0, 128)), (ap("IO", 32, 160), ap("IO", 16, 144))]):
+            o = ap("PK", slice(8, 12), slice(16 * h, 16 * h + 16))
+            group([(o, m0, ap("Tfj", seg, slice(0, 16))), (o, m1, ap("Tfj", seg, slice(16, 32)))])
+        compute("V", "transpose", ap("Town"), [ap("PK", slice(8, 12), ALL)], (ap("Town"), ap("PK", slice(8, 12), ALL)), 1)
+        group([(ap("PK", slice(8, 16), slice(0, 17)), I_f, ap("CE")), (ap("PK", slice(8, 16), slice(1, 17)), I_f, ap("Town")),
+               (ap("PK", slice(8, 16), slice(0, 16)), ap("nIf"), ap("Town"))])
+        act(ap("DT"), ap("PK", slice(8, 16), slice(0, 17)))
+        group([(bank(3, 0, 128), ap("I5"), ap("Tfj", seg, ALL)), (bank(3, 0, 128), ap("BOb"), zs("j", r))])
+        ts(ap("tn"), bank(3, 0, 128), 1.0, A.add)
+        ts(ap("MV", EXT, XW), ap("tn"), W - 1, A.bitwise_and)
+        act(ap("X", EXT, XW), zs("j", r))
+        act(ap("z5"), zs("j", r), bias=0.5)
+
+    def judge_limits(r):
+        ts(ap("zcl"), zs("j", r), ccap, A.max, col("capf", 3), A.min)
+        transposed("j", ap("zcl"))
+        limits("j", (), JB)
+
+    for r in range(RO):
+        R = 128 * r
+        if not r:
+            transposed("c", zs("c", r))
+            limits("c", S_CUT, (0, 1, 2, 3))
+        over("c", S_CUT, "Tuc", r, "IC")
+        judge_points(r)
+        if not (r and EARLY):
+            judge_limits(r)
+        transposed("h", zs("h", r))
+        mm(ap("PD", 128, 256), ap("Dm"), ap("Tfc", R, R + 128))
+        for b in range(8):
+            scan(ap("IM", b, ALL), ap("M16"), ap("IC", 256 * b, 256 * b + 256), 0.0, A.mult, A.max)
+        for b0, b1 in CH:
+            group([(ap("PC", 16 * b0, 16 * b1), sel(k), ap("IM", slice(b0, b1), slice(k, 256, 16))) for k in range(16)])
+        fm = ap("fms", R, R + 128)
+        ts(fm, ap("PC", 0, 128), fc("c", r, 0), A.is_ge)
+        tt(ap("Y"), ap("PD", 128, 256), fm, A.mult)
+        group([(ap("P2", 0, 128), I_b, ap("OD0")), (ap("P2", 0, 128), ap("BOf"), ap("Y"))])
+        mm(ap("PC", 256, 384), ap("BOf"), ap("Y"))
+        scan(ap("S0"), ap("D0"), ap("P2", 0, 128), -1.0, A.max, A.min)
+        mm(ap("PD", 0, 128), I_b, ap("OD1"), True, False)
+        mm(ap("PD", 0, 128), ap("BOf"), ap("Y"), False, False)
+        for s in range(8):
+            e = ap("EQ", 128 * s + 16 * s, 128 * s + 128)
+            tt(e, ap("PC", 256 + 16 * s, 384), ap("S0", 0, 128 - 16 * s), A.is_equal)
+            mm(ap("PD", 16 * s, 128), ap("BO8"), e, False, s == 7)
+        cp(ap("po"), ap("S0", 15, 128, 16))
+        tt(ap("tc"), ind(Xm, ap("po")), ap("ANc", 256 * r + 128, 256 * r + 256), A.min)
+        scan(ap("S1"), ap("D0"), ap("PD", 0, 128), -1.0, A.max, A.min)
+        cp(ap("oc"), ap("S1", 15, 128, 16))
+        tt(ind(Xw, ap("oc")), ap("tc"), ap("ANc", 256 * r, 256 * r + 128), A.add)
+        group([(ap("PZ", slice(8, 16), slice(0, 16)), sel(a), ap("IM", ALL, slice(16 * a, 16 * a + 16))) for a in range(16)])
+        act(ap("sos", R, R + 128), ap("PZ", slice(8, 16), slice(0, 16)), F.Sign, bias=fc("c", r, 1))
+        send(SC - SB, ap("soj", R, R + 128), ap("sos", R, R + 128))
+        act(ap("ocs", 8 * r, 8 * r + 8), ap("S1", 15, 128, 16))
+        send(SC - SB, ap("ocj", 8 * r, 8 * r + 8), ap("ocs", 8 * r, 8 * r + 8))
+        send(-SB, ap("fmh", R, R + 128), fm)
+
+        for c, (b0, b1) in enumerate(CHJ):
+            bs, a, b = slice(b0, b1), 16 * b0, 16 * b1
+            first[0] = 1 - c
+            for x0, x1, on_vector in [u for u in J_UNITS if b0 <= u[0] < b1]:
+                d = ap("RAW", 256 * x0, 256 * x1)
+                tt(d, ind(Xm, ap("Tuj", R + 16 * x0, R + 16 * x1)), ap("THj", 256 * x0, 256 * x1), A.subtract)
+                act(ap("SG", slice(x0, x1), ALL), d, F.Sign, bias=col("half", 1))
+                if on_vector:
+                    ts(ap("AJ", slice(x0, x1), ALL), d, 0.0, A.max)
+                else:
+                    act(ap("AJ", slice(x0, x1), ALL), d, F.Relu)
+            in16 = slice(1, 17)
+            pk, pz = ("P1", "P3") if c else ("PK", "PZ")
+            group([(ap(pk, bs, slice(0, 17)), I_b, ap("CK", bs, ALL))] +
+                  [(ap(pk, bs, in16), sel(x), ap("AJ", bs, slice(16 * x, 16 * x + 16))) for x in range(16)])
+            group([(ap(pz, bs, slice(0, 17)), I_b, ap("CZ", bs, ALL)), (ap(pz, bs, in16), ap("p32"), ap("soj", R + a, R + b))] +
+                  [(ap(pz, bs, in16), sel(x), ap("SG", bs, slice(16 * x, 16 * x + 16))) for x in range(16)])
+            w = lambda name: ap(name, 17 * b0, 17 * b1)
+            act(w("KS"), ap(pk, bs, slice(0, 17)), bias=fc("j", r, 2), scale=1.0 / 8192)
+            tt(w("KM"), ap(pz, bs, slice(0, 17)), w("KS"), A.min)
+            scan(w("RR"), w("RST"), w("KM"), 0.0, A.add, A.max)
+            tt(w("NU"), w("KM"), w("RR"), A.is_lt)
+            scan(w("UU"), w("NU"), w("DT"), 0.0, A.mult, A.add)
+            tm = ap("UU", 17 * b0 + 16, 17 * b1, 17)
+            cp(ap("om", b0, b1), tm)
+            cp(ap("Vus", R + a, R + b), ind(ap("MV"), ap("om", b0, b1)))
+            send(-SC, ap("Vuh", R + a, R + b), ap("Vus", R + a, R + b))
+            ts(ap("of", b0, b1), tm, EXT - 1.0, A.subtract)
+            act(ap("aps", R + a, R + b), ind(ap("FL"), ap("of", b0, b1)), accum=col("acc", c))
+            send(-SC, ap("aph", R + a, R + b), ap("aps", R + a, R + b))
+            tt(ap("SS", a, b), ind(Xe, ap("om", b0, b1)), ap("z5", a, b), A.add)
+        first[0] = 0
+        limits("h", S_HOME, (0, 2))
+        act(ap("q1"), ap("soj", R + 15, R + 128, 16), bias=4096.0, scale=-4096.0)
+        group([(ap("PD", 0, 8), ap("nIf"), ap("DUM8")), (ap("PD", 0, 8), I_f, ap("ocj", 8 * r, 8 * r + 8)), (ap("PD", 0, 8), I_f, ap("q1"))])
+        ts(ap("D2", 0, 136, 17), ap("PD", 0, 8), 0.0, A.min)
+        cp(ap("po"), ap("ocj", 8 * r, 8 * r + 8))
+        tt(ap("ts"), ind(Xw, ap("po")), ap("ANj", 256 * r + 128, 256 * r + 256), A.min)
+        scan(ap("U2"), ap("NU"), ap("D2"), 0.0, A.mult, A.add)
+        cp(ap("osh"), ap("U2", 16, 136, 17))
+        tt(ind(Xw, ap("osh")), ap("ts"), ap("ANj", 256 * r, 256 * r + 128), A.add)
+        act(ap("r1"), ap("SS"), bias=MAG - 0.5, scale=0.5)
+        act(zs("j", r + 1), ap("r1"), F.Relu, bias=-MAG)
+        n0 = (r + 1) * ZW
+        if r + 1 < RO:
+            cnt = col("acc", 0)
+            if len(CHJ) == 2:
+                cnt = col("par", 0)
+                act(cnt, col("acc", 0), bias=col("acc", 1))
+            act(col("par", 1), cnt, bias=1.5 * MAG, scale=0.5)
+            act(col("par", 2), col("par", 1), bias=-1.5 * MAG)
+            act(col("par", 3), col("par", 2), F.Abs, bias=cnt, scale=-2.0)
+            act(ap("ftmp"), ap("cA"), scale=col("par", 3))
+            send(SB - SC, zs("c", r + 1), zs("j", r + 1))
+            tt(ap("Zj", n0 + 128, n0 + ZW), ap("ftmp"), ap("cB"), A.add)
+            send(SB - SC, ap("Zc", n0 + 128, n0 + ZW), ap("Zj", n0 + 128, n0 + ZW))
+            quarters(("ANj", 256 * (r + 1)))
+            send(-SC, ap("Zh", n0, n0 + ZW), ap("Zj", n0, n0 + ZW))
+            send(SB - SC, ap("ANc", 256 * (r + 1), 256 * (r + 2)), ap("ANj", 256 * (r + 1), 256 * (r + 2)))
+        else:
+            send(-SC, zs("h", RO), zs("j", RO))
+            dma("Y", ap("ysect"), Xm, 4.5)
+            dma("Y", ap("yamt"), zs("h", RO), 2.0)
+
+        ts(ap("FA"), ap("isS"), fc("h", r, 3), A.mult, fc("h", r, 4), A.add)
+        over("h", S_HOME, "Vuh", r, "IH")
+        if r + 1 < RO:
+            transposed("c", zs("c", r + 1))
+            limits("c", S_CUT, (0, 1))
+        for c, (b0, b1) in enumerate(CH):
+            a, b = 16 * b0, 16 * b1
+            old, vf, bk = ap("Tfh", R + a, R + b), ap("Vf", a, b), "P2" if c else "PD"
+            first[0] = 1 - c
+            cp(vf, ap("Vuh", R + a, R + b))
+            group([(ap(bk, 2 * a, 2 * b, 2), ap("Ih"), old), (ap(bk, 2 * a, 2 * b, 2), ap("nIh"), vf)])
+            group([(ap(bk, 2 * a + 1, 2 * b, 2), ap("Ih"), old), (ap(bk, 2 * a + 1, 2 * b, 2), ap("Ih"), vf)])
+            o = ap("PK", slice(b0 // 2, b1 // 2), ALL) if c else ap("PC", 128 + a, 128 + b)
+            group([(o, I_b, ap("FA", a, b)), (o, ap("n64"), ap("fmh", R + a, R + b)), (o, ap("n128"), ap("aph", R + a, R + b))] +
+                  [(o, sel(k), ap("IH", 16 * a + k, 16 * b, 16)) for k in range(16)])
+            act(ap("up", 2 * a + 1, 2 * b, 2), o, F.Sign, bias=col("half", 0))
+            scan(ap("tt", 2 * a, 2 * b), ap("up", 2 * a, 2 * b), ap(bk, 2 * a, 2 * b), 0.0, A.mult, A.add)
+            new = ap("Tfh", R + 128 + a, R + 128 + b)
+            if r + 1 < RO:
+                cp(ap("Tuh", R + 128 + a, R + 128 + b), ap("tt", 2 * a + 1, 2 * b, 2))
+            act(new, ap("tt", 2 * a + 1, 2 * b, 2))
+            if r + 1 < RO:
+                send_points(r + 1, c)
+            else:
+                dma("S" if c else "Y", ap("ytraj", a, b), new, 2.0)
+        first[0] = 0
+        if r + 1 < RO and EARLY:
+            judge_limits(r + 1)
+        if r + 1 < RO:
+            cp(ind(Xw, ap("osh")), ap("ts"))
+    return ops
+
+
+def order(ops):
+    n = len(ops)
+    users = [[] for _ in range(n)]
+    for i, o in enumerate(ops):
+        for d in o["deps"]:
+            users[d].append(i)
+    hop = lambda d, i: 0.0 if ops[d]["eng"] == ops[i]["eng"] == "P" else COST["hop"]
+    way = [0.0] * n
+    for i in range(n - 1, -1, -1):
+        way[i] = ops[i]["cost"] + ops[i]["lat"] + max([way[u] + hop(i, u) for u in users[i]], default=0.0)
+    way = [w + URGE.get(o["key"], 0.0) + FIRST * o["first"] for o, w in zip(ops, way)]
+    left = [len(o["deps"]) for o in ops]
+    ready, end, free = [0.0] * n, [0.0] * n, {}
+    pool = {}
+    for i in range(n):
+        if not left[i]:
+            pool.setdefault(ops[i]["eng"], []).append(i)
+    seq = []
+    while len(seq) < n:
+        best = None
+        for e, cand in pool.items():
+            if cand:
+                t = max(free.get(e, 0.0), min(ready[i] for i in cand))
+                i = max((i for i in cand if ready[i] <= t + LOOK), key=lambda i: (way[i], -i))
+                soon = [j for j in cand if t + LOOK < ready[j] < t + ops[i]["cost"]]
+                if soon:
+                    j = max(soon, key=lambda j: way[j])
+                    if max(ready[j] + way[j], ready[j] + ops[j]["cost"] + way[i]) < max(t + way[i], t + ops[i]["cost"] + way[j]):
+                        i, t = j, ready[j]
+                if best is None or t < best[0]:
+                    best = (t, e, i)
+        t, e, i = best
+        t = max(t, ready[i])
+        pool[e].remove(i)
+        free[e] = t + ops[i]["cost"]
+        end[i] = free[e] + ops[i]["lat"]
+        seq.append((i, t))
+        for u in users[i]:
+            ready[u] = max(ready[u], end[i] + hop(i, u))
+            left[u] -= 1
+            if not left[u]:
+                pool.setdefault(ops[u]["eng"], []).append(u)
+    return seq, max(end)
+
+
+def polish(ops, seq, steps):
+    n = len(ops)
+    eng = [o["eng"] for o in ops]
+    cost = [o["cost"] for o in ops]
+    users = [[] for _ in range(n)]
+    for i, o in enumerate(ops):
+        for d in o["deps"]:
+            users[d].append((i, o["cost"] * 0 + ops[d]["cost"] + ops[d]["lat"] + (0.0 if eng[d] == eng[i] == "P" else COST["hop"])))
+    need = [len(o["deps"]) for o in ops]
+    qs = {}
+    for i, _ in seq:
+        qs.setdefault(eng[i], []).append(i)
+
+    def times():
+        left, start, by, nxt = need[:], [0.0] * n, [-1] * n, [-1] * n
+        for q in qs.values():
+            for a, b in zip(q, q[1:]):
+                nxt[a] = b
+                left[b] += 1
+        todo = [i for i in range(n) if not left[i]]
+        for i in todo:
+            s = start[i]
+            for u, d in users[i]:
+                if s + d > start[u]:
+                    start[u], by[u] = s + d, i
+                left[u] -= 1
+                if not left[u]:
+                    todo.append(u)
+            u = nxt[i]
+            if u >= 0:
+                if s + cost[i] > start[u]:
+                    start[u], by[u] = s + cost[i], i
+                left[u] -= 1
+                if not left[u]:
+                    todo.append(u)
+        if len(todo) < n:
+            return 1e9, None, None
+        i = max(range(n), key=lambda i: start[i] + cost[i] + ops[i]["lat"])
+        t, held = start[i] + cost[i] + ops[i]["lat"], []
+        while by[i] >= 0:
+            if nxt[by[i]] == i and by[i] not in ops[i]["deps"]:
+                held.append((by[i], i))
+            i = by[i]
+        return t, held, start
+
+    x = [12345]
+
+    def draw(k):
+        x[0] = (x[0] * 6364136223846793005 + 1442695040888963407) % (1 << 64)
+        return (x[0] >> 33) % k
+
+    cur, held, start = times()
+    best, keep = cur, start
+    for it in range(steps):
+        a, b = held[draw(len(held))]
+        q = qs[eng[a]]
+        p, far = q.index(a), (0, 0, 1, 2, 4, 8)[draw(6)]
+        old = q[:]
+        if draw(2):
+            q.insert(max(0, p - far), q.pop(p + 1))
+        else:
+            q.insert(p + 1 + far, q.pop(p))
+        t, h, s = times()
+        if t <= cur + SLACK * (1 - it / steps) * draw(100) / 100:
+            cur, held = t, h
+            if t < best:
+                best, keep = t, s
+        else:
+            q[:] = old
+    return sorted(((i, keep[i]) for i in range(n)), key=lambda p: (p[1], p[0])), best
+
+
+def squeeze(ops, seq, turns):
+    n = len(ops)
+    cost, lat, eng = [o["cost"] for o in ops], [o["lat"] for o in ops], [o["eng"] for o in ops]
+    hop = lambda d, i: 0.0 if eng[d] == eng[i] == "P" else COST["hop"]
+    fwd = [[(d, cost[d] + lat[d] + hop(d, i)) for d in o["deps"]] for i, o in enumerate(ops)]
+    bwd = [[] for _ in range(n)]
+    for i, o in enumerate(ops):
+        for d in o["deps"]:
+            bwd[d].append((i, cost[i] + lat[d] + hop(d, i)))
+
+    def pack(rank, before, least):
+        left = [len(b) for b in before]
+        after = [[] for _ in range(n)]
+        for i, b in enumerate(before):
+            for d, _ in b:
+                after[d].append(i)
+        free = sorted((rank[i], i) for i in range(n) if not left[i])
+        at, busy = [0.0] * n, {}
+        while free:
+            i = free.pop(0)[1]
+            t = max([least[i]] + [at[d] + w for d, w in before[i]])
+            b = busy.setdefault(eng[i], [])
+            k = len(b)
+            while k and b[k - 1][1] > t:
+                k -= 1
+            while k < len(b) and b[k][0] < t + cost[i] - 1e-9:
+                t = max(t, b[k][1])
+                k += 1
+            b.insert(k, (t, t + cost[i]))
+            at[i] = t
+            for u in after[i]:
+                left[u] -= 1
+                if not left[u]:
+                    free.append((rank[u], u))
+            free.sort()
+        return at
+
+    x, at, best, keep = 777, [0.0] * n, 1e9, None
+    for i, t in seq:
+        at[i] = t
+    keys = sorted(set(o["key"] for o in ops))
+    for it in range(turns):
+        nudge = {}
+        for k in keys:
+            x = (x * 6364136223846793005 + 1442695040888963407) % (1 << 64)
+            nudge[k] = NUDGE * ((x >> 33) % 1000 / 1000 - 0.5) if (x >> 20) % 8 == 0 else 0.0
+        back = pack([-(at[i] + cost[i]) + nudge[ops[i]["key"]] for i in range(n)], bwd, lat)
+        now = pack([-(back[i] + cost[i]) for i in range(n)], fwd, [0.0] * n)
+        t = max(now[i] + cost[i] + lat[i] for i in range(n))
+        if t < best + SLACK:
+            at = now
+        if t < best:
+            best, keep = t, now
+    return sorted(((i, keep[i]) for i in range(n)), key=lambda p: (p[1], p[0])), best
+
+
+CACHE = {}
+
+
+def rank_program(g, core, T, topo):
+    rank = T.rank_of(core)
+    if rank is None:
+        return
+    if not CACHE:
+        CACHE["ops"] = plan()
+        CACHE["seq"] = squeeze(CACHE["ops"], order(CACHE["ops"])[0], STEPS)[0]
+    ops, seq = CACHE["ops"], CACHE["seq"]
+    queue = {"V": g.vector, "S": g.scalar, "P": g.tensor, "G": g, "Y": g.sync}
+
+    def res(x):
+        if not isinstance(x, tuple):
+            return x
+        if x[0] == "*":
+            return res(x[1]).indirect(res(x[2]))
+        return T[x[0]][x[1]]
+
+    token, count, waited = {}, {"V": 0, "S": 0, "P": 0, "G": 0}, {}
+    nd, nm, sent = 0, 0, 0
+    for i, _ in seq:
+        o = ops[i]
+        e, q, a = o["eng"], queue[o["eng"]], o["args"]
+        need = {}
+        for d in o["deps"]:
+            if not (e == "P" and ops[d]["eng"] == "P"):
+                for s, v in token[d]:
+                    need[s] = max(need.get(s, 0), v)
+        for s, v in need.items():
+            if waited.get((e, s), 0) < v:
+                q.wait_ge(T.sem[s], v)
+                waited[(e, s)] = v
+        k = o["kind"]
+        if k == "dma":
+            token[i] = [("d%d" % nd, 16)]
+            q.dma_start(res(a[0]), res(a[1])).then_inc(T.sem["d%d" % nd], 16)
+            nd += 1
+        elif k == "send":
+            dst, src = T.cores[(rank + a[0]) % N], T.cores[(rank - a[0]) % N]
+            rid, pid, _ = topo.addr(dst)
+            g.remote_dma(res(a[1]), res(a[2]), T.sem["m%d" % nm], T.sem.sent, pid, rid, topo.mask(core, dst))
+            token[i] = [("m%d" % nm, len(topo.engines(src, core)))]
+            sent += len(topo.engines(core, dst))
+            nm += 1
+        else:
+            r = [res(x) for x in a]
+            if k == "activation":
+                ins = q.activation(r[0], r[1], r[2], bias=r[3], scale=r[4], accum_out=r[5])
+            elif k == "matmul":
+                ins = q.matmul(*r)
+            elif k == "iota":
+                ins = q.iota(*r)
+            elif k == "tensor_copy":
+                ins = q.tensor_copy(*r)
+            elif k == "tensor_tensor":
+                ins = q.tensor_tensor(*r)
+            elif k == "tensor_scalar":
+                ins = q.tensor_scalar(*r)
+            elif k == "tensor_tensor_scan":
+                ins = q.tensor_tensor_scan(*r)
+            elif k == "transpose":
+                ins = q.transpose(*r)
+            else:
+                ins = q.memset(*r)
+            count[e] += 1
+            ins.then_inc(T.sem[e], 1)
+            token[i] = [(e, count[e])]
+    for e, v in count.items():
+        g.wait_ge(T.sem[e], v)
+    g.wait_ge(T.sem.sent, sent)
+    for i, o in enumerate(ops):
+        if o["kind"] in ("dma", "send"):
+            g.wait_ge(T.sem[token[i][0][0]], token[i][0][1])

@@ -5,21 +5,22 @@ from concourse.mybir import AluOpType as A, ActivationFunctionType as F
 N, RO, SB, SC = 6, 3, 2, 5
 W, L, Q = 4096, 128, 2048
 DUM, EXT, XW = W, W + L, W + 2 * L
-CH = [(0, 4), (4, 8)]
-CHJ = [(0, 4), (4, 8)]
-COST = {"V": 0.03, "S": 0.07, "cyc": 0.00104, "pe": 0.00052, "gather": 1.56, "link": 2.0, "hop": 0.1, "call": 0.4}
-J_UNITS = [(0, 2, 0), (2, 4, 1), (4, 6, 0), (6, 8, 1)]
-LIM_V = ()
-JB = (0, 1)
-EARLY = 0
-FIRST = 1.0
-STEPS, SLACK, NUDGE = 600, 0.3, 1.0
+COST = {"V": 0.03, "S": 0.07, "cyc": 0.00086, "pe": 0.00045, "gather": 1.56, "scatter": 3.8, "link": 2.0, "hop": 0.2, "call": 0.4, "byte": 0.002, "P": 0.0}
+CFG = {
+    "cut": [(1, 2, "S", 3), (0, 1, "A", 0), (4, 6, "T", 2), (2, 4, "T", 1), (6, 8, "S", 2)],
+    "judge": [(0, 2, "T", 0), (2, 3, "S", 1), (3, 4, "T", 2), (6, 7, "S", 0), (4, 6, "S", 3), (7, 8, "S", 2)],
+    "home": [(2, 3, "T", 1), (4, 6, "T", 0), (0, 2, "T", 0), (6, 7, "T", 3), (3, 4, "A", 1), (7, 8, "A", 0)],
+    "points": 0, "so": 1, "sob": ("Q3", "B2"), "tn": (1, "Q2"), "ch": 4, "cj": (4,), "pl": "B1",
+    "rb": ("Q0", "Q2", "Q1", "B0"), "pb": ("Q1", "Q2", "B1", "B2"), "ob": ("Q0", "Q3", "B0", "B3"),
+    "first": 0.0,
+}
+STEPS, SLACK, NUDGE = 1500, 0.3, 1.0
 LOOK = 0.03
-URGE = {}
-S_CUT, S_HOME = (2, 3, 7), (3, 7)
 ZW = 136
 MAG = 8388608.0
-bf, f32, i32, u16 = "bfloat16", "float32", "int32", "uint16"
+MID = 150.0
+HALF = 2048.0
+bf, f16, f32, i32, u16 = "bfloat16", "float16", "float32", "int32", "uint16"
 
 
 def sb(n, t):
@@ -29,35 +30,35 @@ def sb(n, t):
 SCRATCH = {
     "X": sb(XW, bf), "MV": sb(XW, i32), "tr32": sb(128, i32), "cap32": sb(8, i32), "capf": sb(8, f32),
     "Tuc": sb(384, u16), "Tuj": sb(384, u16), "Tuh": sb(384, u16),
-    "Tfc": sb(384, f32), "Tfj": sb((12, 32), f32), "Tfh": sb(512, f32),
-    "Zc": sb(4 * ZW, bf), "Zj": sb(4 * ZW, bf), "Zh": sb(4 * ZW, bf),
+    "Tfc": sb(384, f16), "Tfj": sb((12, 32), f16), "Tfh": sb(384, f16), "To": sb(128, f32),
+    "Z0": sb(128, bf), "Zj": sb(128, bf), "Zy": sb(128, bf), "zcl": sb(128, bf),
+    "ZTc": sb(3 * ZW, bf), "ZTh": sb(3 * ZW, bf), "ZTs": sb(3 * ZW, bf), "ZTj": sb(128, bf),
     "ANc": sb(768, bf), "ANj": sb(768, bf), "ANh": sb(256, bf),
-    "zTc": sb(128, bf), "zTj": sb(128, bf), "zTh": sb(128, bf), "zcl": sb(128, bf), "z5": sb(128, f32),
     "THc": sb(2048, bf), "THj": sb(2048, bf), "THh": sb(2048, bf),
-    "RAW": sb(2048, bf), "IC": sb(2048, bf), "IM": sb((8, 256), bf), "IH": sb(2048, bf),
-    "AJ": sb((8, 256), bf), "SG": sb((8, 256), bf),
-    "fms": sb(384, bf), "fmh": sb(384, bf), "sos": sb(384, bf), "soj": sb(384, bf),
-    "ocs": sb(24, f32), "ocj": sb(24, f32), "Y": sb(128, f32), "S0": sb(128, f32), "S1": sb(128, f32),
-    "EQ": sb(1024, bf), "po": sb(8, u16), "oc": sb(8, u16), "tc": sb(128, bf),
-    "Town": sb(128, f32), "DT": sb(136, f32), "KS": sb(136, f32), "KM": sb(136, f32), "RR": sb(136, f32),
-    "NU": sb(136, f32), "UU": sb(136, f32), "om": sb(8, u16), "of": sb(8, u16),
+    "RAc": sb(2048, bf), "RAj": sb(2048, bf), "RAh": sb(2048, bf),
+    "IC": sb(2048, bf), "IM": sb((8, 256), bf), "IH": sb(2048, bf), "AJ": sb((128, 17), bf),
+    "fms": sb(384, bf), "fmh": sb(384, bf), "sos": sb((24, 17), bf), "soj": sb(408, bf),
+    "oc": sb(24, u16), "ocj": sb(24, u16), "D2s": sb(408, f32), "D2j": sb(408, f32),
+    "Y": sb(256, f16), "Tsh": sb(128, f16), "S0": sb(128, f32), "S1": sb(128, f32),
+    "EQ": sb(1024, bf), "po": sb(8, u16), "tc": sb(128, bf),
+    "Town": sb((8, 17), f32), "DT": sb(136, f32), "t2": sb(136, f32), "RR": sb(144, f32),
+    "NU": sb(136, f32), "UU": sb(136, f32), "om": sb(32, u16), "of": sb(32, u16),
     "Vus": sb(384, u16), "Vuh": sb(384, u16), "aps": sb(384, bf), "aph": sb(384, bf),
-    "SS": sb(128, f32), "r1": sb(128, f32), "r2": sb(128, f32), "acc": sb(8, f32),
-    "par": sb(8, f32), "ftmp": sb(8, f32), "tn": sb(128, i32),
-    "q1": sb(8, f32), "D2": sb(136, f32), "U2": sb(136, f32),
-    "osh": sb(8, u16), "ts": sb(128, bf), "ik": sb(136, i32), "half": sb(8, f32), "Ih": sb(128, f32), "nIh": sb(128, f32),
-    "FA": sb(128, bf), "Vf": sb(128, f32), "up": sb(256, f32), "tt": sb(256, f32),
-    "io": sb(160, i32), "io2": sb(512, i32), "io3": sb(512, i32), "ioc": sb(160, i32), "ioc2": sb(160, i32), "pc": sb(8, i32), "pcf": sb(8, f32),
-    "Iw": sb(160, f32), "IE": sb(160, f32), "IO": sb(160, f32), "nIf": sb(128, f32), "I5": sb(128, f32), "Dm": sb(128, f32),
-    "Ib": sb(128, bf), "n64": sb(128, bf), "n128": sb(128, bf), "p32": sb(128, bf),
-    "BOf": sb(128, f32), "BOb": sb(128, bf), "BO8": sb(128, bf), "SW": sb(144, bf), "E32": sb(512, bf),
-    "M16": sb(256, bf), "dg": sb(128, f32), "OD0": sb(128, bf), "OD1": sb(128, bf), "D0": sb(128, f32), "lf": sb(160, f32),
-    "DUM8": sb(8, f32), "CZ": sb((8, 17), bf), "CK": sb((8, 17), bf), "CE": sb((8, 17), f32), "RST": sb(136, bf),
-    "FL": sb(144, bf), "cA": sb(8, f32), "cB": sb(8, f32), "isS": sb(128, bf),
-    "P0": ("psum", [128, 512], f32), "P1": ("psum", [128, 16, 32], f32), "P2": ("psum", [128, 512], f32), "P3": ("psum", [128, 16, 32], f32),
-    "PZ": ("psum", [128, 16, 32], f32), "PK": ("psum", [128, 16, 32], f32), "PC": ("psum", [128, 512], f32), "PD": ("psum", [128, 512], f32),
+    "SS": sb(128, f32), "r1": sb(128, f32), "acc": sb(8, f32), "pt": sb(8, bf), "eps": sb(8, bf),
+    "tn": sb(128, i32), "U2": sb(136, f32), "osh": sb(8, u16), "ts": sb(128, bf), "ik": sb(136, i32),
+    "Vf": sb(128, f16), "up": sb(256, bf), "tt": sb(256, f32),
+    "io": sb(168, i32), "io2": sb(512, i32), "io3": sb(512, i32), "ioc": sb(160, i32), "ioc2": sb(160, i32), "pc": sb(8, i32), "pcf": sb(8, f32),
+    "ku": sb(256, f32), "U16": sb(256, bf), "M16": sb(256, bf),
+    "Iw": sb(168, f32), "Dt": sb(160, bf), "Dw": sb(160, bf), "DE": sb(160, bf), "DO": sb(160, bf), "nIb": sb(128, bf), "I5": sb(128, bf),
+    "Ib": sb(128, bf), "n35": sb(128, bf), "I32": sb(128, bf), "I8": sb(128, bf), "nI8": sb(128, bf),
+    "nBO": sb(128, bf), "BOb": sb(128, bf), "BO8": sb(128, bf), "SW": sb(144, bf), "SW8": sb(144, bf), "E32": sb(512, bf),
+    "dg": sb(128, bf), "OD0": sb(128, bf), "OD1": sb(128, bf), "D0": sb(128, f32), "lf": sb(160, f32),
+    "DUM8": sb(8, f32), "CK": sb(136, bf), "Z136": sb(136, bf), "CB": sb(128, bf), "C21": sb(128, bf), "CT": sb(128, bf), "CQ": sb(128, bf),
+    "FL": sb(144, bf), "C15": sb(128, bf), "c35": sb(128, bf), "c384": sb(128, bf),
+    "B0": ("psum", [128, 512], f32), "B1": ("psum", [128, 512], f32), "B2": ("psum", [128, 512], f32), "B3": ("psum", [128, 512], f32),
+    "Q0": ("psum", [128, 512], f32), "Q1": ("psum", [128, 512], f32), "Q2": ("psum", [128, 512], f32), "Q3": ("psum", [128, 16, 32], f32),
 }
-SEMAPHORES = ["V", "S", "P", "G", "sent"] + ["d%d" % i for i in range(16)] + ["m%d" % i for i in range(64)]
+SEMAPHORES = ["V", "S", "P", "G", "sent"] + ["d%d" % i for i in range(20)] + ["m%d" % i for i in range(80)]
 IO_SHAPES = {"sect": [128, W], "mv": [128, Q], "traj": [128, L], "amt": [128, L], "cap": [128, 1],
              "ysect": [128, W], "ytraj": [128, L], "yamt": [128, L]}
 ALL = slice(None)
@@ -73,10 +74,16 @@ def ind(win, off):
     return ("*", win, off)
 
 
+SPANS = {}
+
+
 def span(x):
-    shape = SCRATCH[x[0]][1] if x[0] in SCRATCH else IO_SHAPES[x[0]]
-    e = np.arange(int(np.prod(shape[1:]))).reshape(shape[1:])[x[1][1:]]
-    return int(np.min(e)), int(np.max(e)) + 1, int(np.size(e))
+    k = (x[0], str(x[1][1:]))
+    if k not in SPANS:
+        shape = SCRATCH[x[0]][1] if x[0] in SCRATCH else IO_SHAPES[x[0]]
+        e = np.arange(int(np.prod(shape[1:]))).reshape(shape[1:])[x[1][1:]]
+        SPANS[k] = (int(np.min(e)), int(np.max(e)) + 1, int(np.size(e)))
+    return SPANS[k]
 
 
 def is_psum(x):
@@ -84,13 +91,15 @@ def is_psum(x):
 
 
 def two_bytes(x):
-    return SCRATCH[x[0]][2] in (bf, u16)
+    return SCRATCH[x[0]][2] in (bf, f16, u16)
 
 
 def plan():
     ops = []
     last = {}
     first = [0]
+    seen = {}
+    stage = [""]
 
     def add(eng, kind, args, reads, writes, cost, lat=0.0):
         me = len(ops)
@@ -111,13 +120,17 @@ def plan():
             for (a, b, w, o) in last.get(x[0], []):
                 if o != me and a < hi and lo < b and (w or wr):
                     deps.add(o)
-                if not (wr and lo <= a and b <= hi):
+                if not (wr and lo <= a and b <= hi and span(x)[2] == hi - lo):
                     keep.append((a, b, w, o))
             last[x[0]] = keep + [(lo, hi, wr, me)]
-        w0 = writes[0]
-        per = {"Tu": 128, "Tf": 128, "fm": 128, "so": 128, "Vu": 128, "ap": 128, "Zc": ZW, "Zj": ZW, "Zh": ZW, "AN": 256, "oc": 8}.get(w0[0][:2], 9999)
-        key = eng + w0[0] + str(span(w0)[0] % per) + (reads[0][0] + reads[-1][0] if eng == "P" else reads[-1][0] if reads and w0[0] in ("X", "po", "RAW") else "")
-        ops.append({"eng": eng, "kind": kind, "args": args, "deps": deps, "cost": cost, "lat": lat, "key": key, "first": first[0]})
+        deps.discard(me)
+        k = (stage[0], eng, writes[0][0])
+        seen[k] = seen.get(k, 0) + (eng != "P")
+        key = stage[0][:1] + eng + writes[0][0] + str(seen[k])
+        k = k + ("unit",)
+        seen[k] = seen.get(k, 0) + (eng != "P" or args[3])
+        ops.append({"eng": eng, "kind": kind, "args": args, "deps": deps, "cost": cost, "lat": lat, "key": key, "first": first[0],
+                    "unit": key + "." + str(seen[k]), "round": int(stage[0][1:] or 0), "hop": COST["hop"]})
 
     def sides(xs):
         r = []
@@ -126,14 +139,15 @@ def plan():
                 r += [x[1], x[2]] if x[0] == "*" else [x]
         return r
 
-    def compute(eng, kind, out, ins, args, per, extra_w=()):
-        fix = COST[eng]
+    def compute(eng, kind, out, ins, args, per, extra_w=(), more=0.0):
+        fix = COST[eng] + more
         if out[0] == "*":
-            add(eng, kind, args, sides(ins) + [out[2]], [out[1]], fix + 16 * span(out[2])[2] * 3.8 * CYC)
+            add(eng, kind, args, sides(ins) + [out[2]], [out[1]], fix + 0.02 + 16 * span(out[2])[2] * COST["scatter"] * CYC)
             return
         n = span(out)[2]
         if ins and isinstance(ins[0], tuple) and ins[0][0] == "*":
             per = GA
+            fix += 0.02 * (eng == "V")
         elif eng == "V" and all(two_bytes(x) for x in [out] + sides(ins[:2]) if span(x)[2] > 1):
             per = per / 2
         add(eng, kind, args, sides(ins), [out] + list(extra_w), fix + max(64, n * per) * CYC)
@@ -153,16 +167,26 @@ def plan():
     def ms(out, v):
         compute("V", "memset", out, [], (out, v), 1)
 
-    def act(out, in_, func=F.Identity, bias=0.0, scale=1.0, accum=None):
-        compute("S", "activation", out, [in_, bias, scale], (out, in_, func, bias, scale, accum), 1, [accum] if accum else [])
+    def act(out, in_, func=F.Identity, bias=0.0, scale=1.0, accum=None, more=0.0):
+        compute("S", "activation", out, [in_, bias, scale], (out, in_, func, bias, scale, accum), 1, [accum] if accum else [], more)
 
-    def mm(out, lhsT, rhs, start=True, stop=True):
+    def step(out, in_, bias, scale=256.0, more=0.0):
+        act(out, in_, F.Sigmoid, bias, scale, more=more)
+
+    def mm(out, lhsT, rhs, start=True, stop=True, more=()):
         n = span(rhs)[2]
-        add("P", "matmul", (out, lhsT, rhs, start, stop), [lhsT, rhs], [out], max(64, n) * PCYC * (1 if two_bytes(rhs) else 4))
+        add("P", "matmul", (out, lhsT, rhs, start, stop), [lhsT, rhs] + [x for m in more for x in m[1:3]], [out],
+            (1 + len(more)) * (COST["P"] + max(64, n) * PCYC * (1 if two_bytes(rhs) else 4)))
+        ops[-1]["more"] = list(more)
 
     def group(out_lhs_rhs):
-        for i, (o, l, r) in enumerate(out_lhs_rhs):
-            mm(o, l, r, i == 0, i == len(out_lhs_rhs) - 1)
+        n, i = len(out_lhs_rhs), 0
+        while i < n:
+            j = i + 1
+            while j < n and j - i < 4 and out_lhs_rhs[i][1][0][:2] == out_lhs_rhs[j][1][0][:2] == "SW":
+                j += 1
+            mm(*out_lhs_rhs[i], i == 0, i == n - 1, [x + (False, k == n - 1) for k, x in enumerate(out_lhs_rhs) if i < k < j])
+            i = j
 
     def iota(out, pattern, base, cm):
         add("G", "iota", (out, pattern, base, cm), [], [out], 0.16 + 2 * span(out)[2] * CYC)
@@ -171,27 +195,37 @@ def plan():
         add(queue, "dma", (out, in_), [in_], [out], 0.06, lat)
         ops[-1]["deps"].update(after)
 
-    def send(step, dst, src):
-        add("G", "send", (step % N, dst, src), [src], [dst], COST["call"], LAT + span(src)[2] * (2 if two_bytes(src) else 4) * 0.002)
+    def send(by, dst, src):
+        add("G", "send", (by % N, dst, src), [src], [dst], COST["call"], LAT + span(src)[2] * (2 if two_bytes(src) else 4) * COST["byte"])
 
     CYC, PCYC, GA, LAT = COST["cyc"], COST["pe"], COST["gather"], COST["link"]
     sel = lambda a: ap("SW", 15 - a, 143 - a)
     I_b, I_f = ap("Ib"), ap("Iw", 16, 144)
     col = lambda name, c: ap(name, c, c + 1)
-    bank = lambda j, lo, hi: ap("P%d" % j, slice(lo // 32, hi // 32), ALL) if j % 2 else ap("P%d" % j, lo, hi)
-    Xm, Xw, Xe = ap("X", 0, W), ap("X", 0, EXT), ap("X", 0, XW)
-    zs = lambda who, r: ap("Z" + who, r * ZW, r * ZW + 128)
-    fc = lambda who, r, c: col("Z" + who, r * ZW + 128 + c)
-    cap, ncap, ccap = col("capf", 0), col("capf", 1), col("capf", 2)
+    q3 = lambda a, b: ap("Q3", slice(a, b), ALL)
+    part = lambda bank, a, b: ap(bank, slice(a, b), slice(0, 16)) if bank == "Q3" else ap(bank, 16 * a, 16 * b)
+    CH, CJ = [(0, CFG["ch"]), (CFG["ch"], 8)], list(zip((0,) + CFG["cj"], CFG["cj"] + (8,)))
+    ahead = lambda b0: sum(b0 < e for e in CFG["cj"])
+    Xm, Xw, Xe, Zj = ap("X", 0, W), ap("X", 0, EXT), ap("X", 0, XW), ap("Zj")
+    beta = lambda who, r: col("ZT" + who, r * ZW + 128)
+    cap, less, over = col("capf", 0), col("capf", 1), col("capf", 2)
 
+    stage[0] = "0"
     dma("Y", ap("tr32"), ap("traj"), 1.9)
-    dma("S", zs("h", 0), ap("amt"), 1.9)
+    dma("S", ap("Z0"), ap("amt"), 1.9)
     dma("S", col("cap32", 0), ap("cap"), 1.9)
     dma("Y", Xm, ap("sect"), 4.5)
     dma("Y", ap("MV", 0, Q), ap("mv"), 4.5, [3])
     dma("Y", ap("MV", Q, W), ap("mv"), 7.0, [3])
 
-    iota(ap("io"), [[1, 160]], -16, -1)
+    iota(ap("ku"), [[0, 16], [1, 16]], 0, 0)
+    step(ap("U16"), ap("ku"), 256 * 14.5, -256.0, more=1.3)
+    if any(u[2] in "TA" for u in CFG["cut"]):
+        step(ap("M16"), ap("ku"), -128.0)
+    for b0, b1, way, _ in CFG["cut"]:
+        if way == "T":
+            ms(ap("RAc", 256 * b0 + 15, 256 * b1, 16), -256.0)
+    iota(ap("io"), [[1, 168]], -16, -1)
     iota(ap("ioc"), [[1, 160]], 0, 0)
     iota(col("pc", 0), [[0, 1]], 0, 1)
     iota(ap("io2"), [[1, 32], [0, 16]], 128, -1)
@@ -200,298 +234,323 @@ def plan():
     ts(col("pc", 3), col("pc", 0), 4, A.arith_shift_right, 1, A.bitwise_and)
     cp(ap("pcf", 0, 4), ap("pc", 0, 4))
     ts(col("pcf", 4), col("pcf", 3), -1.0, A.mult, 1.0, A.add)
-    ts(col("pcf", 5), col("pcf", 1), 15.0, A.is_lt)
+    ts(col("pcf", 5), col("pcf", 1), 15.0, A.is_equal, 128.0, A.mult)
+    ts(col("pcf", 6), col("pcf", 1), 0.0, A.is_gt)
     ts(ap("Iw"), ap("io"), 0.0, A.is_equal)
     act(ap("Ib"), I_f)
     ts(ap("io3"), ap("io2"), 31, A.bitwise_and)
     ts(ap("E32"), ap("io3"), 0.0, A.is_equal)
     ts(ap("ioc2"), ap("ioc"), 4, A.arith_shift_right)
-    ts(ap("BOf"), ap("ioc2", 0, 128), col("pcf", 2), A.is_equal)
+    ts(ap("BOb"), ap("ioc2", 0, 128), col("pcf", 2), A.is_equal)
     ms(ap("SW"), 0.0)
-    cp(ap("SW", 15, 143, 16), ap("BOf", 0, 128, 16))
-    ms(ap("M16"), 1.0)
-    ms(ap("M16", 0, 256, 16), 0.0)
-    ms(ap("X", W, XW), 0.0)
+    cp(ap("SW", 15, 143, 16), ap("BOb", 0, 128, 16))
+    act(ap("SW8"), ap("SW"), scale=8192.0)
+    act(col("pcf", 7), col("pcf", 5), scale=-HALF / 128)
+    ms(ap("X", W, EXT), 0.0)
     ts(ap("ioc2"), ap("ioc"), 15, A.bitwise_and)
     ts(ap("dg"), ap("ioc2", 0, 128), col("pcf", 1), A.is_equal)
     cp(ap("lf"), ap("ioc"))
     act(ap("OD0"), ap("dg"), bias=8192.0, scale=-8192.0)
     act(ap("OD1"), ap("dg"), bias=8192.0, scale=-16384.0)
+    ts(ap("DUM8"), ap("lf", 0, 128, 16), col("pcf", 1), A.add, float(DUM), A.add)
     ts(ap("D0"), ap("lf", 0, 128), DUM + 1.0, A.add)
     tt(ap("D0"), ap("D0"), ap("dg"), A.mult)
     ts(ap("D0"), ap("D0"), -1.0, A.add)
-    ts(ap("DUM8"), ap("lf", 0, 128, 16), col("pcf", 1), A.add, float(DUM), A.add)
-    tt(ap("Dm"), I_f, ap("Iw", 17, 145), A.subtract)
-    tt(ap("Dm"), ap("Dm"), ap("BOf"), A.mult)
-    act(ap("BOb"), ap("BOf"))
-    act(ap("BO8"), ap("BOf"), scale=8192.0)
-    act(ap("IE"), ap("Iw"), scale=col("pcf", 4))
-    act(ap("IO"), ap("Iw"), scale=col("pcf", 3))
-    act(ap("nIf"), I_f, scale=-1.0)
+    act(ap("Dt"), ap("Iw", 1, 161), scale=col("pcf", 6))
+    tt(ap("Dw"), ap("Iw", 0, 160), ap("Dt"), A.subtract)
+    act(ap("nBO"), ap("BOb"), scale=-1.0)
+    act(ap("BO8"), ap("BOb"), scale=8192.0)
+    act(ap("DE"), ap("Dw"), scale=col("pcf", 4))
+    act(ap("DO"), ap("Dw"), scale=col("pcf", 3))
+    act(ap("nIb"), I_f, scale=-1.0)
+    act(ap("nI8"), I_f, scale=-8192.0)
     act(ap("I5"), I_f, scale=5.0)
-    act(ap("n64"), I_f, scale=-64.0)
-    act(ap("n128"), I_f, scale=-128.0)
-    act(ap("p32"), I_f, scale=32.0)
-    ms(ap("CZ"), 0.0)
-    ms(ap("CZ", ALL, 0), 100.0)
-    ms(ap("CE"), 0.0)
-    ts(ap("CE", ALL, 0), ap("DUM8"), float(L), A.add)
-    iota(ap("ik"), [[0, 8], [-1, 17]], 17, 0)
-    ts(ap("CK"), ap("ik"), 1.0 / 16, A.mult)
-    ms(ap("CK", ALL, 0), 0.0)
-    act(ap("Ih"), I_f, scale=0.5)
-    act(ap("nIh"), I_f, scale=-0.5)
+    act(ap("n35"), I_f, scale=-35.5)
+    act(ap("I32"), I_f, scale=32.0)
+    act(ap("I8"), I_f, scale=8192.0)
+    ms(ap("c35"), -3.5)
+    act(ap("C15"), ap("c35"), bias=col("pcf", 5))
+    ms(ap("c384"), -800.0)
+    act(ap("C21"), ap("C15"), bias=3.5 * (HALF - EXT) / 128, scale=(HALF - EXT) / 128)
+    ms(ap("CT"), 0.0)
+    act(ap("CT", 15, 128, 16), ap("DUM8"), bias=float(DUM), scale=-1.0)
+    compute("V", "transpose", ap("CQ"), [ap("CT")], (ap("CQ"), ap("CT")), 1)
+    act(ap("Town", ALL, 16), ap("DUM8"), bias=float(L))
+    iota(ap("ik"), [[1, 8], [0, 17]], 1, 0)
+    ts(ap("CK"), ap("ik"), 4352.0, A.mult, -8192.0, A.add)
+    ts(ap("CK", 16, 136, 17), ap("ik", 0, 136, 17), 4352.0, A.mult)
     ms(ap("up"), 0.0)
-    ms(ap("D2"), 0.0)
-    cp(ap("D2", 16, 136, 17), ap("DUM8"))
-    ms(col("half", 0), 0.5)
-    ms(ap("RST"), 0.0)
-    ms(ap("RST", 0, 136, 17), -1024.0)
-    ms(ap("FL"), 1.0)
-    ms(ap("FL", 0, 1), 0.0)
+    ms(ap("D2s"), 0.0)
+    for r in range(RO):
+        act(ap("D2s", 136 * r + 15, 136 * r + 136, 17), ap("DUM8"))
+    ms(ap("sos", ALL, 16), 0.0)
+    ms(ap("AJ", ALL, 16), 0.0)
+    ms(ap("Z136"), 0.0)
+    ms(ap("RR"), 0.0)
+    ms(ap("FL"), -576.0)
+    ms(ap("FL", 0, 1), -832.0)
     ms(ap("MV", W, EXT), 0)
-    ms(ap("isS"), 0.0)
-    for b in S_HOME:
-        ms(ap("isS", 16 * b, 16 * b + 16), 1.0)
-    for c, (a_, b_) in enumerate([(0, 0), (-1, -3.5), (2, 23), (-1, 12), (-1, 60), (0, 0), (0, 0), (0, 0)]):
-        if 1 <= c <= 5:
-            hi = 8 if c == 5 else c + 1
-            ms(ap("cA", c, hi), float(a_))
-            ms(ap("cB", c, hi), float(b_))
-    cp(col("cA", 0), col("pcf", 5))
-    ts(col("cB", 0), col("pcf", 5), 5.0, A.mult, -1.0, A.add)
+    ms(ap("ZTh", 128, ZW), 0.0)
+    for r in range(1, RO):
+        ms(ap("ZTs", r * ZW + 128, r * ZW + ZW), 0.0)
+    ms(col("eps", 0), 10.0 / 256)
     cp(cap, col("cap32", 0))
-    ts(ncap, cap, -1.0, A.mult, -0.5, A.add)
-    ts(ccap, cap, -255.0, A.add)
-    ts(col("capf", 3), cap, 1.0, A.add)
-    ms(col("half", 1), -0.5)
+    ts(less, cap, -1.0, A.mult, MID, A.add)
+    ts(over, cap, -MID, A.add)
 
-    def quarters(an):
-        act(ap("r2"), ap("SS"), bias=MAG - 0.5, scale=0.125)
-        act(ap(an[0], an[1], an[1] + 128), ap("r2"), F.Relu, bias=-MAG)
-        act(ap(an[0], an[1] + 128, an[1] + 256), ap(an[0], an[1], an[1] + 128), bias=255.0, scale=-1.0)
+    def quarters(an, s, scale, bias):
+        act(ap(an[0], an[1] + 128, an[1] + 256), s, bias=bias, scale=scale)
+        act(ap(an[0], an[1], an[1] + 128), ap(an[0], an[1] + 128, an[1] + 256), bias=255.0, scale=-1.0)
 
-    def send_points(r, c):
-        a, b = 16 * CH[c][0], 16 * CH[c][1]
-        u, f = ap("Tuh", 128 * r + a, 128 * r + b), ap("Tfh", 128 * r + a, 128 * r + b)
-        send(SB, ap("Tuc", 128 * r + a, 128 * r + b), u)
-        send(SB, ap("Tfc", 128 * r + a, 128 * r + b), f)
-        if c == len(CH) - 1:
-            u, f = ap("Tuh", 128 * r, 128 * r + 128), ap("Tfh", 128 * r, 128 * r + 128)
-            send(SC, ap("Tfj", slice(4 * r, 4 * r + 4), ALL), f)
-            send(SC, ap("Tuj", 128 * r, 128 * r + 128), u)
+    def turned(out, z, bias, bank):
+        mm(bank, z, I_b)
+        act(out, bank, bias=bias)
 
-    def transposed(who, z):
-        p = ap("PZ", slice(8, 12), ALL)
-        mm(p, z, I_b)
-        act(ap("zT" + who), p)
-
-    def runs(on_scalar):
-        r = []
-        for j in range(4):
-            s0, s1 = 2 * j in on_scalar, 2 * j + 1 in on_scalar
-            r += [(2 * j, 2 * j + 2, s0)] if s0 == s1 else [(2 * j, 2 * j + 1, s0), (2 * j + 1, 2 * j + 2, s1)]
-        return r
-
-    def spread(who, b0, b1, banks=(0, 1, 2, 3)):
+    def spread(who, r, u, start, stop):
+        b0, b1, _, bk = u
         j = b0 // 2
         rows = slice(32 * j, 32 * j + 32)
         lo, hi = 256 * (b0 - 2 * j), 256 * (b1 - 2 * j)
-        return bank(banks[j % len(banks)], lo, hi), ap("zT" + who, rows=rows), ap("E32", lo, hi, rows=rows)
+        z = ap("ZTj", rows=rows) if who == "j" else ap("ZT" + who, r * ZW, r * ZW + 128, rows=rows)
+        p = ap("B%d" % bk, lo, hi)
+        mm(p, z, ap("E32", lo, hi, rows=rows), start, stop)
+        return p
 
-    def limits(who, on_scalar, banks):
-        for b0, b1, s in runs(on_scalar):
-            if not s:
-                o, l, r_ = spread(who, b0, b1, banks)
-                mm(o, l, r_)
-                if (who, b0) in LIM_V:
-                    ts(ap("TH" + who, 256 * b0, 256 * b1), o, -1.0, A.mult, cap, A.add)
-                else:
-                    act(ap("TH" + who, 256 * b0, 256 * b1), o, bias=cap, scale=-1.0)
+    def limits(who, r, units):
+        for u in units:
+            if u[2] == "T":
+                p = spread(who, r, u, True, True)
+                act(ap("TH" + who, 256 * u[0], 256 * u[1]), p, bias=0.0 if who == "j" else over, scale=-1.0)
 
-    def over(who, on_scalar, offs, r, out):
-        for b0, b1, s in runs(on_scalar):
-            src = ind(Xm, ap(offs, 128 * r + 16 * b0, 128 * r + 16 * b1))
-            o = ap(out, 256 * b0, 256 * b1)
-            first[0] = int(b0 < CH[0][1])
-            if s:
-                raw = ap("RAW", 256 * b0, 256 * b1)
-                act(raw, src)
-                p, l, r_ = spread(who, b0, b1)
-                group([(p, l, r_), (p, I_b, raw)])
-                act(o, p, F.Sign, bias=ncap)
+    def summed(who, r, u, offs):
+        b0, b1, way, _ = u
+        src = ind(Xm, ap(offs, 128 * r + 16 * b0, 128 * r + 16 * b1))
+        raw = ap("RA" + who, 256 * b0, 256 * b1)
+        p = spread(who, r, u, True, False)
+        if way == "V":
+            if who == "j":
+                cp(raw, src)
             else:
-                tt(o, src, ap("TH" + who, 256 * b0, 256 * b1), A.is_gt)
-        first[0] = 0
+                ts(raw, src, less, A.add)
+        else:
+            act(raw, src, bias=0.0 if who == "j" else less)
+        mm(p, I_b, raw, False, True)
+        return p
+
+    def judge_limits(r):
+        dma("Y", ap("X", EXT, XW), Zj, 2.0)
+        ts(ap("zcl"), Zj, cap, A.subtract, 1.0, A.min)
+        turned(ap("ZTj"), ap("zcl"), 0.0, q3(4, 8))
+
+    def judge_points(r):
+        seg = slice(4 * r, 4 * r + 4)
+        g_ = [(q3(8, 12), I_b, ap("CQ")), (q3(8, 12), I_b, ap("C21"))]
+        for h, (m0, m1) in enumerate([(ap("DE", 16, 144), ap("DE", 0, 128)), (ap("DO", 32, 160), ap("DO", 16, 144))]):
+            o = ap("Q3", slice(8, 12), slice(16 * h, 16 * h + 16))
+            g_ += [(o, m0, ap("Tfj", seg, slice(0, 16))), (o, m1, ap("Tfj", seg, slice(16, 32)))]
+        group(g_)
+        o = ap("Town", ALL, slice(0, 16))
+        compute("V", "transpose", o, [q3(8, 12)], (o, q3(8, 12)), 1)
+        act(ap("DT"), ap("Town"))
+
+    def new_points(r):
+        o = part(CFG["tn"][1], 8, 16)
+        group([(o, ap("I5"), ap("Tfj", slice(4 * r, 4 * r + 4), ALL)), (o, ap("BOb"), Zj)])
+        ts(ap("tn"), o, 5 * HALF + 1, A.add)
+        ts(ap("MV", EXT, XW), ap("tn"), W - 1, A.bitwise_and)
 
     cp(ap("Tuh", 0, 128), ap("tr32"))
-    cp(ap("Tfh", 0, 128), ap("tr32"))
-    cp(ap("Zh", 128, ZW), ap("cB"))
-    send(SB, ap("Zc", 0, 128), ap("Zh", 0, 128))
-    cp(ap("Zc", 128, ZW), ap("cB"))
+    ts(ap("Tfh", 0, 128), ap("tr32"), -HALF, A.add)
+    turned(ap("ZTh", 0, 128), ap("Z0"), -MID, q3(4, 8))
+    send(SB, ap("ZTc", 0, ZW), ap("ZTh", 0, ZW))
     send(SB, ap("Tuc", 0, 128), ap("Tuh", 0, 128))
+    send(SC, Zj, ap("Z0"))
     send(SB, ap("Tfc", 0, 128), ap("Tfh", 0, 128))
-    send(SC, ap("Zj", 0, 128), ap("Zh", 0, 128))
-    cp(ap("Zj", 128, ZW), ap("cB"))
-    act(ap("SS"), zs("h", 0), bias=0.5, scale=2.0)
-    quarters(("ANh", 0))
+    quarters(("ANh", 0), ap("Z0"), -0.25, 255.375)
     send(SB, ap("ANc", 0, 256), ap("ANh"))
     send(SC, ap("Tuj", 0, 128), ap("Tuh", 0, 128))
     send(SC, ap("Tfj", slice(0, 4), ALL), ap("Tfh", 0, 128))
     send(SC, ap("ANj", 0, 256), ap("ANh"))
-
-    def judge_points(r):
-        seg = slice(4 * r, 4 * r + 4)
-        for h, (m0, m1) in enumerate([(ap("IE", 16, 144), ap("IE", 0, 128)), (ap("IO", 32, 160), ap("IO", 16, 144))]):
-            o = ap("PK", slice(8, 12), slice(16 * h, 16 * h + 16))
-            group([(o, m0, ap("Tfj", seg, slice(0, 16))), (o, m1, ap("Tfj", seg, slice(16, 32)))])
-        compute("V", "transpose", ap("Town"), [ap("PK", slice(8, 12), ALL)], (ap("Town"), ap("PK", slice(8, 12), ALL)), 1)
-        group([(ap("PK", slice(8, 16), slice(0, 17)), I_f, ap("CE")), (ap("PK", slice(8, 16), slice(1, 17)), I_f, ap("Town")),
-               (ap("PK", slice(8, 16), slice(0, 16)), ap("nIf"), ap("Town"))])
-        act(ap("DT"), ap("PK", slice(8, 16), slice(0, 17)))
-        group([(bank(3, 0, 128), ap("I5"), ap("Tfj", seg, ALL)), (bank(3, 0, 128), ap("BOb"), zs("j", r))])
-        ts(ap("tn"), bank(3, 0, 128), 1.0, A.add)
-        ts(ap("MV", EXT, XW), ap("tn"), W - 1, A.bitwise_and)
-        act(ap("X", EXT, XW), zs("j", r))
-        act(ap("z5"), zs("j", r), bias=0.5)
-
-    def judge_limits(r):
-        ts(ap("zcl"), zs("j", r), ccap, A.max, col("capf", 3), A.min)
-        transposed("j", ap("zcl"))
-        limits("j", (), JB)
+    limits("c", 0, CFG["cut"])
+    judge_limits(0)
 
     for r in range(RO):
         R = 128 * r
-        if not r:
-            transposed("c", zs("c", r))
-            limits("c", S_CUT, (0, 1, 2, 3))
-        over("c", S_CUT, "Tuc", r, "IC")
-        judge_points(r)
-        if not (r and EARLY):
-            judge_limits(r)
-        transposed("h", zs("h", r))
-        mm(ap("PD", 128, 256), ap("Dm"), ap("Tfc", R, R + 128))
-        for b in range(8):
-            scan(ap("IM", b, ALL), ap("M16"), ap("IC", 256 * b, 256 * b + 256), 0.0, A.mult, A.max)
+        stage[0] = "c%d" % r
+        for u in CFG["cut"]:
+            b0, b1, way, _ = u
+            first[0] = ahead(b0)
+            if way in "TA":
+                if way == "T":
+                    tt(ap("IC", 256 * b0, 256 * b1), ind(Xm, ap("Tuc", R + 16 * b0, R + 16 * b1)), ap("THc", 256 * b0, 256 * b1), A.is_gt)
+                else:
+                    step(ap("IC", 256 * b0, 256 * b1), summed("c", r, u, "Tuc"), -128.0)
+                for b in range(b0, b1):
+                    scan(ap("IM", b, ALL), ap("M16"), ap("IC", 256 * b, 256 * b + 256), 0.0, A.mult, A.max)
+            else:
+                p = summed("c", r, u, "Tuc")
+                for b in range(b0, b1):
+                    scan(ap("IM", b, ALL), ap(p[0], 256 * (b % 2), 256 * (b % 2) + 256), ap("U16"), 0.0, A.max, A.min)
+        first[0] = 0
+        mm(ap("Q1", 0, 128), ap("Dt", 16, 144), ap("Tfc", R, R + 128))
+        act(ap("Tsh"), ap("Q1", 0, 128), bias=col("pcf", 7))
+        act(ap("CB"), ap("C15"), bias=beta("c", r), scale=256.0)
         for b0, b1 in CH:
-            group([(ap("PC", 16 * b0, 16 * b1), sel(k), ap("IM", slice(b0, b1), slice(k, 256, 16))) for k in range(16)])
+            o = ap("Q0", 16 * b0, 16 * b1)
+            group([(o, ap("I32"), ap("CB", 16 * b0, 16 * b1))] +
+                  [(o, ap("SW8", 15 - k, 143 - k), ap("IM", slice(b0, b1), slice(k, 256, 16))) for k in range(15)])
+        y0, y1, pl = ap("Y", 0, 128), ap("Y", 128, 256), CFG["pl"]
+        tt(y0, ap("Q0", 0, 128), ap("Tfc", R, R + 128), A.min)
+        tt(y1, ap("Q0", 0, 128), ap("Tsh"), A.min)
         fm = ap("fms", R, R + 128)
-        ts(fm, ap("PC", 0, 128), fc("c", r, 0), A.is_ge)
-        tt(ap("Y"), ap("PD", 128, 256), fm, A.mult)
-        group([(ap("P2", 0, 128), I_b, ap("OD0")), (ap("P2", 0, 128), ap("BOf"), ap("Y"))])
-        mm(ap("PC", 256, 384), ap("BOf"), ap("Y"))
-        scan(ap("S0"), ap("D0"), ap("P2", 0, 128), -1.0, A.max, A.min)
-        mm(ap("PD", 0, 128), I_b, ap("OD1"), True, False)
-        mm(ap("PD", 0, 128), ap("BOf"), ap("Y"), False, False)
+        step(fm, ap("Q0", 0, 128), 0.0, 1.0 / 32)
+        place = lambda o: [(o, ap("BOb"), y0), (o, ap("nBO"), y1)]
+        group([(ap("Q2", 0, 128), I_b, ap("OD0"))] + place(ap("Q2", 0, 128)))
+        group(place(ap(pl, 128, 256)))
+        scan(ap("S0"), ap("D0"), ap("Q2", 0, 128), -1.0, A.max, A.min)
+        mm(ap("Q1", 128, 256), I_b, ap("OD1"), True, False)
+        for x in place(ap("Q1", 128, 256)):
+            mm(*x, False, False)
         for s in range(8):
             e = ap("EQ", 128 * s + 16 * s, 128 * s + 128)
-            tt(e, ap("PC", 256 + 16 * s, 384), ap("S0", 0, 128 - 16 * s), A.is_equal)
-            mm(ap("PD", 16 * s, 128), ap("BO8"), e, False, s == 7)
+            tt(e, ap(pl, 128 + 16 * s, 256), ap("S0", 0, 128 - 16 * s), A.is_equal)
+            mm(ap("Q1", 128 + 16 * s, 256), ap("BO8"), e, False, s == 7)
         cp(ap("po"), ap("S0", 15, 128, 16))
         tt(ap("tc"), ind(Xm, ap("po")), ap("ANc", 256 * r + 128, 256 * r + 256), A.min)
-        scan(ap("S1"), ap("D0"), ap("PD", 0, 128), -1.0, A.max, A.min)
-        cp(ap("oc"), ap("S1", 15, 128, 16))
-        tt(ind(Xw, ap("oc")), ap("tc"), ap("ANc", 256 * r, 256 * r + 128), A.add)
-        group([(ap("PZ", slice(8, 16), slice(0, 16)), sel(a), ap("IM", ALL, slice(16 * a, 16 * a + 16))) for a in range(16)])
-        act(ap("sos", R, R + 128), ap("PZ", slice(8, 16), slice(0, 16)), F.Sign, bias=fc("c", r, 1))
-        send(SC - SB, ap("soj", R, R + 128), ap("sos", R, R + 128))
-        act(ap("ocs", 8 * r, 8 * r + 8), ap("S1", 15, 128, 16))
-        send(SC - SB, ap("ocj", 8 * r, 8 * r + 8), ap("ocs", 8 * r, 8 * r + 8))
+        scan(ap("S1"), ap("D0"), ap("Q1", 128, 256), -1.0, A.max, A.min)
+        if CFG["tn"][0] == 1:
+            new_points(r)
+        oc = ap("oc", 8 * r, 8 * r + 8)
+        cp(oc, ap("S1", 15, 128, 16))
+        tt(ind(Xw, oc), ap("tc"), ap("ANc", 256 * r, 256 * r + 128), A.add)
         send(-SB, ap("fmh", R, R + 128), fm)
-
-        for c, (b0, b1) in enumerate(CHJ):
+        send(SC - SB, ap("ocj", 8 * r, 8 * r + 8), oc)
+        seg = slice(8 * r, 8 * r + 8)
+        for c, (b0, b1) in enumerate(CH):
+            if CFG["points"] == c:
+                judge_points(r)
             bs, a, b = slice(b0, b1), 16 * b0, 16 * b1
-            first[0] = 1 - c
-            for x0, x1, on_vector in [u for u in J_UNITS if b0 <= u[0] < b1]:
-                d = ap("RAW", 256 * x0, 256 * x1)
-                tt(d, ind(Xm, ap("Tuj", R + 16 * x0, R + 16 * x1)), ap("THj", 256 * x0, 256 * x1), A.subtract)
-                act(ap("SG", slice(x0, x1), ALL), d, F.Sign, bias=col("half", 1))
-                if on_vector:
-                    ts(ap("AJ", slice(x0, x1), ALL), d, 0.0, A.max)
-                else:
-                    act(ap("AJ", slice(x0, x1), ALL), d, F.Relu)
-            in16 = slice(1, 17)
-            pk, pz = ("P1", "P3") if c else ("PK", "PZ")
-            group([(ap(pk, bs, slice(0, 17)), I_b, ap("CK", bs, ALL))] +
-                  [(ap(pk, bs, in16), sel(x), ap("AJ", bs, slice(16 * x, 16 * x + 16))) for x in range(16)])
-            group([(ap(pz, bs, slice(0, 17)), I_b, ap("CZ", bs, ALL)), (ap(pz, bs, in16), ap("p32"), ap("soj", R + a, R + b))] +
-                  [(ap(pz, bs, in16), sel(x), ap("SG", bs, slice(16 * x, 16 * x + 16))) for x in range(16)])
-            w = lambda name: ap(name, 17 * b0, 17 * b1)
-            act(w("KS"), ap(pk, bs, slice(0, 17)), bias=fc("j", r, 2), scale=1.0 / 8192)
-            tt(w("KM"), ap(pz, bs, slice(0, 17)), w("KS"), A.min)
-            scan(w("RR"), w("RST"), w("KM"), 0.0, A.add, A.max)
-            tt(w("NU"), w("KM"), w("RR"), A.is_lt)
+            o = part(CFG["sob"][c], b0, b1)
+            group([(o, ap("ZTc", r * ZW, r * ZW + 128), ap("Ib", a, b)), (o, I_b, ap("RAc", 16 * a + 15, 16 * b, 16)),
+                   (o, ap("I8"), ap("IM", bs, slice(14, 256, 16))), (o, ap("I8"), ap("IM", bs, slice(15, 256, 16)))])
+            step(ap("IM", bs, slice(15, 256, 16)), o, -128.0)
+            group([(o, I_b, ap("c35", a, b))] + [(o, sel(x), ap("IM", bs, slice(16 * x, 16 * x + 16))) for x in range(16)])
+            step(ap("sos", slice(8 * r + b0, 8 * r + b1), slice(0, 16)), o, beta("c", r))
+            if CFG["so"] == 2 or c:
+                s0 = b0 if CFG["so"] == 2 else 0
+                send(SC - SB, ap("soj", 136 * r + 17 * s0, 136 * r + 17 * b1), ap("sos", slice(8 * r + s0, 8 * r + b1), ALL))
+        if CFG["points"] == 2:
+            judge_points(r)
+        if CFG["tn"][0] == 2:
+            new_points(r)
+        o = ap("Q1", 256, 264)
+        group([(o, ap("I8"), ap("U16", 0, 8)), (o, ap("nI8"), ap("sos", seg, 15)), (o, I_f, ap("S1", 15, 128, 16))])
+        tt(ap("D2s", 136 * r + 16, 136 * r + 136, 17), o, ap("DUM8"), A.min)
+        send(SC - SB, ap("D2j", 136 * r, 136 * r + 136), ap("D2s", 136 * r, 136 * r + 136))
+
+        stage[0] = "j%d" % r
+        limits("j", r, CFG["judge"])
+        for u in CFG["judge"]:
+            b0, b1, way, _ = u
+            first[0] = ahead(b0)
+            if way == "T":
+                p = ap("RAj", 256 * b0, 256 * b1)
+                tt(p, ind(Xm, ap("Tuj", R + 16 * b0, R + 16 * b1)), ap("THj", 256 * b0, 256 * b1), A.subtract)
+            else:
+                p = summed("j", r, u, "Tuj")
+                if way == "A":
+                    act(ap("THj", 256 * b0, 256 * b1), p)
+                    p = ap("THj", 256 * b0, 256 * b1)
+            ts(ap("AJ", slice(16 * b0, 16 * b1), slice(0, 16)), p, col("eps", r), A.max)
+        for c, (b0, b1) in enumerate(CJ):
+            a, b = 16 * b0, 16 * b1
+            first[0] = len(CJ) - 1 - c
+            w = lambda name, off=0: ap(name, 17 * b0 + off, 17 * b1 + off)
+            o = ap(CFG["rb"][c], 256, 256 + 17 * (b1 - b0))
+            om, of = ap("om", 8 * c, 8 * c + b1 - b0), ap("of", 8 * c, 8 * c + b1 - b0)
+            group([(o, I_b, w("CK"))] + [(o, sel(x), ap("AJ", slice(a + x, b, 16), ALL)) for x in range(16)] + [(o, ap("I8"), w("soj", 136 * r))])
+            ts(w("t2"), o, MAG, A.add, -MAG, A.add)
+            tt(o, w("t2"), o, A.is_le)
+            tt(o, o, w("t2"), A.mult)
+            scan(w("RR", c + 1), w("Z136"), o, 0.0, A.add, A.max)
+            tt(w("NU"), o, w("RR", c), A.is_le)
             scan(w("UU"), w("NU"), w("DT"), 0.0, A.mult, A.add)
-            tm = ap("UU", 17 * b0 + 16, 17 * b1, 17)
-            cp(ap("om", b0, b1), tm)
-            cp(ap("Vus", R + a, R + b), ind(ap("MV"), ap("om", b0, b1)))
+            cp(om, ap("UU", 17 * b0 + 16, 17 * b1, 17))
+            cp(ap("Vus", R + a, R + b), ind(ap("MV"), om))
             send(-SC, ap("Vuh", R + a, R + b), ap("Vus", R + a, R + b))
-            ts(ap("of", b0, b1), tm, EXT - 1.0, A.subtract)
-            act(ap("aps", R + a, R + b), ind(ap("FL"), ap("of", b0, b1)), accum=col("acc", c))
+            tt(ap("SS", a, b), ind(Xe, om), ap("Zj", a, b), A.add)
+            ts(of, ap("UU", 17 * b0 + 16, 17 * b1, 17), EXT - 1.0, A.subtract)
+            act(ap("aps", R + a, R + b), ind(ap("FL"), of), accum=col("acc", c))
             send(-SC, ap("aph", R + a, R + b), ap("aps", R + a, R + b))
-            tt(ap("SS", a, b), ind(Xe, ap("om", b0, b1)), ap("z5", a, b), A.add)
+            if c and r + 1 < RO:
+                act(col("acc", 0), col("acc", 0), bias=col("acc", c))
         first[0] = 0
-        limits("h", S_HOME, (0, 2))
-        act(ap("q1"), ap("soj", R + 15, R + 128, 16), bias=4096.0, scale=-4096.0)
-        group([(ap("PD", 0, 8), ap("nIf"), ap("DUM8")), (ap("PD", 0, 8), I_f, ap("ocj", 8 * r, 8 * r + 8)), (ap("PD", 0, 8), I_f, ap("q1"))])
-        ts(ap("D2", 0, 136, 17), ap("PD", 0, 8), 0.0, A.min)
-        cp(ap("po"), ap("ocj", 8 * r, 8 * r + 8))
-        tt(ap("ts"), ind(Xw, ap("po")), ap("ANj", 256 * r + 128, 256 * r + 256), A.min)
-        scan(ap("U2"), ap("NU"), ap("D2"), 0.0, A.mult, A.add)
+        limits("h", r, CFG["home"])
+        tt(ap("ts"), ind(Xw, ap("ocj", 8 * r, 8 * r + 8)), ap("ANj", 256 * r + 128, 256 * r + 256), A.min)
+        scan(ap("U2"), ap("NU"), ap("D2j", 136 * r, 136 * r + 136), 0.0, A.mult, A.max)
         cp(ap("osh"), ap("U2", 16, 136, 17))
         tt(ind(Xw, ap("osh")), ap("ts"), ap("ANj", 256 * r, 256 * r + 128), A.add)
-        act(ap("r1"), ap("SS"), bias=MAG - 0.5, scale=0.5)
-        act(zs("j", r + 1), ap("r1"), F.Relu, bias=-MAG)
+        act(ap("r1"), ap("SS"), bias=MAG, scale=0.4995)
+        act(Zj, ap("r1"), bias=-MAG)
         n0 = (r + 1) * ZW
         if r + 1 < RO:
-            cnt = col("acc", 0)
-            if len(CHJ) == 2:
-                cnt = col("par", 0)
-                act(cnt, col("acc", 0), bias=col("acc", 1))
-            act(col("par", 1), cnt, bias=1.5 * MAG, scale=0.5)
-            act(col("par", 2), col("par", 1), bias=-1.5 * MAG)
-            act(col("par", 3), col("par", 2), F.Abs, bias=cnt, scale=-2.0)
-            act(ap("ftmp"), ap("cA"), scale=col("par", 3))
-            send(SB - SC, zs("c", r + 1), zs("j", r + 1))
-            tt(ap("Zj", n0 + 128, n0 + ZW), ap("ftmp"), ap("cB"), A.add)
-            send(SB - SC, ap("Zc", n0 + 128, n0 + ZW), ap("Zj", n0 + 128, n0 + ZW))
-            quarters(("ANj", 256 * (r + 1)))
-            send(-SC, ap("Zh", n0, n0 + ZW), ap("Zj", n0, n0 + ZW))
+            turned(ap("ZTs", n0, n0 + 128), Zj, -MID, q3(4, 8))
+            act(col("pt", 0), col("acc", 0), bias=-0.25, scale=-1.0 / 512)
+            act(beta("s", r + 1), col("pt", 0), bias=col("acc", 0), scale=512.0)
+            act(col("eps", r + 1), beta("s", r + 1), bias=10.0 / 256, scale=-1.0 / 65536)
+            send(SB - SC, ap("ZTc", n0, n0 + ZW), ap("ZTs", n0, n0 + ZW))
+            send(-SC, ap("ZTh", n0, n0 + ZW), ap("ZTs", n0, n0 + ZW))
+            quarters(("ANj", 256 * (r + 1)), ap("SS"), -0.125, 255.4375)
             send(SB - SC, ap("ANc", 256 * (r + 1), 256 * (r + 2)), ap("ANj", 256 * (r + 1), 256 * (r + 2)))
-        else:
-            send(-SC, zs("h", RO), zs("j", RO))
-            dma("Y", ap("ysect"), Xm, 4.5)
-            dma("Y", ap("yamt"), zs("h", RO), 2.0)
-
-        ts(ap("FA"), ap("isS"), fc("h", r, 3), A.mult, fc("h", r, 4), A.add)
-        over("h", S_HOME, "Vuh", r, "IH")
-        if r + 1 < RO:
-            transposed("c", zs("c", r + 1))
-            limits("c", S_CUT, (0, 1))
-        for c, (b0, b1) in enumerate(CH):
-            a, b = 16 * b0, 16 * b1
-            old, vf, bk = ap("Tfh", R + a, R + b), ap("Vf", a, b), "P2" if c else "PD"
-            first[0] = 1 - c
-            cp(vf, ap("Vuh", R + a, R + b))
-            group([(ap(bk, 2 * a, 2 * b, 2), ap("Ih"), old), (ap(bk, 2 * a, 2 * b, 2), ap("nIh"), vf)])
-            group([(ap(bk, 2 * a + 1, 2 * b, 2), ap("Ih"), old), (ap(bk, 2 * a + 1, 2 * b, 2), ap("Ih"), vf)])
-            o = ap("PK", slice(b0 // 2, b1 // 2), ALL) if c else ap("PC", 128 + a, 128 + b)
-            group([(o, I_b, ap("FA", a, b)), (o, ap("n64"), ap("fmh", R + a, R + b)), (o, ap("n128"), ap("aph", R + a, R + b))] +
-                  [(o, sel(k), ap("IH", 16 * a + k, 16 * b, 16)) for k in range(16)])
-            act(ap("up", 2 * a + 1, 2 * b, 2), o, F.Sign, bias=col("half", 0))
-            scan(ap("tt", 2 * a, 2 * b), ap("up", 2 * a, 2 * b), ap(bk, 2 * a, 2 * b), 0.0, A.mult, A.add)
-            new = ap("Tfh", R + 128 + a, R + 128 + b)
-            if r + 1 < RO:
-                cp(ap("Tuh", R + 128 + a, R + 128 + b), ap("tt", 2 * a + 1, 2 * b, 2))
-            act(new, ap("tt", 2 * a + 1, 2 * b, 2))
-            if r + 1 < RO:
-                send_points(r + 1, c)
-            else:
-                dma("S" if c else "Y", ap("ytraj", a, b), new, 2.0)
-        first[0] = 0
-        if r + 1 < RO and EARLY:
             judge_limits(r + 1)
+        else:
+            send(-SC, ap("Zy"), Zj)
+            dma("Y", ap("ysect"), Xm, 4.5)
+            dma("Y", ap("yamt"), ap("Zy"), 2.0)
+
+        stage[0] = "h%d" % r
+        for u in CFG["home"]:
+            b0, b1, way, _ = u
+            first[0] = ahead(b0)
+            src, o = ind(Xm, ap("Vuh", R + 16 * b0, R + 16 * b1)), ap("IH", 256 * b0, 256 * b1)
+            if way == "T":
+                tt(o, src, ap("THh", 256 * b0, 256 * b1), A.is_gt)
+            elif way == "C":
+                p = spread("h", r, u, True, True)
+                act(ap("RAh", 256 * b0, 256 * b1), src, bias=over, scale=-1.0)
+                tt(o, p, ap("RAh", 256 * b0, 256 * b1), A.is_gt)
+            else:
+                step(o, summed("h", r, u, "Vuh"), -128.0)
+        first[0] = 0
         if r + 1 < RO:
+            limits("c", r + 1, CFG["cut"])
+        for c, (b0, b1) in enumerate(CJ):
+            a, b = 16 * b0, 16 * b1
+            old, vf, bk, e = ap("Tfh", R + a, R + b), ap("Vf", a, b), CFG["pb"][c], 272 + 2 * (b - a)
+            first[0] = len(CJ) - 1 - c
+            ts(vf, ap("Vuh", R + a, R + b), -HALF, A.add)
+            group([(ap(bk, 272, e, 2), I_b, old), (ap(bk, 272, e, 2), ap("nIb"), vf)])
+            mm(ap(bk, 273, e, 2), I_b, vf)
+            o = part(CFG["ob"][c], b0, b1)
+            group([(o, I_b, ap("c384", a, b)), (o, ap("n35"), ap("fmh", R + a, R + b))] +
+                  [(o, sel(k), ap("IH", 16 * a + k, 16 * b, 16)) for k in range(16)] + [(o, ap("nIb"), ap("aph", R + a, R + b))])
+            step(ap("up", 2 * a + 1, 2 * b, 2), o, beta("h", r))
+            scan(ap("tt", 2 * a, 2 * b), ap("up", 2 * a, 2 * b), ap(bk, 272, e), 0.0, A.mult, A.add)
+            new = ap("tt", 2 * a + 1, 2 * b, 2)
+            if r + 1 < RO:
+                u_ = ap("Tuh", R + 128 + a, R + 128 + b)
+                ts(u_, new, HALF, A.add)
+                send(SB, ap("Tuc", R + 128 + a, R + 128 + b), u_)
+                act(ap("Tfh", R + 128 + a, R + 128 + b), new)
+            else:
+                act(ap("To", a, b), new, bias=HALF)
+                dma("S" if c == len(CJ) - 1 else "Y", ap("ytraj", a, b), ap("To", a, b), 2.0)
+        first[0] = 0
+        if r + 1 < RO:
+            u_, f_ = ap("Tuh", R + 128, R + 256), ap("Tfh", R + 128, R + 256)
+            send(SB, ap("Tfc", R + 128, R + 256), f_)
+            send(SC, ap("Tfj", slice(4 * r + 4, 4 * r + 8), ALL), f_)
+            send(SC, ap("Tuj", R + 128, R + 256), u_)
             cp(ind(Xw, ap("osh")), ap("ts"))
     return ops
 
@@ -506,7 +565,7 @@ def order(ops):
     way = [0.0] * n
     for i in range(n - 1, -1, -1):
         way[i] = ops[i]["cost"] + ops[i]["lat"] + max([way[u] + hop(i, u) for u in users[i]], default=0.0)
-    way = [w + URGE.get(o["key"], 0.0) + FIRST * o["first"] for o, w in zip(ops, way)]
+    way = [w + CFG["first"] * o["first"] for o, w in zip(ops, way)]
     left = [len(o["deps"]) for o in ops]
     ready, end, free = [0.0] * n, [0.0] * n, {}
     pool = {}
@@ -541,78 +600,6 @@ def order(ops):
     return seq, max(end)
 
 
-def polish(ops, seq, steps):
-    n = len(ops)
-    eng = [o["eng"] for o in ops]
-    cost = [o["cost"] for o in ops]
-    users = [[] for _ in range(n)]
-    for i, o in enumerate(ops):
-        for d in o["deps"]:
-            users[d].append((i, o["cost"] * 0 + ops[d]["cost"] + ops[d]["lat"] + (0.0 if eng[d] == eng[i] == "P" else COST["hop"])))
-    need = [len(o["deps"]) for o in ops]
-    qs = {}
-    for i, _ in seq:
-        qs.setdefault(eng[i], []).append(i)
-
-    def times():
-        left, start, by, nxt = need[:], [0.0] * n, [-1] * n, [-1] * n
-        for q in qs.values():
-            for a, b in zip(q, q[1:]):
-                nxt[a] = b
-                left[b] += 1
-        todo = [i for i in range(n) if not left[i]]
-        for i in todo:
-            s = start[i]
-            for u, d in users[i]:
-                if s + d > start[u]:
-                    start[u], by[u] = s + d, i
-                left[u] -= 1
-                if not left[u]:
-                    todo.append(u)
-            u = nxt[i]
-            if u >= 0:
-                if s + cost[i] > start[u]:
-                    start[u], by[u] = s + cost[i], i
-                left[u] -= 1
-                if not left[u]:
-                    todo.append(u)
-        if len(todo) < n:
-            return 1e9, None, None
-        i = max(range(n), key=lambda i: start[i] + cost[i] + ops[i]["lat"])
-        t, held = start[i] + cost[i] + ops[i]["lat"], []
-        while by[i] >= 0:
-            if nxt[by[i]] == i and by[i] not in ops[i]["deps"]:
-                held.append((by[i], i))
-            i = by[i]
-        return t, held, start
-
-    x = [12345]
-
-    def draw(k):
-        x[0] = (x[0] * 6364136223846793005 + 1442695040888963407) % (1 << 64)
-        return (x[0] >> 33) % k
-
-    cur, held, start = times()
-    best, keep = cur, start
-    for it in range(steps):
-        a, b = held[draw(len(held))]
-        q = qs[eng[a]]
-        p, far = q.index(a), (0, 0, 1, 2, 4, 8)[draw(6)]
-        old = q[:]
-        if draw(2):
-            q.insert(max(0, p - far), q.pop(p + 1))
-        else:
-            q.insert(p + 1 + far, q.pop(p))
-        t, h, s = times()
-        if t <= cur + SLACK * (1 - it / steps) * draw(100) / 100:
-            cur, held = t, h
-            if t < best:
-                best, keep = t, s
-        else:
-            q[:] = old
-    return sorted(((i, keep[i]) for i in range(n)), key=lambda p: (p[1], p[0])), best
-
-
 def squeeze(ops, seq, turns):
     n = len(ops)
     cost, lat, eng = [o["cost"] for o in ops], [o["lat"] for o in ops], [o["eng"] for o in ops]
@@ -629,12 +616,15 @@ def squeeze(ops, seq, turns):
         for i, b in enumerate(before):
             for d, _ in b:
                 after[d].append(i)
-        free = sorted((rank[i], i) for i in range(n) if not left[i])
-        at, busy = [0.0] * n, {}
+        free = sorted((-rank[i], -i) for i in range(n) if not left[i])
+        at, busy = [0.0] * n, {e: [] for e in eng}
         while free:
-            i = free.pop(0)[1]
-            t = max([least[i]] + [at[d] + w for d, w in before[i]])
-            b = busy.setdefault(eng[i], [])
+            i = -free.pop()[1]
+            t = least[i]
+            for d, w in before[i]:
+                if at[d] + w > t:
+                    t = at[d] + w
+            b = busy[eng[i]]
             k = len(b)
             while k and b[k - 1][1] > t:
                 k -= 1
@@ -646,8 +636,10 @@ def squeeze(ops, seq, turns):
             for u in after[i]:
                 left[u] -= 1
                 if not left[u]:
-                    free.append((rank[u], u))
-            free.sort()
+                    x_, k = (-rank[u], -u), len(free)
+                    while k and free[k - 1] > x_:
+                        k -= 1
+                    free.insert(k, x_)
         return at
 
     x, at, best, keep = 777, [0.0] * n, 1e9, None
@@ -666,6 +658,91 @@ def squeeze(ops, seq, turns):
             at = now
         if t < best:
             best, keep = t, now
+    return sorted(((i, keep[i]) for i in range(n)), key=lambda p: (p[1], p[0])), best
+
+
+def anneal(plans, seq, steps, heat=0.15, seed=4321, alike=True):
+    ops = plans[0]
+    n = len(ops)
+    eng = [o["eng"] for o in ops]
+    names = sorted(set(eng))
+    en = [names.index(e) for e in eng]
+    deps = [sorted(o["deps"]) for o in ops]
+    costs = [[o["cost"] for o in p] for p in plans]
+    tails = [[o["cost"] + o["lat"] for o in p] for p in plans]
+    waits = [[[(d, p[d]["cost"] + p[d]["lat"] + (0.0 if eng[d] == eng[i] == "P" else p[i]["hop"])) for d in deps[i]] for i in range(n)] for p in plans]
+    at = [0.0] * n
+    for i, t in seq:
+        at[i] = t
+    key = [o["unit"] if alike else (o["unit"], o["round"]) for o in ops]
+    mid = {}
+    for i, o in enumerate(ops):
+        mid.setdefault(o["unit"], {}).setdefault(o["round"], at[i])
+    gaps = [m[1] - m[0] for m in mid.values() if 0 in m and 1 in m]
+    period = sorted(gaps)[len(gaps) // 2] if alike else 0.0
+    place = {}
+    for i, o in enumerate(ops):
+        r = 1 if alike and 1 in mid[o["unit"]] else o["round"]
+        place.setdefault(key[i], mid[o["unit"]][r] - period * r)
+    off = [period * o["round"] + 1e-6 * i for i, o in enumerate(ops)]
+
+    def times():
+        v = [0.0] * n
+        for i in range(n):
+            x = place[key[i]] + off[i]
+            for d in deps[i]:
+                if v[d] >= x:
+                    x = v[d] + 1e-7
+            v[i] = x
+        line = sorted(range(n), key=lambda i: v[i])
+        total, held = 0.0, []
+        for cost, tail, wait in zip(costs, tails, waits):
+            start, by, free, prev = [0.0] * n, [-1] * n, [0.0] * len(names), [-1] * len(names)
+            end, last = 0.0, -1
+            for i in line:
+                e = en[i]
+                t, b = free[e], -2 - prev[e]
+                for d, w in wait[i]:
+                    if start[d] + w > t:
+                        t, b = start[d] + w, d
+                start[i], by[i] = t, b
+                free[e], prev[e] = t + cost[i], i
+                if t + tail[i] > end:
+                    end, last = t + tail[i], i
+            total += end
+            while last != -1:
+                b = by[last]
+                if b < -1:
+                    b = -2 - b
+                    if key[b] != key[last]:
+                        held.append((b, last))
+                last = b
+        return total / len(plans), held, v, start
+
+    x = [seed]
+
+    def draw():
+        x[0] = (x[0] * 6364136223846793005 + 1442695040888963407) % (1 << 64)
+        return (x[0] >> 33) / float(1 << 31)
+
+    cur, held, v, start = times()
+    best, keep = cur, start
+    for it in range(steps):
+        if held and draw() < 0.7:
+            a, b = held[int(draw() * len(held))]
+            k, to = (key[b], v[a] - off[b] - draw() ** 2) if draw() < 0.5 else (key[a], v[b] - off[a] + draw() ** 2)
+        else:
+            k = key[int(draw() * n)]
+            to = place[k] + 2 * (draw() - 0.5)
+        old = place[k]
+        place[k] = to
+        t, h, w, s = times()
+        if t <= cur + heat * (1 - it / steps) * draw():
+            cur, held, v = t, h, w
+            if t < best:
+                best, keep = t, s
+        else:
+            place[k] = old
     return sorted(((i, keep[i]) for i in range(n)), key=lambda p: (p[1], p[0])), best
 
 
@@ -721,8 +798,10 @@ def rank_program(g, core, T, topo):
                 ins = q.activation(r[0], r[1], r[2], bias=r[3], scale=r[4], accum_out=r[5])
             elif k == "matmul":
                 ins = q.matmul(*r)
+                for m in o["more"]:
+                    ins = q.matmul(*[res(x) for x in m])
             elif k == "iota":
-                ins = q.iota(*r)
+                ins = q.iota(*r, allow_small_or_imprecise_dtypes=SCRATCH[a[0][0]][2] != i32)
             elif k == "tensor_copy":
                 ins = q.tensor_copy(*r)
             elif k == "tensor_tensor":

@@ -5,20 +5,24 @@ from concourse.mybir import AluOpType as A, ActivationFunctionType as F
 N, RO, SB, SC = 6, 3, 2, 5
 W, L, Q = 4096, 128, 2048
 DUM, EXT, XW = W, W + L, W + 2 * L
-COST = {"V": 0.03, "S": 0.07, "cyc": 0.00086, "pe": 0.00045, "gather": 1.56, "scatter": 3.8, "link": 2.0, "hop": 0.2, "call": 0.4, "byte": 0.002, "P": 0.0}
+COST = {"V": 0.025, "S": 0.065, "cyc": 0.00086, "pe": 0.00045, "gather": 1.56, "scatter": 3.8, "link": 2.0, "hop": 0.18, "same": 0.15,
+        "call": 0.2, "byte": 0.0007, "P": 0.0}
 CFG = {
-    "cut": [(1, 2, "S", 3), (0, 1, "A", 0), (4, 6, "T", 2), (2, 4, "T", 1), (6, 8, "S", 2)],
-    "judge": [(0, 2, "T", 0), (2, 3, "S", 1), (3, 4, "T", 2), (6, 7, "S", 0), (4, 6, "S", 3), (7, 8, "S", 2)],
-    "home": [(2, 3, "T", 1), (4, 6, "T", 0), (0, 2, "T", 0), (6, 7, "T", 3), (3, 4, "A", 1), (7, 8, "A", 0)],
-    "points": 0, "so": 1, "sob": ("Q3", "B2"), "tn": (1, "Q2"), "ch": 4, "cj": (4,), "pl": "B1",
-    "rb": ("Q0", "Q2", "Q1", "B0"), "pb": ("Q1", "Q2", "B1", "B2"), "ob": ("Q0", "Q3", "B0", "B3"),
-    "first": 0.0,
+    "cut": [(0, 1, "V"), (1, 2, "S"), (2, 3, "S"), (3, 4, "T"), (4, 6, "S"), (6, 7, "T"), (7, 8, "S")],
+    "judge": [(0, 1, "T"), (1, 2, "T"), (2, 4, "S"), (4, 6, "A"), (6, 7, "T"), (7, 8, "S")],
+    "home": [(0, 2, "T"), (2, 3, "A"), (3, 4, "T"), (4, 6, "T"), (6, 7, "A"), (7, 8, "T")],
+    "so": 2, "ch": 4, "cj": (4, 6), "cp": 1, "war": 1, "ts": 1, "fl": 0, "cx": 4, "cxo": 0, "xa": 4096, "tf": "c", "ap": (4, 6),
+    "first": 0.5,
 }
-STEPS, SLACK, NUDGE = 1500, 0.3, 1.0
+STEPS, TRIES, SLACK, NUDGE = 600, 10, 0.3, 1.0
+MOVES = 1
+SPREAD = [{}, {"cyc": 0.00115, "pe": 0.0006, "gather": 1.8, "odd": 0.4}, {"link": 2.8, "call": 0.4, "odd": 0.8},
+          {"hop": 0.22, "same": 0.08, "link": 1.4, "V": 0.01}, {"odd": 0.6, "byte": 0.0015, "hop": 0.25, "same": 0.2}]
+EARLY = 0.1
 LOOK = 0.03
-ZW = 136
+AW = 392
 MAG = 8388608.0
-MID = 150.0
+ZO = 1152.0
 HALF = 2048.0
 bf, f16, f32, i32, u16 = "bfloat16", "float16", "float32", "int32", "uint16"
 
@@ -31,11 +35,11 @@ SCRATCH = {
     "X": sb(XW, bf), "MV": sb(XW, i32), "tr32": sb(128, i32), "cap32": sb(8, i32), "capf": sb(8, f32),
     "Tuc": sb(384, u16), "Tuj": sb(384, u16), "Tuh": sb(384, u16),
     "Tfc": sb(384, f16), "Tfj": sb((12, 32), f16), "Tfh": sb(384, f16), "To": sb(128, f32),
-    "Z0": sb(128, bf), "Zj": sb(128, bf), "Zy": sb(128, bf), "zcl": sb(128, bf),
-    "ZTc": sb(3 * ZW, bf), "ZTh": sb(3 * ZW, bf), "ZTs": sb(3 * ZW, bf), "ZTj": sb(128, bf),
-    "ANc": sb(768, bf), "ANj": sb(768, bf), "ANh": sb(256, bf),
+    "Z0": sb(128, bf), "Z1": sb(128, f16), "Zj": sb(128, f16), "Zy": sb(128, bf), "zcl": sb(128, bf),
+    "ZTc": sb(384, f16), "ZTh": sb(384, f16), "ZTs": sb(384, f16), "ZTj": sb(128, bf),
+    "ANc": sb(3 * AW, bf), "ANj": sb(3 * AW, bf), "ANh": sb(264, bf),
     "THc": sb(2048, bf), "THj": sb(2048, bf), "THh": sb(2048, bf),
-    "RAc": sb(2048, bf), "RAj": sb(2048, bf), "RAh": sb(2048, bf),
+    "RAc": sb(2048, f16), "RAj": sb(2048, bf), "RAh": sb(2048, f16),
     "IC": sb(2048, bf), "IM": sb((8, 256), bf), "IH": sb(2048, bf), "AJ": sb((128, 17), bf),
     "fms": sb(384, bf), "fmh": sb(384, bf), "sos": sb((24, 17), bf), "soj": sb(408, bf),
     "oc": sb(24, u16), "ocj": sb(24, u16), "D2s": sb(408, f32), "D2j": sb(408, f32),
@@ -43,22 +47,22 @@ SCRATCH = {
     "EQ": sb(1024, bf), "po": sb(8, u16), "tc": sb(128, bf),
     "Town": sb((8, 17), f32), "DT": sb(136, f32), "t2": sb(136, f32), "RR": sb(144, f32),
     "NU": sb(136, f32), "UU": sb(136, f32), "om": sb(32, u16), "of": sb(32, u16),
-    "Vus": sb(384, u16), "Vuh": sb(384, u16), "aps": sb(384, bf), "aph": sb(384, bf),
-    "SS": sb(128, f32), "r1": sb(128, f32), "acc": sb(8, f32), "pt": sb(8, bf), "eps": sb(8, bf),
+    "Vus": sb(384, u16), "Vuh": sb(384, u16), "aph": sb(408, bf),
+    "Yg": sb(128, f16), "sh": sb(384, bf), "acc": sb(8, f32), "pt": sb(8, bf), "eps": sb(8, bf),
     "tn": sb(128, i32), "U2": sb(136, f32), "osh": sb(8, u16), "ts": sb(128, bf), "ik": sb(136, i32),
     "Vf": sb(128, f16), "up": sb(256, bf), "tt": sb(256, f32),
-    "io": sb(168, i32), "io2": sb(512, i32), "io3": sb(512, i32), "ioc": sb(160, i32), "ioc2": sb(160, i32), "pc": sb(8, i32), "pcf": sb(8, f32),
+    "io": sb(168, i32), "ei": sb(512, bf), "pc": sb(8, i32), "pcf": sb(16, f32), "pcb": sb(8, bf),
     "ku": sb(256, f32), "U16": sb(256, bf), "M16": sb(256, bf),
     "Iw": sb(168, f32), "Dt": sb(160, bf), "Dw": sb(160, bf), "DE": sb(160, bf), "DO": sb(160, bf), "nIb": sb(128, bf), "I5": sb(128, bf),
     "Ib": sb(128, bf), "n35": sb(128, bf), "I32": sb(128, bf), "I8": sb(128, bf), "nI8": sb(128, bf),
     "nBO": sb(128, bf), "BOb": sb(128, bf), "BO8": sb(128, bf), "SW": sb(144, bf), "SW8": sb(144, bf), "E32": sb(512, bf),
-    "dg": sb(128, bf), "OD0": sb(128, bf), "OD1": sb(128, bf), "D0": sb(128, f32), "lf": sb(160, f32),
+    "dg": sb(128, bf), "OD0": sb(128, bf), "OD1": sb(128, bf), "D0": sb(128, f32),
     "DUM8": sb(8, f32), "CK": sb(136, bf), "Z136": sb(136, bf), "CB": sb(128, bf), "C21": sb(128, bf), "CT": sb(128, bf), "CQ": sb(128, bf),
     "FL": sb(144, bf), "C15": sb(128, bf), "c35": sb(128, bf), "c384": sb(128, bf),
-    "B0": ("psum", [128, 512], f32), "B1": ("psum", [128, 512], f32), "B2": ("psum", [128, 512], f32), "B3": ("psum", [128, 512], f32),
-    "Q0": ("psum", [128, 512], f32), "Q1": ("psum", [128, 512], f32), "Q2": ("psum", [128, 512], f32), "Q3": ("psum", [128, 16, 32], f32),
+    "B7": ("psum", [128, 16, 32], f32),
 }
-SEMAPHORES = ["V", "S", "P", "G", "sent"] + ["d%d" % i for i in range(20)] + ["m%d" % i for i in range(80)]
+SCRATCH.update(("B%d" % i, ("psum", [128, 512], f32)) for i in range(7))
+SEMAPHORES = ["V", "S", "P", "G", "sent", "mark"] + ["d%d" % i for i in range(20)] + ["m%d" % i for i in range(80)]
 IO_SHAPES = {"sect": [128, W], "mv": [128, Q], "traj": [128, L], "amt": [128, L], "cap": [128, 1],
              "ysect": [128, W], "ytraj": [128, L], "yamt": [128, L]}
 ALL = slice(None)
@@ -78,20 +82,20 @@ SPANS = {}
 
 
 def span(x):
-    k = (x[0], str(x[1][1:]))
+    k = (x[0][0] if is_psum(x) else x[0], str(x[1][1:]))
     if k not in SPANS:
-        shape = SCRATCH[x[0]][1] if x[0] in SCRATCH else IO_SHAPES[x[0]]
+        shape = SCRATCH[{"#": "B0", "%": "B7"}.get(x[0][0], x[0])][1] if x[0] not in IO_SHAPES else IO_SHAPES[x[0]]
         e = np.arange(int(np.prod(shape[1:]))).reshape(shape[1:])[x[1][1:]]
         SPANS[k] = (int(np.min(e)), int(np.max(e)) + 1, int(np.size(e)))
     return SPANS[k]
 
 
 def is_psum(x):
-    return x[0] in SCRATCH and SCRATCH[x[0]][0] == "psum"
+    return x[0][0] in "#%"
 
 
 def two_bytes(x):
-    return SCRATCH[x[0]][2] in (bf, f16, u16)
+    return not is_psum(x) and SCRATCH[x[0]][2] in (bf, f16, u16)
 
 
 def plan():
@@ -103,7 +107,7 @@ def plan():
 
     def add(eng, kind, args, reads, writes, cost, lat=0.0):
         me = len(ops)
-        deps = set()
+        deps, fed = set(), set()
         for x, wr in [(x, False) for x in reads] + [(x, True) for x in writes]:
             lo, hi, _ = span(x)
             if is_psum(x):
@@ -112,6 +116,7 @@ def plan():
                     before, now = now, []
                 deps.update(o for (_, _, _, o) in before)
                 deps.update(o for (a, b, w, o) in now if o != me and a < hi and lo < b and (w or wr))
+                fed.update(o for (a, b, w, o) in now if a < hi and lo < b and w)
                 if eng == "P" and now:
                     deps.add(now[-1][3])
                 last[x[0]] = (eng, before, now + [(lo, hi, wr, me)])
@@ -120,17 +125,22 @@ def plan():
             for (a, b, w, o) in last.get(x[0], []):
                 if o != me and a < hi and lo < b and (w or wr):
                     deps.add(o)
+                    if w:
+                        fed.add(o)
                 if not (wr and lo <= a and b <= hi and span(x)[2] == hi - lo):
                     keep.append((a, b, w, o))
             last[x[0]] = keep + [(lo, hi, wr, me)]
         deps.discard(me)
-        k = (stage[0], eng, writes[0][0])
+        free = set(d for d in deps if ops[d]["eng"] == eng and (eng == "P" or CFG["war"] and d not in fed and
+                                                                  kind not in ("dma", "send") and ops[d]["kind"] not in ("dma", "send")))
+        name = writes[0][0].split(".")[0]
+        k = (stage[0], eng, name)
         seen[k] = seen.get(k, 0) + (eng != "P")
-        key = stage[0][:1] + eng + writes[0][0] + str(seen[k])
+        key = stage[0][:1] + eng + name + str(seen[k])
         k = k + ("unit",)
         seen[k] = seen.get(k, 0) + (eng != "P" or args[3])
-        ops.append({"eng": eng, "kind": kind, "args": args, "deps": deps, "cost": cost, "lat": lat, "key": key, "first": first[0],
-                    "unit": key + "." + str(seen[k]), "round": int(stage[0][1:] or 0), "hop": COST["hop"]})
+        ops.append({"eng": eng, "kind": kind, "args": args, "deps": deps, "free": free, "turns": set(x[0] for x in reads + writes if is_psum(x)), "cost": cost, "lat": lat, "key": key, "first": first[0],
+                    "unit": key + "." + str(seen[k]), "round": int(stage[0][1:] or 0), "hop": COST["hop"], "same": COST["same"]})
 
     def sides(xs):
         r = []
@@ -162,7 +172,7 @@ def plan():
         compute("V", "tensor_scalar", out, [a, s1, s2], (out, a, s1, s2, op0) + ((op1,) if op1 is not None else ()), 1)
 
     def scan(out, d0, d1, init, op0, op1):
-        compute("V", "tensor_tensor_scan", out, [d0, d1], (out, d0, d1, init, op0, op1), 1)
+        compute("V", "tensor_tensor_scan", out, [d0, d1, init], (out, d0, d1, init, op0, op1), 1)
 
     def ms(out, v):
         compute("V", "memset", out, [], (out, v), 1)
@@ -196,66 +206,70 @@ def plan():
         ops[-1]["deps"].update(after)
 
     def send(by, dst, src):
-        add("G", "send", (by % N, dst, src), [src], [dst], COST["call"], LAT + span(src)[2] * (2 if two_bytes(src) else 4) * COST["byte"])
+        add("G", "send", (by % N, dst, src), [src], [dst], COST["call"] + span(src)[2] * (2 if two_bytes(src) else 4) * COST["byte"], LAT)
+        return len(ops) - 1
+
+    def mark(after):
+        add("G", "mark", (), [], [ap("pc", 7, 8)], 0.02)
+        ops[-1]["deps"] = set(after)
+        ops[-1]["free"] = set(after)
+        return len(ops) - 1
 
     CYC, PCYC, GA, LAT = COST["cyc"], COST["pe"], COST["gather"], COST["link"]
     sel = lambda a: ap("SW", 15 - a, 143 - a)
     I_b, I_f = ap("Ib"), ap("Iw", 16, 144)
     col = lambda name, c: ap(name, c, c + 1)
-    q3 = lambda a, b: ap("Q3", slice(a, b), ALL)
-    part = lambda bank, a, b: ap(bank, slice(a, b), slice(0, 16)) if bank == "Q3" else ap(bank, 16 * a, 16 * b)
+    turn = lambda name: name + "." + str(len(ops))
     CH, CJ = [(0, CFG["ch"]), (CFG["ch"], 8)], list(zip((0,) + CFG["cj"], CFG["cj"] + (8,)))
     ahead = lambda b0: sum(b0 < e for e in CFG["cj"])
     Xm, Xw, Xe, Zj = ap("X", 0, W), ap("X", 0, EXT), ap("X", 0, XW), ap("Zj")
-    beta = lambda who, r: col("ZT" + who, r * ZW + 128)
-    cap, less, over = col("capf", 0), col("capf", 1), col("capf", 2)
+    an = lambda who, r, k: ap("AN" + who, AW * r + 128 * k, AW * r + min(128 * k + 128, 264))
+    beta = lambda who, r: col("aph", 136 * r) if who == "h" else col("AN" + who, AW * r + 256)
+    less, over = col("capf", 1), col("capf", 2)
 
     stage[0] = "0"
     dma("Y", ap("tr32"), ap("traj"), 1.9)
     dma("S", ap("Z0"), ap("amt"), 1.9)
-    dma("S", col("cap32", 0), ap("cap"), 1.9)
-    dma("Y", Xm, ap("sect"), 4.5)
-    dma("Y", ap("MV", 0, Q), ap("mv"), 4.5, [3])
-    dma("Y", ap("MV", Q, W), ap("mv"), 7.0, [3])
+    dma("Y", col("cap32", 0), ap("cap"), 1.9)
+    dma("Y", ap("X", 0, CFG["xa"]), ap("sect", 0, CFG["xa"]), 1.7 + 2.8 * CFG["xa"] / W, [0, 2])
+    ops[-1]["free"] = {0, 2}
 
     iota(ap("ku"), [[0, 16], [1, 16]], 0, 0)
     step(ap("U16"), ap("ku"), 256 * 14.5, -256.0, more=1.3)
     if any(u[2] in "TA" for u in CFG["cut"]):
         step(ap("M16"), ap("ku"), -128.0)
-    for b0, b1, way, _ in CFG["cut"]:
+    for b0, b1, way in CFG["cut"]:
         if way == "T":
-            ms(ap("RAc", 256 * b0 + 15, 256 * b1, 16), -256.0)
+            ms(ap("RAc", 256 * b0 + 15, 256 * b1, 16), -2000.0)
     iota(ap("io"), [[1, 168]], -16, -1)
-    iota(ap("ioc"), [[1, 160]], 0, 0)
-    iota(col("pc", 0), [[0, 1]], 0, 1)
-    iota(ap("io2"), [[1, 32], [0, 16]], 128, -1)
-    ts(col("pc", 1), col("pc", 0), 15, A.bitwise_and)
-    ts(col("pc", 2), col("pc", 0), 4, A.arith_shift_right)
-    ts(col("pc", 3), col("pc", 0), 4, A.arith_shift_right, 1, A.bitwise_and)
+    iota(col("pc", 4), [[0, 1]], 0, 1)
+    iota(ap("ei"), [[1, 32], [0, 16]], 0, 0)
+    ts(col("pc", 0), col("pc", 4), 31, A.bitwise_and)
+    ts(col("pc", 1), col("pc", 4), 15, A.bitwise_and)
+    ts(col("pc", 2), col("pc", 4), 4, A.arith_shift_right)
+    ts(col("pc", 3), col("pc", 4), 4, A.arith_shift_right, 1, A.bitwise_and)
     cp(ap("pcf", 0, 4), ap("pc", 0, 4))
+    cp(ap("pcb", 0, 4), ap("pc", 0, 4))
+    act(col("pcf", 8), col("pcf", 1), bias=float(DUM))
     ts(col("pcf", 4), col("pcf", 3), -1.0, A.mult, 1.0, A.add)
     ts(col("pcf", 5), col("pcf", 1), 15.0, A.is_equal, 128.0, A.mult)
     ts(col("pcf", 6), col("pcf", 1), 0.0, A.is_gt)
     ts(ap("Iw"), ap("io"), 0.0, A.is_equal)
     act(ap("Ib"), I_f)
-    ts(ap("io3"), ap("io2"), 31, A.bitwise_and)
-    ts(ap("E32"), ap("io3"), 0.0, A.is_equal)
-    ts(ap("ioc2"), ap("ioc"), 4, A.arith_shift_right)
-    ts(ap("BOb"), ap("ioc2", 0, 128), col("pcf", 2), A.is_equal)
+    ts(ap("E32"), ap("ei"), col("pcb", 0), A.is_equal)
+    ts(ap("BOb"), ap("ei", 0, 128), col("pcb", 2), A.is_equal)
     ms(ap("SW"), 0.0)
     cp(ap("SW", 15, 143, 16), ap("BOb", 0, 128, 16))
     act(ap("SW8"), ap("SW"), scale=8192.0)
     act(col("pcf", 7), col("pcf", 5), scale=-HALF / 128)
     ms(ap("X", W, EXT), 0.0)
-    ts(ap("ioc2"), ap("ioc"), 15, A.bitwise_and)
-    ts(ap("dg"), ap("ioc2", 0, 128), col("pcf", 1), A.is_equal)
-    cp(ap("lf"), ap("ioc"))
+    ts(ap("dg"), ap("ku", 0, 128), col("pcf", 1), A.is_equal)
     act(ap("OD0"), ap("dg"), bias=8192.0, scale=-8192.0)
     act(ap("OD1"), ap("dg"), bias=8192.0, scale=-16384.0)
-    ts(ap("DUM8"), ap("lf", 0, 128, 16), col("pcf", 1), A.add, float(DUM), A.add)
-    ts(ap("D0"), ap("lf", 0, 128), DUM + 1.0, A.add)
-    tt(ap("D0"), ap("D0"), ap("dg"), A.mult)
-    ts(ap("D0"), ap("D0"), -1.0, A.add)
+    act(ap("DUM8"), ap("ei", 0, 128, 16), bias=col("pcf", 8), scale=16.0)
+    act(ap("S0"), ap("ei", 0, 128), bias=col("pcf", 8), scale=16.0)
+    act(ap("S1"), ap("dg"), bias=-1.0, scale=8192.0)
+    tt(ap("D0"), ap("S0"), ap("S1"), A.min)
     act(ap("Dt"), ap("Iw", 1, 161), scale=col("pcf", 6))
     tt(ap("Dw"), ap("Iw", 0, 160), ap("Dt"), A.subtract)
     act(ap("nBO"), ap("BOb"), scale=-1.0)
@@ -270,7 +284,7 @@ def plan():
     act(ap("I8"), I_f, scale=8192.0)
     ms(ap("c35"), -3.5)
     act(ap("C15"), ap("c35"), bias=col("pcf", 5))
-    ms(ap("c384"), -800.0)
+    ms(ap("c384"), 32.0 - 8192)
     act(ap("C21"), ap("C15"), bias=3.5 * (HALF - EXT) / 128, scale=(HALF - EXT) / 128)
     ms(ap("CT"), 0.0)
     act(ap("CT", 15, 128, 16), ap("DUM8"), bias=float(DUM), scale=-1.0)
@@ -287,32 +301,34 @@ def plan():
     ms(ap("AJ", ALL, 16), 0.0)
     ms(ap("Z136"), 0.0)
     ms(ap("RR"), 0.0)
-    ms(ap("FL"), -576.0)
-    ms(ap("FL", 0, 1), -832.0)
+    if CFG["fl"]:
+        ms(ap("FL", 16, 144), 0.0)
+        ms(ap("FL", 0, 16), 0.0)
+        ms(ap("FL", 0, 1), 1.0)
     ms(ap("MV", W, EXT), 0)
-    ms(ap("ZTh", 128, ZW), 0.0)
-    for r in range(1, RO):
-        ms(ap("ZTs", r * ZW + 128, r * ZW + ZW), 0.0)
+    ms(an("h", 0, 2), 0.0)
+    for r in range(RO):
+        ms(an("j", r, 2), 0.0)
     ms(col("eps", 0), 10.0 / 256)
-    cp(cap, col("cap32", 0))
-    ts(less, cap, -1.0, A.mult, MID, A.add)
-    ts(over, cap, -MID, A.add)
+    ts(less, col("cap32", 0), -1.0, A.mult, -ZO, A.add)
+    ts(over, col("cap32", 0), ZO, A.add)
 
-    def quarters(an, s, scale, bias):
-        act(ap(an[0], an[1] + 128, an[1] + 256), s, bias=bias, scale=scale)
-        act(ap(an[0], an[1], an[1] + 128), ap(an[0], an[1] + 128, an[1] + 256), bias=255.0, scale=-1.0)
+    def quarters(who, r, s, scale, bias):
+        act(an(who, r, 1), s, bias=bias, scale=scale)
+        act(an(who, r, 0), an(who, r, 1), bias=255.0, scale=-1.0)
 
-    def turned(out, z, bias, bank):
-        mm(bank, z, I_b)
-        act(out, bank, bias=bias)
+    def turned(out, z, bias):
+        p = ap(turn("#z"), 0, 128)
+        mm(p, z, I_b)
+        act(out, p, bias=bias)
 
     def spread(who, r, u, start, stop):
-        b0, b1, _, bk = u
+        b0, b1, _ = u
         j = b0 // 2
         rows = slice(32 * j, 32 * j + 32)
         lo, hi = 256 * (b0 - 2 * j), 256 * (b1 - 2 * j)
-        z = ap("ZTj", rows=rows) if who == "j" else ap("ZT" + who, r * ZW, r * ZW + 128, rows=rows)
-        p = ap("B%d" % bk, lo, hi)
+        z = ap("ZTj", rows=rows) if who == "j" else ap("ZT" + who, 128 * r, 128 * r + 128, rows=rows)
+        p = ap(turn("#%s%d" % (who, b0)), 0, hi - lo)
         mm(p, z, ap("E32", lo, hi, rows=rows), start, stop)
         return p
 
@@ -323,7 +339,7 @@ def plan():
                 act(ap("TH" + who, 256 * u[0], 256 * u[1]), p, bias=0.0 if who == "j" else over, scale=-1.0)
 
     def summed(who, r, u, offs):
-        b0, b1, way, _ = u
+        b0, b1, way = u
         src = ind(Xm, ap(offs, 128 * r + 16 * b0, 128 * r + 16 * b1))
         raw = ap("RA" + who, 256 * b0, 256 * b1)
         p = spread(who, r, u, True, False)
@@ -338,39 +354,51 @@ def plan():
         return p
 
     def judge_limits(r):
-        dma("Y", ap("X", EXT, XW), Zj, 2.0)
-        ts(ap("zcl"), Zj, cap, A.subtract, 1.0, A.min)
-        turned(ap("ZTj"), ap("zcl"), 0.0, q3(4, 8))
+        ts(ap("zcl"), Zj, over, A.subtract, 1.0, A.min)
+        turned(ap("ZTj"), ap("zcl"), 0.0)
 
     def judge_points(r):
-        seg = slice(4 * r, 4 * r + 4)
-        g_ = [(q3(8, 12), I_b, ap("CQ")), (q3(8, 12), I_b, ap("C21"))]
+        seg, bk = slice(4 * r, 4 * r + 4), turn("%t")
+        p = ap(bk, slice(0, 4), ALL)
+        g_ = [(p, I_b, ap("CQ")), (p, I_b, ap("C21"))]
         for h, (m0, m1) in enumerate([(ap("DE", 16, 144), ap("DE", 0, 128)), (ap("DO", 32, 160), ap("DO", 16, 144))]):
-            o = ap("Q3", slice(8, 12), slice(16 * h, 16 * h + 16))
+            o = ap(bk, slice(0, 4), slice(16 * h, 16 * h + 16))
             g_ += [(o, m0, ap("Tfj", seg, slice(0, 16))), (o, m1, ap("Tfj", seg, slice(16, 32)))]
         group(g_)
         o = ap("Town", ALL, slice(0, 16))
-        compute("V", "transpose", o, [q3(8, 12)], (o, q3(8, 12)), 1)
+        compute("V", "transpose", o, [p], (o, p), 1)
         act(ap("DT"), ap("Town"))
 
     def new_points(r):
-        o = part(CFG["tn"][1], 8, 16)
+        o = ap(turn("#n"), 0, 128)
         group([(o, ap("I5"), ap("Tfj", slice(4 * r, 4 * r + 4), ALL)), (o, ap("BOb"), Zj)])
-        ts(ap("tn"), o, 5 * HALF + 1, A.add)
+        ts(ap("tn"), o, 5 * HALF + 1 - 16 * ZO, A.add)
         ts(ap("MV", EXT, XW), ap("tn"), W - 1, A.bitwise_and)
+
+    def halved(by, out, who, a, b):
+        if who in CFG["tf"]:
+            send(by, out, ap("Tfh", a, b))
+        else:
+            ts(out, ap("Tu" + who, a, b), -HALF, A.add)
 
     cp(ap("Tuh", 0, 128), ap("tr32"))
     ts(ap("Tfh", 0, 128), ap("tr32"), -HALF, A.add)
-    turned(ap("ZTh", 0, 128), ap("Z0"), -MID, q3(4, 8))
-    send(SB, ap("ZTc", 0, ZW), ap("ZTh", 0, ZW))
-    send(SB, ap("Tuc", 0, 128), ap("Tuh", 0, 128))
-    send(SC, Zj, ap("Z0"))
-    send(SB, ap("Tfc", 0, 128), ap("Tfh", 0, 128))
-    quarters(("ANh", 0), ap("Z0"), -0.25, 255.375)
-    send(SB, ap("ANc", 0, 256), ap("ANh"))
+    turned(ap("ZTh", 0, 128), ap("Z0"), ZO)
+    early = [send(SB, ap("ZTc", 0, 128), ap("ZTh", 0, 128)), send(SB, ap("Tuc", 0, 128), ap("Tuh", 0, 128))]
+    if CFG["xa"] < W:
+        dma("Y", ap("X", CFG["xa"], W), ap("sect", CFG["xa"], W), 1.7 + 2.8 * (1 - CFG["xa"] / W), [mark(early)])
+    act(ap("Z1"), ap("Z0"), bias=ZO)
+    send(SC, Zj, ap("Z1"))
+    act(ap("X", EXT, XW), Zj, bias=ZO - 1, scale=-1.0)
+    halved(SB, ap("Tfc", 0, 128), "c", 0, 128)
+    quarters("h", 0, ap("Z0"), -0.25, 255.375)
+    send(SB, ap("ANc", 0, 264), ap("ANh"))
     send(SC, ap("Tuj", 0, 128), ap("Tuh", 0, 128))
-    send(SC, ap("Tfj", slice(0, 4), ALL), ap("Tfh", 0, 128))
-    send(SC, ap("ANj", 0, 256), ap("ANh"))
+    halved(SC, ap("Tfj", slice(0, 4), ALL), "j", 0, 128)
+    send(SC, ap("ANj", 0, 256), ap("ANh", 0, 256))
+    early = mark([i for i, o in enumerate(ops) if o["kind"] == "send"])
+    dma("Y", ap("MV", 0, Q), ap("mv"), 6.0, [early])
+    dma("Y", ap("MV", Q, W), ap("mv"), 9.0, [early])
     limits("c", 0, CFG["cut"])
     judge_limits(0)
 
@@ -378,7 +406,7 @@ def plan():
         R = 128 * r
         stage[0] = "c%d" % r
         for u in CFG["cut"]:
-            b0, b1, way, _ = u
+            b0, b1, way = u
             first[0] = ahead(b0)
             if way in "TA":
                 if way == "T":
@@ -390,68 +418,84 @@ def plan():
             else:
                 p = summed("c", r, u, "Tuc")
                 for b in range(b0, b1):
-                    scan(ap("IM", b, ALL), ap(p[0], 256 * (b % 2), 256 * (b % 2) + 256), ap("U16"), 0.0, A.max, A.min)
+                    scan(ap("IM", b, ALL), ap(p[0], 256 * (b - b0), 256 * (b - b0) + 256), ap("U16"), 0.0, A.max, A.min)
         first[0] = 0
-        mm(ap("Q1", 0, 128), ap("Dt", 16, 144), ap("Tfc", R, R + 128))
-        act(ap("Tsh"), ap("Q1", 0, 128), bias=col("pcf", 7))
         act(ap("CB"), ap("C15"), bias=beta("c", r), scale=256.0)
-        for b0, b1 in CH:
-            o = ap("Q0", 16 * b0, 16 * b1)
+        for c, (b0, b1) in enumerate(CH):
+            if CFG["cp"] or not c:
+                cnt = turn("#a%d" % c)
+            o = ap(cnt, 16 * b0, 16 * b1)
             group([(o, ap("I32"), ap("CB", 16 * b0, 16 * b1))] +
                   [(o, ap("SW8", 15 - k, 143 - k), ap("IM", slice(b0, b1), slice(k, 256, 16))) for k in range(15)])
-        y0, y1, pl = ap("Y", 0, 128), ap("Y", 128, 256), CFG["pl"]
-        tt(y0, ap("Q0", 0, 128), ap("Tfc", R, R + 128), A.min)
-        tt(y1, ap("Q0", 0, 128), ap("Tsh"), A.min)
-        fm = ap("fms", R, R + 128)
-        step(fm, ap("Q0", 0, 128), 0.0, 1.0 / 32)
-        place = lambda o: [(o, ap("BOb"), y0), (o, ap("nBO"), y1)]
-        group([(ap("Q2", 0, 128), I_b, ap("OD0"))] + place(ap("Q2", 0, 128)))
-        group(place(ap(pl, 128, 256)))
-        scan(ap("S0"), ap("D0"), ap("Q2", 0, 128), -1.0, A.max, A.min)
-        mm(ap("Q1", 128, 256), I_b, ap("OD1"), True, False)
-        for x in place(ap("Q1", 128, 256)):
-            mm(*x, False, False)
-        for s in range(8):
-            e = ap("EQ", 128 * s + 16 * s, 128 * s + 128)
-            tt(e, ap(pl, 128 + 16 * s, 256), ap("S0", 0, 128 - 16 * s), A.is_equal)
-            mm(ap("Q1", 128 + 16 * s, 256), ap("BO8"), e, False, s == 7)
-        cp(ap("po"), ap("S0", 15, 128, 16))
-        tt(ap("tc"), ind(Xm, ap("po")), ap("ANc", 256 * r + 128, 256 * r + 256), A.min)
-        scan(ap("S1"), ap("D0"), ap("Q1", 128, 256), -1.0, A.max, A.min)
-        if CFG["tn"][0] == 1:
-            new_points(r)
+            if not (CFG["cp"] or c):
+                continue
+            a, b = 16 * b0 * CFG["cp"], 16 * b1
+            first[0] = 1 - c
+            o = ap(turn("#s"), a, b)
+            mm(o, ap("Dt", 16, 144), ap("Tfc", R + a, R + b))
+            act(ap("Tsh", a, b), o, bias=col("pcf", 7))
+            y0, y1 = ap("Y", a, b), ap("Y", 128 + a, 128 + b)
+            tt(y0, ap(cnt, a, b), ap("Tfc", R + a, R + b), A.min)
+            tt(y1, ap(cnt, a, b), ap("Tsh", a, b), A.min)
+            step(ap("fms", R + a, R + b), ap(cnt, a, b), 0.0, 1.0 / 32)
+            place = lambda o: [(o, ap("BOb"), y0), (o, ap("nBO"), y1)]
+            o = ap(turn("#p"), a, b)
+            group([(o, I_b, ap("OD0", a, b))] + place(o))
+            pl = turn("#q")
+            group(place(ap(pl, a, b)))
+            scan(ap("S0", a, b), ap("D0", a, b), o, col("S0", a - 1) if a else -1.0, A.max, A.min)
+            pd = turn("#l")
+            mm(ap(pd, a, b), I_b, ap("OD1", a, b), True, False)
+            for x in place(ap(pd, a, b)):
+                mm(*x, False, False)
+            for s in range(b1):
+                lo = max(a, 16 * s)
+                e = ap("EQ", 128 * s + lo, 128 * s + b)
+                tt(e, ap(pl, lo, b), ap("S0", lo - 16 * s, b - 16 * s), A.is_equal)
+                mm(ap(pd, lo, b), ap("BO8"), e, False, s == b1 - 1)
+            scan(ap("S1", a, b), ap("D0", a, b), ap(pd, a, b), -1.0, A.max, A.min)
+        first[0] = 0
+        new_points(r)
+        judge_points(r)
         oc = ap("oc", 8 * r, 8 * r + 8)
-        cp(oc, ap("S1", 15, 128, 16))
-        tt(ind(Xw, oc), ap("tc"), ap("ANc", 256 * r, 256 * r + 128), A.add)
-        send(-SB, ap("fmh", R, R + 128), fm)
+        parts = [(0, CFG["cx"]), (CFG["cx"], 8)] if CFG["cx"] else [(0, 8)]
+        for b0, b1 in parts:
+            if CFG["cxo"] and not b0:
+                cp(ap("po"), ap("S0", 15, 128, 16))
+                tt(ap("tc"), ind(Xm, ap("po")), an("c", r, 1), A.min)
+            if CFG["cxo"]:
+                cp(ap("oc", 8 * r + b0, 8 * r + b1), ap("S1", 16 * b0 + 15, 16 * b1, 16))
+                tt(ind(Xw, ap("oc", 8 * r + b0, 8 * r + b1)), ap("tc", 16 * b0, 16 * b1), ap("ANc", AW * r + 16 * b0, AW * r + 16 * b1), A.add)
+                continue
+            cp(ap("po", b0, b1), ap("S0", 16 * b0 + 15, 16 * b1, 16))
+            tt(ap("tc", 16 * b0, 16 * b1), ind(Xm, ap("po", b0, b1)), ap("ANc", AW * r + 128 + 16 * b0, AW * r + 128 + 16 * b1), A.min)
+            cp(ap("oc", 8 * r + b0, 8 * r + b1), ap("S1", 16 * b0 + 15, 16 * b1, 16))
+            tt(ind(Xw, ap("oc", 8 * r + b0, 8 * r + b1)), ap("tc", 16 * b0, 16 * b1), ap("ANc", AW * r + 16 * b0, AW * r + 16 * b1), A.add)
+        send(-SB, ap("fmh", R, R + 128), ap("fms", R, R + 128))
         send(SC - SB, ap("ocj", 8 * r, 8 * r + 8), oc)
         seg = slice(8 * r, 8 * r + 8)
         for c, (b0, b1) in enumerate(CH):
-            if CFG["points"] == c:
-                judge_points(r)
             bs, a, b = slice(b0, b1), 16 * b0, 16 * b1
-            o = part(CFG["sob"][c], b0, b1)
-            group([(o, ap("ZTc", r * ZW, r * ZW + 128), ap("Ib", a, b)), (o, I_b, ap("RAc", 16 * a + 15, 16 * b, 16)),
+            o = ap(turn("#f%d" % c), a, b)
+            group([(o, ap("ZTc", R, R + 128), ap("Ib", a, b)), (o, I_b, ap("RAc", 16 * a + 15, 16 * b, 16)),
                    (o, ap("I8"), ap("IM", bs, slice(14, 256, 16))), (o, ap("I8"), ap("IM", bs, slice(15, 256, 16)))])
             step(ap("IM", bs, slice(15, 256, 16)), o, -128.0)
+            o = ap(turn("#g%d" % c), a, b)
             group([(o, I_b, ap("c35", a, b))] + [(o, sel(x), ap("IM", bs, slice(16 * x, 16 * x + 16))) for x in range(16)])
             step(ap("sos", slice(8 * r + b0, 8 * r + b1), slice(0, 16)), o, beta("c", r))
             if CFG["so"] == 2 or c:
                 s0 = b0 if CFG["so"] == 2 else 0
                 send(SC - SB, ap("soj", 136 * r + 17 * s0, 136 * r + 17 * b1), ap("sos", slice(8 * r + s0, 8 * r + b1), ALL))
-        if CFG["points"] == 2:
-            judge_points(r)
-        if CFG["tn"][0] == 2:
-            new_points(r)
-        o = ap("Q1", 256, 264)
+        o = ap(turn("#d"), 0, 8)
         group([(o, ap("I8"), ap("U16", 0, 8)), (o, ap("nI8"), ap("sos", seg, 15)), (o, I_f, ap("S1", 15, 128, 16))])
         tt(ap("D2s", 136 * r + 16, 136 * r + 136, 17), o, ap("DUM8"), A.min)
         send(SC - SB, ap("D2j", 136 * r, 136 * r + 136), ap("D2s", 136 * r, 136 * r + 136))
 
         stage[0] = "j%d" % r
+        limits("h", r, CFG["home"])
         limits("j", r, CFG["judge"])
         for u in CFG["judge"]:
-            b0, b1, way, _ = u
+            b0, b1, way = u
             first[0] = ahead(b0)
             if way == "T":
                 p = ap("RAj", 256 * b0, 256 * b1)
@@ -462,11 +506,12 @@ def plan():
                     act(ap("THj", 256 * b0, 256 * b1), p)
                     p = ap("THj", 256 * b0, 256 * b1)
             ts(ap("AJ", slice(16 * b0, 16 * b1), slice(0, 16)), p, col("eps", r), A.max)
+        told = 0
         for c, (b0, b1) in enumerate(CJ):
             a, b = 16 * b0, 16 * b1
             first[0] = len(CJ) - 1 - c
             w = lambda name, off=0: ap(name, 17 * b0 + off, 17 * b1 + off)
-            o = ap(CFG["rb"][c], 256, 256 + 17 * (b1 - b0))
+            o = ap(turn("#r%d" % c), 0, 17 * (b1 - b0))
             om, of = ap("om", 8 * c, 8 * c + b1 - b0), ap("of", 8 * c, 8 * c + b1 - b0)
             group([(o, I_b, w("CK"))] + [(o, sel(x), ap("AJ", slice(a + x, b, 16), ALL)) for x in range(16)] + [(o, ap("I8"), w("soj", 136 * r))])
             ts(w("t2"), o, MAG, A.add, -MAG, A.add)
@@ -478,39 +523,64 @@ def plan():
             cp(om, ap("UU", 17 * b0 + 16, 17 * b1, 17))
             cp(ap("Vus", R + a, R + b), ind(ap("MV"), om))
             send(-SC, ap("Vuh", R + a, R + b), ap("Vus", R + a, R + b))
-            tt(ap("SS", a, b), ind(Xe, om), ap("Zj", a, b), A.add)
-            ts(of, ap("UU", 17 * b0 + 16, 17 * b1, 17), EXT - 1.0, A.subtract)
-            act(ap("aps", R + a, R + b), ind(ap("FL"), of), accum=col("acc", c))
-            send(-SC, ap("aph", R + a, R + b), ap("aps", R + a, R + b))
+            act(ap("Yg", a, b), ind(Xe, om), F.Abs, bias=0.5)
+            if CFG["fl"]:
+                ts(of, ap("UU", 17 * b0 + 16, 17 * b1, 17), EXT - 1.0, A.subtract)
+                act(ap("ANj", AW * r + 264 + a, AW * r + 264 + b), ind(ap("FL"), of), accum=col("acc", c))
+            else:
+                act(ap("ANj", AW * r + 264 + a, AW * r + 264 + b), ind(Xe, om), F.Sigmoid, 128.0, 256.0, col("acc", c))
+            if b1 in CFG["ap"] + (8,):
+                send(-SC, ap("aph", 136 * r + told, 136 * r + 8 + b), ap("ANj", AW * r + 256 + told, AW * r + 264 + b))
+                told = 8 + b
             if c and r + 1 < RO:
                 act(col("acc", 0), col("acc", 0), bias=col("acc", c))
         first[0] = 0
-        limits("h", r, CFG["home"])
-        tt(ap("ts"), ind(Xw, ap("ocj", 8 * r, 8 * r + 8)), ap("ANj", 256 * r + 128, 256 * r + 256), A.min)
         scan(ap("U2"), ap("NU"), ap("D2j", 136 * r, 136 * r + 136), 0.0, A.mult, A.max)
         cp(ap("osh"), ap("U2", 16, 136, 17))
-        tt(ind(Xw, ap("osh")), ap("ts"), ap("ANj", 256 * r, 256 * r + 128), A.add)
-        act(ap("r1"), ap("SS"), bias=MAG, scale=0.4995)
-        act(Zj, ap("r1"), bias=-MAG)
-        n0 = (r + 1) * ZW
+        old = ind(Xw, ap("ocj", 8 * r, 8 * r + 8))
+        if CFG["ts"]:
+            sh = [ap("sh", 128 * k, 128 * k + 128) for k in range(3)]
+            act(sh[0], old, bias=255.0, scale=-1.0)
+            o = ap(turn("#u"), 0, 128)
+            group([(o, ap("nIb"), an("j", r, 0)), (o, I_b, sh[0])])
+            act(sh[1], o, F.Relu)
+            act(sh[2], sh[1], bias=255.0, scale=-1.0)
+            cp(ind(Xw, ap("osh")), sh[2])
+            if r + 1 < RO:
+                o = ap(turn("#v"), 0, 128)
+                group([(o, I_b, an("j", r, 1)), (o, ap("nIb"), sh[1])])
+                act(ap("ts"), o)
+        else:
+            tt(ap("ts"), old, an("j", r, 1), A.min)
+            tt(ind(Xw, ap("osh")), ap("ts"), an("j", r, 0), A.add)
+        n0 = R + 128
         if r + 1 < RO:
-            turned(ap("ZTs", n0, n0 + 128), Zj, -MID, q3(4, 8))
-            act(col("pt", 0), col("acc", 0), bias=-0.25, scale=-1.0 / 512)
-            act(beta("s", r + 1), col("pt", 0), bias=col("acc", 0), scale=512.0)
-            act(col("eps", r + 1), beta("s", r + 1), bias=10.0 / 256, scale=-1.0 / 65536)
-            send(SB - SC, ap("ZTc", n0, n0 + ZW), ap("ZTs", n0, n0 + ZW))
-            send(-SC, ap("ZTh", n0, n0 + ZW), ap("ZTs", n0, n0 + ZW))
-            quarters(("ANj", 256 * (r + 1)), ap("SS"), -0.125, 255.4375)
-            send(SB - SC, ap("ANc", 256 * (r + 1), 256 * (r + 2)), ap("ANj", 256 * (r + 1), 256 * (r + 2)))
+            o = ap(turn("#y"), 0, 128)
+            group([(o, Zj, I_b), (o, ap("Yg"), I_b)])
+            act(ap("ZTs", n0, n0 + 128), o, bias=ZO / 2 - 0.5, scale=0.5)
+            send(SB - SC, ap("ZTc", n0, n0 + 128), ap("ZTs", n0, n0 + 128))
+            send(-SC, ap("ZTh", n0, n0 + 128), ap("ZTs", n0, n0 + 128))
+        o = ap(turn("#x"), 0, 128)
+        group([(o, I_b, Zj), (o, I_b, ap("Yg"))])
+        act(Zj, o, bias=ZO / 2 - 0.5, scale=0.5)
+        if r + 1 < RO:
+            act(ap("X", EXT, XW), Zj, bias=ZO - 1, scale=-1.0)
+            quarters("j", r + 1, o, -0.125, ZO / 8 + 255.5)
+            act(col("pt", 0), col("acc", 0), bias=143.75, scale=0.5)
+            act(col("acc", 7), col("pt", 0), bias=col("acc", 0), scale=-2.0)
+            act(beta("j", r + 1), col("acc", 7), bias=-288.0 * 256, scale=-256.0)
+            act(col("eps", r + 1), col("acc", 7), bias=298.0 / 256, scale=1.0 / 256)
+            send(SB - SC, ap("ANc", AW * (r + 1), AW * (r + 1) + 264), ap("ANj", AW * (r + 1), AW * (r + 1) + 264))
             judge_limits(r + 1)
         else:
-            send(-SC, ap("Zy"), Zj)
-            dma("Y", ap("ysect"), Xm, 4.5)
+            act(ap("zcl"), Zj, bias=-ZO)
+            send(-SC, ap("Zy"), ap("zcl"))
+            dma("Y", ap("ysect"), Xm, 4.5, [mark([i for i, o in enumerate(ops) if o["kind"] == "send" and o["round"] == r])])
             dma("Y", ap("yamt"), ap("Zy"), 2.0)
 
         stage[0] = "h%d" % r
         for u in CFG["home"]:
-            b0, b1, way, _ = u
+            b0, b1, way = u
             first[0] = ahead(b0)
             src, o = ind(Xm, ap("Vuh", R + 16 * b0, R + 16 * b1)), ap("IH", 256 * b0, 256 * b1)
             if way == "T":
@@ -526,33 +596,43 @@ def plan():
             limits("c", r + 1, CFG["cut"])
         for c, (b0, b1) in enumerate(CJ):
             a, b = 16 * b0, 16 * b1
-            old, vf, bk, e = ap("Tfh", R + a, R + b), ap("Vf", a, b), CFG["pb"][c], 272 + 2 * (b - a)
+            old, vf, bk, e = ap("Tfh", R + a, R + b), ap("Vf", a, b), turn("#w%d" % c), 2 * (b - a)
             first[0] = len(CJ) - 1 - c
             ts(vf, ap("Vuh", R + a, R + b), -HALF, A.add)
-            group([(ap(bk, 272, e, 2), I_b, old), (ap(bk, 272, e, 2), ap("nIb"), vf)])
-            mm(ap(bk, 273, e, 2), I_b, vf)
-            o = part(CFG["ob"][c], b0, b1)
+            group([(ap(bk, 0, e, 2), I_b, old), (ap(bk, 0, e, 2), ap("nIb"), vf)])
+            mm(ap(bk, 1, e, 2), I_b, vf)
+            o = ap(turn("#o%d" % c), a, b)
             group([(o, I_b, ap("c384", a, b)), (o, ap("n35"), ap("fmh", R + a, R + b))] +
-                  [(o, sel(k), ap("IH", 16 * a + k, 16 * b, 16)) for k in range(16)] + [(o, ap("nIb"), ap("aph", R + a, R + b))])
+                  [(o, sel(k), ap("IH", 16 * a + k, 16 * b, 16)) for k in range(16)] + [(o, ap("I8"), ap("aph", 136 * r + 8 + a, 136 * r + 8 + b))])
             step(ap("up", 2 * a + 1, 2 * b, 2), o, beta("h", r))
-            scan(ap("tt", 2 * a, 2 * b), ap("up", 2 * a, 2 * b), ap(bk, 272, e), 0.0, A.mult, A.add)
+            scan(ap("tt", 2 * a, 2 * b), ap("up", 2 * a, 2 * b), ap(bk, 0, e), 0.0, A.mult, A.add)
             new = ap("tt", 2 * a + 1, 2 * b, 2)
             if r + 1 < RO:
                 u_ = ap("Tuh", R + 128 + a, R + 128 + b)
                 ts(u_, new, HALF, A.add)
                 send(SB, ap("Tuc", R + 128 + a, R + 128 + b), u_)
                 act(ap("Tfh", R + 128 + a, R + 128 + b), new)
+                if CFG["cp"] and b1 in (CFG["ch"], 8):
+                    a = 16 * CFG["ch"] * (b1 == 8)
+                    halved(SB, ap("Tfc", R + 128 + a, R + 128 + b), "c", R + 128 + a, R + 128 + b)
             else:
                 act(ap("To", a, b), new, bias=HALF)
                 dma("S" if c == len(CJ) - 1 else "Y", ap("ytraj", a, b), ap("To", a, b), 2.0)
         first[0] = 0
         if r + 1 < RO:
-            u_, f_ = ap("Tuh", R + 128, R + 256), ap("Tfh", R + 128, R + 256)
-            send(SB, ap("Tfc", R + 128, R + 256), f_)
-            send(SC, ap("Tfj", slice(4 * r + 4, 4 * r + 8), ALL), f_)
-            send(SC, ap("Tuj", R + 128, R + 256), u_)
+            if not CFG["cp"]:
+                halved(SB, ap("Tfc", R + 128, R + 256), "c", R + 128, R + 256)
+            send(SC, ap("Tuj", R + 128, R + 256), ap("Tuh", R + 128, R + 256))
+            halved(SC, ap("Tfj", slice(4 * r + 4, 4 * r + 8), ALL), "j", R + 128, R + 256)
             cp(ind(Xw, ap("osh")), ap("ts"))
     return ops
+
+
+def gap(ops, d, i):
+    a, b = ops[d], ops[i]
+    if d in b["free"]:
+        return a["cost"]
+    return a["cost"] + a["lat"] + (b["same"] if a["eng"] == b["eng"] and not a["lat"] else b["hop"])
 
 
 def order(ops):
@@ -561,10 +641,10 @@ def order(ops):
     for i, o in enumerate(ops):
         for d in o["deps"]:
             users[d].append(i)
-    hop = lambda d, i: 0.0 if ops[d]["eng"] == ops[i]["eng"] == "P" else COST["hop"]
+    hop = lambda d, i: gap(ops, d, i) - ops[d]["cost"] - ops[d]["lat"]
     way = [0.0] * n
     for i in range(n - 1, -1, -1):
-        way[i] = ops[i]["cost"] + ops[i]["lat"] + max([way[u] + hop(i, u) for u in users[i]], default=0.0)
+        way[i] = max([ops[i]["cost"] + ops[i]["lat"]] + [way[u] + gap(ops, i, u) for u in users[i]])
     way = [w + CFG["first"] * o["first"] for o, w in zip(ops, way)]
     left = [len(o["deps"]) for o in ops]
     ready, end, free = [0.0] * n, [0.0] * n, {}
@@ -600,10 +680,10 @@ def order(ops):
     return seq, max(end)
 
 
-def squeeze(ops, seq, turns):
+def squeeze(ops, seq, turns, late=False, seed=0):
     n = len(ops)
     cost, lat, eng = [o["cost"] for o in ops], [o["lat"] for o in ops], [o["eng"] for o in ops]
-    hop = lambda d, i: 0.0 if eng[d] == eng[i] == "P" else COST["hop"]
+    hop = lambda d, i: gap(ops, d, i) - cost[d] - lat[d]
     fwd = [[(d, cost[d] + lat[d] + hop(d, i)) for d in o["deps"]] for i, o in enumerate(ops)]
     bwd = [[] for _ in range(n)]
     for i, o in enumerate(ops):
@@ -642,7 +722,7 @@ def squeeze(ops, seq, turns):
                     free.insert(k, x_)
         return at
 
-    x, at, best, keep = 777, [0.0] * n, 1e9, None
+    x, at, best, keep = 777 + seed, [0.0] * n, 1e9, None
     for i, t in seq:
         at[i] = t
     keys = sorted(set(o["key"] for o in ops))
@@ -658,7 +738,94 @@ def squeeze(ops, seq, turns):
             at = now
         if t < best:
             best, keep = t, now
+    if late:
+        back = pack([-(keep[i] + cost[i]) for i in range(n)], bwd, lat)
+        back = [best - back[i] - cost[i] for i in range(n)]
+        least, opener = [0.0] * n, {}
+        for i, o in enumerate(ops):
+            for name in o["turns"]:
+                if opener.setdefault(name, i) not in (i, None):
+                    least[opener[name]] = back[i] - cost[opener[name]] - hop(opener[name], i) - EARLY
+                    opener[name] = None
+        keep = pack([max(back[i], least[i]) for i in range(n)], fwd, least)
     return sorted(((i, keep[i]) for i in range(n)), key=lambda p: (p[1], p[0])), best
+
+
+def bind(ops, seq):
+    at = dict(seq)
+    users, after = {}, [set() for _ in ops]
+    for i, o in enumerate(ops):
+        for d in o["deps"]:
+            after[d].add(i)
+    for i, _ in seq:
+        for name in ops[i]["turns"]:
+            users.setdefault(name, []).append(i)
+    pieces = lambda o: [x for a in [o["args"]] + o.get("more", []) for x in a if isinstance(x, tuple) and is_psum(x)]
+    held, where = {"B%d" % k: (-1.0 - k, []) for k in range(8)}, {}
+    for name, us in users.items():
+        cols = [x[1][1] for i in us for x in pieces(ops[i]) if x[0] == name]
+        narrow = name[0] == "%" or all(ops[i]["kind"] != "tensor_tensor_scan" for i in us) and all(
+            c.step is None and c.start % 16 == c.stop % 16 == 0 and c.stop <= 256 for c in cols)
+        banks = ["B7"] if name[0] == "%" else [b for b in held if b != "B7" or narrow]
+        below, todo = set(us), list(us)
+        while todo:
+            for i in after[todo.pop()] - below:
+                below.add(i)
+                todo.append(i)
+        b = min((b for b in banks if not below & set(held[b][1])), key=lambda b: (held[b][0] > at[us[0]], b != "B7", held[b][0]))
+        ops[us[0]]["deps"] |= set(held[b][1])
+        for i in held[b][1]:
+            after[i].add(us[0])
+        ops[us[0]]["free"] |= set(i for i in held[b][1] if ops[i]["eng"] == "P")
+        held[b], where[name] = (max(at[i] + ops[i]["cost"] for i in us) + COST["hop"], us), b
+
+    def moved(x):
+        if not (isinstance(x, tuple) and is_psum(x)):
+            return x
+        if where[x[0]] == "B7" and x[0][0] == "#":
+            return ("B7", (x[1][0], slice(x[1][1].start // 16, x[1][1].stop // 16), slice(0, 16)))
+        return (where[x[0]], x[1])
+
+    for o in ops:
+        o["args"] = tuple(moved(x) for x in o["args"])
+        o["more"] = [tuple(moved(x) for x in a) for a in o.get("more", [])]
+
+
+def replay(ops, seq, costs):
+    start, free = {}, {}
+    for i, _ in seq:
+        o = ops[i]
+        costs[i]["free"] = o["free"]
+        start[i] = max([free.get(o["eng"], 0.0)] + [start[d] + gap(costs, d, i) for d in o["deps"]])
+        free[o["eng"]] = start[i] + costs[i]["cost"]
+    return max(start[i] + costs[i]["cost"] + costs[i]["lat"] for i in start)
+
+
+def schedule(turns, tries):
+    base, others = dict(COST), []
+    for m in SPREAD:
+        COST.update(m)
+        others.append(plan())
+        COST.update(base)
+        for o in others[-1]:
+            if o["kind"] == "send":
+                o["lat"] += m.get("odd", 0.0) * (sum(map(ord, o["key"])) * (7 + len(others)) % 11 / 10 - 0.3)
+    ops = plan()
+    seq, best = squeeze(ops, order(ops)[0], turns)[0], None
+    for k in range(tries):
+        mine = plan()
+        late = squeeze(ops, seq, turns // 8, True, k)[0]
+        bind(mine, late)
+        late = squeeze(mine, late, turns // 4, False, k)[0]
+        t = sum(replay(mine, late, p) / replay(ops, seq, p) for p in others)
+        if best is None or t < best[0]:
+            best = (t, mine, late)
+    _, mine, late = best
+    for p in others:
+        for o, m in zip(p, mine):
+            o["deps"], o["free"] = m["deps"], m["free"]
+    late = anneal(others, late, MOVES, alike=False)[0]
+    return mine, late, replay(mine, late, ops)
 
 
 def anneal(plans, seq, steps, heat=0.15, seed=4321, alike=True):
@@ -670,7 +837,7 @@ def anneal(plans, seq, steps, heat=0.15, seed=4321, alike=True):
     deps = [sorted(o["deps"]) for o in ops]
     costs = [[o["cost"] for o in p] for p in plans]
     tails = [[o["cost"] + o["lat"] for o in p] for p in plans]
-    waits = [[[(d, p[d]["cost"] + p[d]["lat"] + (0.0 if eng[d] == eng[i] == "P" else p[i]["hop"])) for d in deps[i]] for i in range(n)] for p in plans]
+    waits = [[[(d, gap(p, d, i)) for d in deps[i]] for i in range(n)] for p in plans]
     at = [0.0] * n
     for i, t in seq:
         at[i] = t
@@ -684,11 +851,11 @@ def anneal(plans, seq, steps, heat=0.15, seed=4321, alike=True):
     for i, o in enumerate(ops):
         r = 1 if alike and 1 in mid[o["unit"]] else o["round"]
         place.setdefault(key[i], mid[o["unit"]][r] - period * r)
-    off = [period * o["round"] + 1e-6 * i for i, o in enumerate(ops)]
+    key, place, off = list(range(n)), {i: t + 1e-6 * p for p, (i, t) in enumerate(seq)}, [0.0] * n
 
     def times():
         v = [0.0] * n
-        for i in range(n):
+        for i, _ in seq:
             x = place[key[i]] + off[i]
             for d in deps[i]:
                 if v[d] >= x:
@@ -726,7 +893,7 @@ def anneal(plans, seq, steps, heat=0.15, seed=4321, alike=True):
         return (x[0] >> 33) / float(1 << 31)
 
     cur, held, v, start = times()
-    best, keep = cur, start
+    best, keep = cur, v
     for it in range(steps):
         if held and draw() < 0.7:
             a, b = held[int(draw() * len(held))]
@@ -740,7 +907,7 @@ def anneal(plans, seq, steps, heat=0.15, seed=4321, alike=True):
         if t <= cur + heat * (1 - it / steps) * draw():
             cur, held, v = t, h, w
             if t < best:
-                best, keep = t, s
+                best, keep = t, w
         else:
             place[k] = old
     return sorted(((i, keep[i]) for i in range(n)), key=lambda p: (p[1], p[0])), best
@@ -754,8 +921,7 @@ def rank_program(g, core, T, topo):
     if rank is None:
         return
     if not CACHE:
-        CACHE["ops"] = plan()
-        CACHE["seq"] = squeeze(CACHE["ops"], order(CACHE["ops"])[0], STEPS)[0]
+        CACHE["ops"], CACHE["seq"], _ = schedule(STEPS, TRIES)
     ops, seq = CACHE["ops"], CACHE["seq"]
     queue = {"V": g.vector, "S": g.scalar, "P": g.tensor, "G": g, "Y": g.sync}
 
@@ -766,25 +932,35 @@ def rank_program(g, core, T, topo):
             return res(x[1]).indirect(res(x[2]))
         return T[x[0]][x[1]]
 
-    token, count, waited = {}, {"V": 0, "S": 0, "P": 0, "G": 0}, {}
-    nd, nm, sent = 0, 0, 0
+    place, waits, seen, knew = {i: p for p, (i, _) in enumerate(seq)}, {}, {e: {} for e in queue}, {}
+    for i, _ in seq:
+        mine, waits[i] = seen[ops[i]["eng"]], []
+        for d in sorted(ops[i]["deps"] - ops[i]["free"], key=lambda d: -place[d]):
+            s = d if ops[d]["kind"] in ("dma", "send", "mark") else ops[d]["eng"]
+            if mine.get(s, -1) < place[d]:
+                waits[i].append(d)
+                mine[s] = place[d]
+                if ops[d]["kind"] not in ("send", "mark"):
+                    mine.update((k, v) for k, v in knew[d].items() if mine.get(k, -1) < v)
+        knew[i] = dict(mine)
+    told = set(d for w in waits.values() for d in w)
+
+    token, count = {}, {"V": 0, "S": 0, "P": 0, "G": 0}
+    nd, nm, sent, marks = 0, 0, 0, 0
     for i, _ in seq:
         o = ops[i]
         e, q, a = o["eng"], queue[o["eng"]], o["args"]
-        need = {}
-        for d in o["deps"]:
-            if not (e == "P" and ops[d]["eng"] == "P"):
-                for s, v in token[d]:
-                    need[s] = max(need.get(s, 0), v)
-        for s, v in need.items():
-            if waited.get((e, s), 0) < v:
-                q.wait_ge(T.sem[s], v)
-                waited[(e, s)] = v
+        for d in waits[i]:
+            q.wait_ge(T.sem[token[d][0][0]], token[d][0][1])
         k = o["kind"]
         if k == "dma":
             token[i] = [("d%d" % nd, 16)]
             q.dma_start(res(a[0]), res(a[1])).then_inc(T.sem["d%d" % nd], 16)
             nd += 1
+        elif k == "mark":
+            marks += 1
+            g.sem_inc(T.sem.mark, 1)
+            token[i] = [("mark", marks)]
         elif k == "send":
             dst, src = T.cores[(rank + a[0]) % N], T.cores[(rank - a[0]) % N]
             rid, pid, _ = topo.addr(dst)
@@ -814,11 +990,13 @@ def rank_program(g, core, T, topo):
                 ins = q.transpose(*r)
             else:
                 ins = q.memset(*r)
-            count[e] += 1
-            ins.then_inc(T.sem[e], 1)
-            token[i] = [(e, count[e])]
+            if i in told:
+                count[e] += 1
+                ins.then_inc(T.sem[e], 1)
+                token[i] = [(e, count[e])]
     for e, v in count.items():
-        g.wait_ge(T.sem[e], v)
+        if v:
+            g.wait_ge(T.sem[e], v)
     g.wait_ge(T.sem.sent, sent)
     for i, o in enumerate(ops):
         if o["kind"] in ("dma", "send"):

import numpy as np
from concourse.bass import DstId, RemoteDMATransfer
from concourse.mybir import AluOpType as A, ActivationFunctionType as F

N, RO, SB, SC = 6, 3, 2, 5
W, L, Q = 4096, 128, 2048
DUM, EXT, XW = W, W + L, W + 2 * L
COST = {"V": 0.025, "S": 0.065, "cyc": 0.00086, "pe": 0.00045, "gather": 1.56, "scatter": 3.8, "link": 2.0, "hop": 0.18, "same": 0.15,
        "call": 0.2, "byte": 0.0007, "P": 0.0}
CFG = {
    "cut": [(0, 1, "V"), (1, 2, "S"), (2, 3, "S"), (3, 4, "T"), (4, 6, "S"), (6, 7, "T"), (7, 8, "S")],
    "judge": [(0, 1, "T"), (1, 2, "T"), (2, 4, "S"), (4, 6, "A"), (6, 7, "T"), (7, 8, "S")],
    "home": [(0, 2, "T"), (2, 3, "A"), (3, 4, "T"), (4, 6, "T"), (6, 7, "A"), (7, 8, "T")],
    "so": 2, "ch": 4, "cj": (4, 6), "cp": 1, "war": 1, "ts": 1, "fl": 0, "cx": 4, "cxo": 0, "xa": 4096, "tf": "c", "ap": (4, 6),
    "first": 0.5,
}
STEPS, TRIES, SLACK, NUDGE = 600, 10, 0.3, 1.0
MOVES = 1
SPREAD = [{}, {"cyc": 0.00115, "pe": 0.0006, "gather": 1.8, "odd": 0.4}, {"link": 2.8, "call": 0.4, "odd": 0.8},
          {"hop": 0.22, "same": 0.08, "link": 1.4, "V": 0.01}, {"odd": 0.6, "byte": 0.0015, "hop": 0.25, "same": 0.2}]
EARLY = 0.1
LOOK = 0.03
AW = 392
MAG = 8388608.0
ZO = 1152.0
HALF = 2048.0
bf, f16, f32, i32, u16 = "bfloat16", "float16", "float32", "int32", "uint16"


def sb(n, t):
    return ("sbuf", [128] + (list(n) if isinstance(n, tuple) else [n]), t)


SCRATCH = {
    "X": sb(XW, bf), "MV": sb(XW, i32), "tr32": sb(128, i32), "cap32": sb(8, i32), "capf": sb(8, f32),
    "Tuc": sb(384, u16), "Tuj": sb(384, u16), "Tuh": sb(384, u16),
    "Tfc": sb(384, f16), "Tfj": sb((12, 32), f16), "Tfh": sb(384, f16), "To": sb(128, f32),
    "Z0": sb(128, bf), "Z1": sb(128, f16), "Zj": sb(128, f16), "Zy": sb(128, bf), "zcl": sb(128, bf),
    "ZTc": sb(384, f16), "ZTh": sb(384, f16), "ZTs": sb(384, f16), "ZTj": sb(128, bf),
    "ANc": sb(3 * AW, bf), "ANj": sb(3 * AW, bf), "ANh": sb(264, bf),
    "THc": sb(2048, bf), "THj": sb(2048, bf), "THh": sb(2048, bf),
    "RAc": sb(2048, f16), "RAj": sb(2048, bf), "RAh": sb(2048, f16),
    "IC": sb(2048, bf), "IM": sb((8, 256), bf), "IH": sb(2048, bf), "AJ": sb((128, 17), bf),
    "fms": sb(384, bf), "fmh": sb(384, bf), "sos": sb((24, 17), bf), "soj": sb(408, bf),
    "oc": sb(24, u16), "ocj": sb(24, u16), "D2s": sb(408, f32), "D2j": sb(408, f32),
    "Y": sb(256, f16), "Tsh": sb(128, f16), "S0": sb(128, f32), "S1": sb(128, f32),
    "EQ": sb(1024, bf), "po": sb(8, u16), "tc": sb(128, bf),
    "Town": sb((8, 17), f32), "DT": sb(136, f32), "t2": sb(136, f32), "RR": sb(144, f32),
    "NU": sb(136, f32), "UU": sb(136, f32), "om": sb(32, u16), "of": sb(32, u16),
    "Vus": sb(384, u16), "Vuh": sb(384, u16), "aph": sb(408, bf),
    "Yg": sb(128, f16), "sh": sb(384, bf), "acc": sb(8, f32), "pt": sb(8, bf), "eps": sb(8, bf),
    "tn": sb(128, i32), "U2": sb(136, f32), "osh": sb(8, u16), "ts": sb(128, bf), "ik": sb(136, i32),
    "Vf": sb(128, f16), "up": sb(256, bf), "tt": sb(256, f32),
    "io": sb(168, i32), "ei": sb(512, bf), "pc": sb(8, i32), "pcf": sb(16, f32), "pcb": sb(8, bf),
    "ku": sb(256, f32), "U16": sb(256, bf), "M16": sb(256, bf),
    "Iw": sb(168, f32), "Dt": sb(160, bf), "Dw": sb(160, bf), "DE": sb(160, bf), "DO": sb(160, bf), "nIb": sb(128, bf), "I5": sb(128, bf),
    "Ib": sb(128, bf), "n35": sb(128, bf), "I32": sb(128, bf), "I8": sb(128, bf), "nI8": sb(128, bf),
    "nBO": sb(128, bf), "BOb": sb(128, bf), "BO8": sb(128, bf), "SW": sb(144, bf), "SW8": sb(144, bf), "E32": sb(512, bf),
    "dg": sb(128, bf), "OD0": sb(128, bf), "OD1": sb(128, bf), "D0": sb(128, f32),
    "DUM8": sb(8, f32), "CK": sb(136, bf), "Z136": sb(136, bf), "CB": sb(128, bf), "C21": sb(128, bf), "CT": sb(128, bf), "CQ": sb(128, bf),
    "FL": sb(144, bf), "C15": sb(128, bf), "c35": sb(128, bf), "c384": sb(128, bf),
    "B7": ("psum", [128, 16, 32], f32),
}
SCRATCH.update(("B%d" % i, ("psum", [128, 512], f32)) for i in range(7))
SEMAPHORES = ["V", "S", "P", "G", "sent", "mark"] + ["d%d" % i for i in range(20)] + ["m%d" % i for i in range(80)]
IO_SHAPES = {"sect": [128, W], "mv": [128, Q], "traj": [128, L], "amt": [128, L], "cap": [128, 1],
             "ysect": [128, W], "ytraj": [128, L], "yamt": [128, L]}
ALL = slice(None)


def ap(name, *idx, rows=ALL):
    if len(idx) >= 2 and all(isinstance(i, int) for i in idx):
        idx = (slice(*idx),)
    return (name, (rows,) + tuple(idx))


def ind(win, off):
    return ("*", win, off)


SPANS = {}


def span(x):
    k = (x[0][0] if is_psum(x) else x[0], str(x[1][1:]))
    if k not in SPANS:
        shape = SCRATCH[{"#": "B0", "%": "B7"}.get(x[0][0], x[0])][1] if x[0] not in IO_SHAPES else IO_SHAPES[x[0]]
        e = np.arange(int(np.prod(shape[1:]))).reshape(shape[1:])[x[1][1:]]
        SPANS[k] = (int(np.min(e)), int(np.max(e)) + 1, int(np.size(e)))
    return SPANS[k]


def is_psum(x):
    return x[0][0] in "#%"


def two_bytes(x):
    return not is_psum(x) and SCRATCH[x[0]][2] in (bf, f16, u16)


def plan():
    ops = []
    last = {}
    first = [0]
    seen = {}
    stage = [""]

    def add(eng, kind, args, reads, writes, cost, lat=0.0):
        me = len(ops)
        deps, fed = set(), set()
        for x, wr in [(x, False) for x in reads] + [(x, True) for x in writes]:
            lo, hi, _ = span(x)
            if is_psum(x):
                who, before, now = last.get(x[0], (eng, [], []))
                if who != eng:
                    before, now = now, []
                deps.update(o for (_, _, _, o) in before)
                deps.update(o for (a, b, w, o) in now if o != me and a < hi and lo < b and (w or wr))
                fed.update(o for (a, b, w, o) in now if a < hi and lo < b and w)
                if eng == "P" and now:
                    deps.add(now[-1][3])
                last[x[0]] = (eng, before, now + [(lo, hi, wr, me)])
                continue
            keep = []
            for (a, b, w, o) in last.get(x[0], []):
                if o != me and a < hi and lo < b and (w or wr):
                    deps.add(o)
                    if w:
                        fed.add(o)
                if not (wr and lo <= a and b <= hi and span(x)[2] == hi - lo):
                    keep.append((a, b, w, o))
            last[x[0]] = keep + [(lo, hi, wr, me)]
        deps.discard(me)
        free = set(d for d in deps if ops[d]["eng"] == eng and (eng == "P" or CFG["war"] and d not in fed and
                                                                  kind not in ("dma", "send") and ops[d]["kind"] not in ("dma", "send")))
        name = writes[0][0].split(".")[0]
        k = (stage[0], eng, name)
        seen[k] = seen.get(k, 0) + (eng != "P")
        key = stage[0][:1] + eng + name + str(seen[k])
        k = k + ("unit",)
        seen[k] = seen.get(k, 0) + (eng != "P" or args[3])
        ops.append({"eng": eng, "kind": kind, "args": args, "deps": deps, "free": free, "turns": set(x[0] for x in reads + writes if is_psum(x)), "cost": cost, "lat": lat, "key": key, "first": first[0],
                    "unit": key + "." + str(seen[k]), "round": int(stage[0][1:] or 0), "hop": COST["hop"], "same": COST["same"]})

    def sides(xs):
        r = []
        for x in xs:
            if isinstance(x, tuple):
                r += [x[1], x[2]] if x[0] == "*" else [x]
        return r

    def compute(eng, kind, out, ins, args, per, extra_w=(), more=0.0):
        fix = COST[eng] + more
        if out[0] == "*":
            add(eng, kind, args, sides(ins) + [out[2]], [out[1]], fix + 0.02 + 16 * span(out[2])[2] * COST["scatter"] * CYC)
            return
        n = span(out)[2]
        if ins and isinstance(ins[0], tuple) and ins[0][0] == "*":
            per = GA
            fix += 0.02 * (eng == "V")
        elif eng == "V" and all(two_bytes(x) for x in [out] + sides(ins[:2]) if span(x)[2] > 1):
            per = per / 2
        add(eng, kind, args, sides(ins), [out] + list(extra_w), fix + max(64, n * per) * CYC)

    def cp(out, in_):
        compute("V", "tensor_copy", out, [in_], (out, in_), 1)

    def tt(out, a, b, op):
        compute("V", "tensor_tensor", out, [a, b], (out, a, b, op), 1 if a[0] == "*" or is_psum(a) or is_psum(b) else 2)

    def ts(out, a, s1, op0, s2=None, op1=None):
        compute("V", "tensor_scalar", out, [a, s1, s2], (out, a, s1, s2, op0) + ((op1,) if op1 is not None else ()), 1)

    def scan(out, d0, d1, init, op0, op1):
        compute("V", "tensor_tensor_scan", out, [d0, d1, init], (out, d0, d1, init, op0, op1), 1)

    def ms(out, v):
        compute("V", "memset", out, [], (out, v), 1)

    def act(out, in_, func=F.Identity, bias=0.0, scale=1.0, accum=None, more=0.0):
        compute("S", "activation", out, [in_, bias, scale], (out, in_, func, bias, scale, accum), 1, [accum] if accum else [], more)

    def step(out, in_, bias, scale=256.0, more=0.0):
        act(out, in_, F.Sigmoid, bias, scale, more=more)

    def mm(out, lhsT, rhs, start=True, stop=True, more=()):
        n = span(rhs)[2]
        add("P", "matmul", (out, lhsT, rhs, start, stop), [lhsT, rhs] + [x for m in more for x in m[1:3]], [out],
            (1 + len(more)) * (COST["P"] + max(64, n) * PCYC * (1 if two_bytes(rhs) else 4)))
        ops[-1]["more"] = list(more)

    def group(out_lhs_rhs):
        n, i = len(out_lhs_rhs), 0
        while i < n:
            j = i + 1
            while j < n and j - i < 4 and out_lhs_rhs[i][1][0][:2] == out_lhs_rhs[j][1][0][:2] == "SW":
                j += 1
            mm(*out_lhs_rhs[i], i == 0, i == n - 1, [x + (False, k == n - 1) for k, x in enumerate(out_lhs_rhs) if i < k < j])
            i = j

    def iota(out, pattern, base, cm):
        add("G", "iota", (out, pattern, base, cm), [], [out], 0.16 + 2 * span(out)[2] * CYC)

    def dma(queue, out, in_, lat, after=()):
        add(queue, "dma", (out, in_), [in_], [out], 0.06, lat)
        ops[-1]["deps"].update(after)

    def send(by, dst, src):
        add("G", "send", (by % N, dst, src), [src], [dst], COST["call"] + span(src)[2] * (2 if two_bytes(src) else 4) * COST["byte"], LAT)
        return len(ops) - 1

    def mark(after):
        add("G", "mark", (), [], [ap("pc", 7, 8)], 0.02)
        ops[-1]["deps"] = set(after)
        ops[-1]["free"] = set(after)
        return len(ops) - 1

    CYC, PCYC, GA, LAT = COST["cyc"], COST["pe"], COST["gather"], COST["link"]
    sel = lambda a: ap("SW", 15 - a, 143 - a)
    I_b, I_f = ap("Ib"), ap("Iw", 16, 144)
    col = lambda name, c: ap(name, c, c + 1)
    turn = lambda name: name + "." + str(len(ops))
    CH, CJ = [(0, CFG["ch"]), (CFG["ch"], 8)], list(zip((0,) + CFG["cj"], CFG["cj"] + (8,)))
    ahead = lambda b0: sum(b0 < e for e in CFG["cj"])
    Xm, Xw, Xe, Zj = ap("X", 0, W), ap("X", 0, EXT), ap("X", 0, XW), ap("Zj")
    an = lambda who, r, k: ap("AN" + who, AW * r + 128 * k, AW * r + min(128 * k + 128, 264))
    beta = lambda who, r: col("aph", 136 * r) if who == "h" else col("AN" + who, AW * r + 256)
    less, over = col("capf", 1), col("capf", 2)

    stage[0] = "0"
    dma("Y", ap("tr32"), ap("traj"), 1.9)
    dma("S", ap("Z0"), ap("amt"), 1.9)
    dma("Y", col("cap32", 0), ap("cap"), 1.9)
    dma("Y", ap("X", 0, CFG["xa"]), ap("sect", 0, CFG["xa"]), 1.7 + 2.8 * CFG["xa"] / W, [0, 2])
    ops[-1]["free"] = {0, 2}

    iota(ap("ku"), [[0, 16], [1, 16]], 0, 0)
    step(ap("U16"), ap("ku"), 256 * 14.5, -256.0, more=1.3)
    if any(u[2] in "TA" for u in CFG["cut"]):
        step(ap("M16"), ap("ku"), -128.0)
    for b0, b1, way in CFG["cut"]:
        if way == "T":
            ms(ap("RAc", 256 * b0 + 15, 256 * b1, 16), -2000.0)
    iota(ap("io"), [[1, 168]], -16, -1)
    iota(col("pc", 4), [[0, 1]], 0, 1)
    iota(ap("ei"), [[1, 32], [0, 16]], 0, 0)
    ts(col("pc", 0), col("pc", 4), 31, A.bitwise_and)
    ts(col("pc", 1), col("pc", 4), 15, A.bitwise_and)
    ts(col("pc", 2), col("pc", 4), 4, A.arith_shift_right)
    ts(col("pc", 3), col("pc", 4), 4, A.arith_shift_right, 1, A.bitwise_and)
    cp(ap("pcf", 0, 4), ap("pc", 0, 4))
    cp(ap("pcb", 0, 4), ap("pc", 0, 4))
    act(col("pcf", 8), col("pcf", 1), bias=float(DUM))
    ts(col("pcf", 4), col("pcf", 3), -1.0, A.mult, 1.0, A.add)
    ts(col("pcf", 5), col("pcf", 1), 15.0, A.is_equal, 128.0, A.mult)
    ts(col("pcf", 6), col("pcf", 1), 0.0, A.is_gt)
    ts(ap("Iw"), ap("io"), 0.0, A.is_equal)
    act(ap("Ib"), I_f)
    ts(ap("E32"), ap("ei"), col("pcb", 0), A.is_equal)
    ts(ap("BOb"), ap("ei", 0, 128), col("pcb", 2), A.is_equal)
    ms(ap("SW"), 0.0)
    cp(ap("SW", 15, 143, 16), ap("BOb", 0, 128, 16))
    act(ap("SW8"), ap("SW"), scale=8192.0)
    act(col("pcf", 7), col("pcf", 5), scale=-HALF / 128)
    ms(ap("X", W, EXT), 0.0)
    ts(ap("dg"), ap("ku", 0, 128), col("pcf", 1), A.is_equal)
    act(ap("OD0"), ap("dg"), bias=8192.0, scale=-8192.0)
    act(ap("OD1"), ap("dg"), bias=8192.0, scale=-16384.0)
    act(ap("DUM8"), ap("ei", 0, 128, 16), bias=col("pcf", 8), scale=16.0)
    act(ap("S0"), ap("ei", 0, 128), bias=col("pcf", 8), scale=16.0)
    act(ap("S1"), ap("dg"), bias=-1.0, scale=8192.0)
    tt(ap("D0"), ap("S0"), ap("S1"), A.min)
    act(ap("Dt"), ap("Iw", 1, 161), scale=col("pcf", 6))
    tt(ap("Dw"), ap("Iw", 0, 160), ap("Dt"), A.subtract)
    act(ap("nBO"), ap("BOb"), scale=-1.0)
    act(ap("BO8"), ap("BOb"), scale=8192.0)
    act(ap("DE"), ap("Dw"), scale=col("pcf", 4))
    act(ap("DO"), ap("Dw"), scale=col("pcf", 3))
    act(ap("nIb"), I_f, scale=-1.0)
    act(ap("nI8"), I_f, scale=-8192.0)
    act(ap("I5"), I_f, scale=5.0)
    act(ap("n35"), I_f, scale=-35.5)
    act(ap("I32"), I_f, scale=32.0)
    act(ap("I8"), I_f, scale=8192.0)
    ms(ap("c35"), -3.5)
    act(ap("C15"), ap("c35"), bias=col("pcf", 5))
    ms(ap("c384"), 32.0 - 8192)
    act(ap("C21"), ap("C15"), bias=3.5 * (HALF - EXT) / 128, scale=(HALF - EXT) / 128)
    ms(ap("CT"), 0.0)
    act(ap("CT", 15, 128, 16), ap("DUM8"), bias=float(DUM), scale=-1.0)
    compute("V", "transpose", ap("CQ"), [ap("CT")], (ap("CQ"), ap("CT")), 1)
    act(ap("Town", ALL, 16), ap("DUM8"), bias=float(L))
    iota(ap("ik"), [[1, 8], [0, 17]], 1, 0)
    ts(ap("CK"), ap("ik"), 4352.0, A.mult, -8192.0, A.add)
    ts(ap("CK", 16, 136, 17), ap("ik", 0, 136, 17), 4352.0, A.mult)
    ms(ap("up"), 0.0)
    ms(ap("D2s"), 0.0)
    for r in range(RO):
        act(ap("D2s", 136 * r + 15, 136 * r + 136, 17), ap("DUM8"))
    ms(ap("sos", ALL, 16), 0.0)
    ms(ap("AJ", ALL, 16), 0.0)
    ms(ap("Z136"), 0.0)
    ms(ap("RR"), 0.0)
    if CFG["fl"]:
        ms(ap("FL", 16, 144), 0.0)
        ms(ap("FL", 0, 16), 0.0)
        ms(ap("FL", 0, 1), 1.0)
    ms(ap("MV", W, EXT), 0)
    ms(an("h", 0, 2), 0.0)
    for r in range(RO):
        ms(an("j", r, 2), 0.0)
    ms(col("eps", 0), 10.0 / 256)
    ts(less, col("cap32", 0), -1.0, A.mult, -ZO, A.add)
    ts(over, col("cap32", 0), ZO, A.add)

    def quarters(who, r, s, scale, bias):
        act(an(who, r, 1), s, bias=bias, scale=scale)
        act(an(who, r, 0), an(who, r, 1), bias=255.0, scale=-1.0)

    def turned(out, z, bias):
        p = ap(turn("#z"), 0, 128)
        mm(p, z, I_b)
        act(out, p, bias=bias)

    def spread(who, r, u, start, stop):
        b0, b1, _ = u
        j = b0 // 2
        rows = slice(32 * j, 32 * j + 32)
        lo, hi = 256 * (b0 - 2 * j), 256 * (b1 - 2 * j)
        z = ap("ZTj", rows=rows) if who == "j" else ap("ZT" + who, 128 * r, 128 * r + 128, rows=rows)
        p = ap(turn("#%s%d" % (who, b0)), 0, hi - lo)
        mm(p, z, ap("E32", lo, hi, rows=rows), start, stop)
        return p

    def limits(who, r, units):
        for u in units:
            if u[2] == "T":
                p = spread(who, r, u, True, True)
                act(ap("TH" + who, 256 * u[0], 256 * u[1]), p, bias=0.0 if who == "j" else over, scale=-1.0)

    def summed(who, r, u, offs):
        b0, b1, way = u
        src = ind(Xm, ap(offs, 128 * r + 16 * b0, 128 * r + 16 * b1))
        raw = ap("RA" + who, 256 * b0, 256 * b1)
        p = spread(who, r, u, True, False)
        if way == "V":
            if who == "j":
                cp(raw, src)
            else:
                ts(raw, src, less, A.add)
        else:
            act(raw, src, bias=0.0 if who == "j" else less)
        mm(p, I_b, raw, False, True)
        return p

    def judge_limits(r):
        ts(ap("zcl"), Zj, over, A.subtract, 1.0, A.min)
        turned(ap("ZTj"), ap("zcl"), 0.0)

    def judge_points(r):
        seg, bk = slice(4 * r, 4 * r + 4), turn("%t")
        p = ap(bk, slice(0, 4), ALL)
        g_ = [(p, I_b, ap("CQ")), (p, I_b, ap("C21"))]
        for h, (m0, m1) in enumerate([(ap("DE", 16, 144), ap("DE", 0, 128)), (ap("DO", 32, 160), ap("DO", 16, 144))]):
            o = ap(bk, slice(0, 4), slice(16 * h, 16 * h + 16))
            g_ += [(o, m0, ap("Tfj", seg, slice(0, 16))), (o, m1, ap("Tfj", seg, slice(16, 32)))]
        group(g_)
        o = ap("Town", ALL, slice(0, 16))
        compute("V", "transpose", o, [p], (o, p), 1)
        act(ap("DT"), ap("Town"))

    def new_points(r):
        o = ap(turn("#n"), 0, 128)
        group([(o, ap("I5"), ap("Tfj", slice(4 * r, 4 * r + 4), ALL)), (o, ap("BOb"), Zj)])
        ts(ap("tn"), o, 5 * HALF + 1 - 16 * ZO, A.add)
        ts(ap("MV", EXT, XW), ap("tn"), W - 1, A.bitwise_and)

    def halved(by, out, who, a, b):
        if who in CFG["tf"]:
            send(by, out, ap("Tfh", a, b))
        else:
            ts(out, ap("Tu" + who, a, b), -HALF, A.add)

    cp(ap("Tuh", 0, 128), ap("tr32"))
    ts(ap("Tfh", 0, 128), ap("tr32"), -HALF, A.add)
    turned(ap("ZTh", 0, 128), ap("Z0"), ZO)
    early = [send(SB, ap("ZTc", 0, 128), ap("ZTh", 0, 128)), send(SB, ap("Tuc", 0, 128), ap("Tuh", 0, 128))]
    if CFG["xa"] < W:
        dma("Y", ap("X", CFG["xa"], W), ap("sect", CFG["xa"], W), 1.7 + 2.8 * (1 - CFG["xa"] / W), [mark(early)])
    act(ap("Z1"), ap("Z0"), bias=ZO)
    send(SC, Zj, ap("Z1"))
    act(ap("X", EXT, XW), Zj, bias=ZO - 1, scale=-1.0)
    halved(SB, ap("Tfc", 0, 128), "c", 0, 128)
    quarters("h", 0, ap("Z0"), -0.25, 255.375)
    send(SB, ap("ANc", 0, 264), ap("ANh"))
    send(SC, ap("Tuj", 0, 128), ap("Tuh", 0, 128))
    halved(SC, ap("Tfj", slice(0, 4), ALL), "j", 0, 128)
    send(SC, ap("ANj", 0, 256), ap("ANh", 0, 256))
    early = mark([i for i, o in enumerate(ops) if o["kind"] == "send"])
    dma("Y", ap("MV", 0, Q), ap("mv"), 6.0, [early])
    dma("Y", ap("MV", Q, W), ap("mv"), 9.0, [early])
    limits("c", 0, CFG["cut"])
    judge_limits(0)

    for r in range(RO):
        R = 128 * r
        stage[0] = "c%d" % r
        for u in CFG["cut"]:
            b0, b1, way = u
            first[0] = ahead(b0)
            if way in "TA":
                if way == "T":
                    tt(ap("IC", 256 * b0, 256 * b1), ind(Xm, ap("Tuc", R + 16 * b0, R + 16 * b1)), ap("THc", 256 * b0, 256 * b1), A.is_gt)
                else:
                    step(ap("IC", 256 * b0, 256 * b1), summed("c", r, u, "Tuc"), -128.0)
                for b in range(b0, b1):
                    scan(ap("IM", b, ALL), ap("M16"), ap("IC", 256 * b, 256 * b + 256), 0.0, A.mult, A.max)
            else:
                p = summed("c", r, u, "Tuc")
                for b in range(b0, b1):
                    scan(ap("IM", b, ALL), ap(p[0], 256 * (b - b0), 256 * (b - b0) + 256), ap("U16"), 0.0, A.max, A.min)
        first[0] = 0
        act(ap("CB"), ap("C15"), bias=beta("c", r), scale=256.0)
        for c, (b0, b1) in enumerate(CH):
            if CFG["cp"] or not c:
                cnt = turn("#a%d" % c)
            o = ap(cnt, 16 * b0, 16 * b1)
            group([(o, ap("I32"), ap("CB", 16 * b0, 16 * b1))] +
                  [(o, ap("SW8", 15 - k, 143 - k), ap("IM", slice(b0, b1), slice(k, 256, 16))) for k in range(15)])
            if not (CFG["cp"] or c):
                continue
            a, b = 16 * b0 * CFG["cp"], 16 * b1
            first[0] = 1 - c
            o = ap(turn("#s"), a, b)
            mm(o, ap("Dt", 16, 144), ap("Tfc", R + a, R + b))
            act(ap("Tsh", a, b), o, bias=col("pcf", 7))
            y0, y1 = ap("Y", a, b), ap("Y", 128 + a, 128 + b)
            tt(y0, ap(cnt, a, b), ap("Tfc", R + a, R + b), A.min)
            tt(y1, ap(cnt, a, b), ap("Tsh", a, b), A.min)
            step(ap("fms", R + a, R + b), ap(cnt, a, b), 0.0, 1.0 / 32)
            place = lambda o: [(o, ap("BOb"), y0), (o, ap("nBO"), y1)]
            o = ap(turn("#p"), a, b)
            group([(o, I_b, ap("OD0", a, b))] + place(o))
            pl = turn("#q")
            group(place(ap(pl, a, b)))
            scan(ap("S0", a, b), ap("D0", a, b), o, col("S0", a - 1) if a else -1.0, A.max, A.min)
            pd = turn("#l")
            mm(ap(pd, a, b), I_b, ap("OD1", a, b), True, False)
            for x in place(ap(pd, a, b)):
                mm(*x, False, False)
            for s in range(b1):
                lo = max(a, 16 * s)
                e = ap("EQ", 128 * s + lo, 128 * s + b)
                tt(e, ap(pl, lo, b), ap("S0", lo - 16 * s, b - 16 * s), A.is_equal)
                mm(ap(pd, lo, b), ap("BO8"), e, False, s == b1 - 1)
            scan(ap("S1", a, b), ap("D0", a, b), ap(pd, a, b), -1.0, A.max, A.min)
        first[0] = 0
        new_points(r)
        judge_points(r)
        oc = ap("oc", 8 * r, 8 * r + 8)
        parts = [(0, CFG["cx"]), (CFG["cx"], 8)] if CFG["cx"] else [(0, 8)]
        for b0, b1 in parts:
            if CFG["cxo"] and not b0:
                cp(ap("po"), ap("S0", 15, 128, 16))
                tt(ap("tc"), ind(Xm, ap("po")), an("c", r, 1), A.min)
            if CFG["cxo"]:
                cp(ap("oc", 8 * r + b0, 8 * r + b1), ap("S1", 16 * b0 + 15, 16 * b1, 16))
                tt(ind(Xw, ap("oc", 8 * r + b0, 8 * r + b1)), ap("tc", 16 * b0, 16 * b1), ap("ANc", AW * r + 16 * b0, AW * r + 16 * b1), A.add)
                continue
            cp(ap("po", b0, b1), ap("S0", 16 * b0 + 15, 16 * b1, 16))
            tt(ap("tc", 16 * b0, 16 * b1), ind(Xm, ap("po", b0, b1)), ap("ANc", AW * r + 128 + 16 * b0, AW * r + 128 + 16 * b1), A.min)
            cp(ap("oc", 8 * r + b0, 8 * r + b1), ap("S1", 16 * b0 + 15, 16 * b1, 16))
            tt(ind(Xw, ap("oc", 8 * r + b0, 8 * r + b1)), ap("tc", 16 * b0, 16 * b1), ap("ANc", AW * r + 16 * b0, AW * r + 16 * b1), A.add)
        send(-SB, ap("fmh", R, R + 128), ap("fms", R, R + 128))
        send(SC - SB, ap("ocj", 8 * r, 8 * r + 8), oc)
        seg = slice(8 * r, 8 * r + 8)
        for c, (b0, b1) in enumerate(CH):
            bs, a, b = slice(b0, b1), 16 * b0, 16 * b1
            o = ap(turn("#f%d" % c), a, b)
            group([(o, ap("ZTc", R, R + 128), ap("Ib", a, b)), (o, I_b, ap("RAc", 16 * a + 15, 16 * b, 16)),
                   (o, ap("I8"), ap("IM", bs, slice(14, 256, 16))), (o, ap("I8"), ap("IM", bs, slice(15, 256, 16)))])
            step(ap("IM", bs, slice(15, 256, 16)), o, -128.0)
            o = ap(turn("#g%d" % c), a, b)
            group([(o, I_b, ap("c35", a, b))] + [(o, sel(x), ap("IM", bs, slice(16 * x, 16 * x + 16))) for x in range(16)])
            step(ap("sos", slice(8 * r + b0, 8 * r + b1), slice(0, 16)), o, beta("c", r))
            if CFG["so"] == 2 or c:
                s0 = b0 if CFG["so"] == 2 else 0
                send(SC - SB, ap("soj", 136 * r + 17 * s0, 136 * r + 17 * b1), ap("sos", slice(8 * r + s0, 8 * r + b1), ALL))
        o = ap(turn("#d"), 0, 8)
        group([(o, ap("I8"), ap("U16", 0, 8)), (o, ap("nI8"), ap("sos", seg, 15)), (o, I_f, ap("S1", 15, 128, 16))])
        tt(ap("D2s", 136 * r + 16, 136 * r + 136, 17), o, ap("DUM8"), A.min)
        send(SC - SB, ap("D2j", 136 * r, 136 * r + 136), ap("D2s", 136 * r, 136 * r + 136))

        stage[0] = "j%d" % r
        limits("h", r, CFG["home"])
        limits("j", r, CFG["judge"])
        for u in CFG["judge"]:
            b0, b1, way = u
            first[0] = ahead(b0)
            if way == "T":
                p = ap("RAj", 256 * b0, 256 * b1)
                tt(p, ind(Xm, ap("Tuj", R + 16 * b0, R + 16 * b1)), ap("THj", 256 * b0, 256 * b1), A.subtract)
            else:
                p = summed("j", r, u, "Tuj")
                if way == "A":
                    act(ap("THj", 256 * b0, 256 * b1), p)
                    p = ap("THj", 256 * b0, 256 * b1)
            ts(ap("AJ", slice(16 * b0, 16 * b1), slice(0, 16)), p, col("eps", r), A.max)
        told = 0
        for c, (b0, b1) in enumerate(CJ):
            a, b = 16 * b0, 16 * b1
            first[0] = len(CJ) - 1 - c
            w = lambda name, off=0: ap(name, 17 * b0 + off, 17 * b1 + off)
            o = ap(turn("#r%d" % c), 0, 17 * (b1 - b0))
            om, of = ap("om", 8 * c, 8 * c + b1 - b0), ap("of", 8 * c, 8 * c + b1 - b0)
            group([(o, I_b, w("CK"))] + [(o, sel(x), ap("AJ", slice(a + x, b, 16), ALL)) for x in range(16)] + [(o, ap("I8"), w("soj", 136 * r))])
            ts(w("t2"), o, MAG, A.add, -MAG, A.add)
            tt(o, w("t2"), o, A.is_le)
            tt(o, o, w("t2"), A.mult)
            scan(w("RR", c + 1), w("Z136"), o, 0.0, A.add, A.max)
            tt(w("NU"), o, w("RR", c), A.is_le)
            scan(w("UU"), w("NU"), w("DT"), 0.0, A.mult, A.add)
            cp(om, ap("UU", 17 * b0 + 16, 17 * b1, 17))
            cp(ap("Vus", R + a, R + b), ind(ap("MV"), om))
            send(-SC, ap("Vuh", R + a, R + b), ap("Vus", R + a, R + b))
            act(ap("Yg", a, b), ind(Xe, om), F.Abs, bias=0.5)
            if CFG["fl"]:
                ts(of, ap("UU", 17 * b0 + 16, 17 * b1, 17), EXT - 1.0, A.subtract)
                act(ap("ANj", AW * r + 264 + a, AW * r + 264 + b), ind(ap("FL"), of), accum=col("acc", c))
            else:
                act(ap("ANj", AW * r + 264 + a, AW * r + 264 + b), ind(Xe, om), F.Sigmoid, 128.0, 256.0, col("acc", c))
            if b1 in CFG["ap"] + (8,):
                send(-SC, ap("aph", 136 * r + told, 136 * r + 8 + b), ap("ANj", AW * r + 256 + told, AW * r + 264 + b))
                told = 8 + b
            if c and r + 1 < RO:
                act(col("acc", 0), col("acc", 0), bias=col("acc", c))
        first[0] = 0
        scan(ap("U2"), ap("NU"), ap("D2j", 136 * r, 136 * r + 136), 0.0, A.mult, A.max)
        cp(ap("osh"), ap("U2", 16, 136, 17))
        old = ind(Xw, ap("ocj", 8 * r, 8 * r + 8))
        if CFG["ts"]:
            sh = [ap("sh", 128 * k, 128 * k + 128) for k in range(3)]
            act(sh[0], old, bias=255.0, scale=-1.0)
            o = ap(turn("#u"), 0, 128)
            group([(o, ap("nIb"), an("j", r, 0)), (o, I_b, sh[0])])
            act(sh[1], o, F.Relu)
            act(sh[2], sh[1], bias=255.0, scale=-1.0)
            cp(ind(Xw, ap("osh")), sh[2])
            if r + 1 < RO:
                o = ap(turn("#v"), 0, 128)
                group([(o, I_b, an("j", r, 1)), (o, ap("nIb"), sh[1])])
                act(ap("ts"), o)
        else:
            tt(ap("ts"), old, an("j", r, 1), A.min)
            tt(ind(Xw, ap("osh")), ap("ts"), an("j", r, 0), A.add)
        n0 = R + 128
        if r + 1 < RO:
            o = ap(turn("#y"), 0, 128)
            group([(o, Zj, I_b), (o, ap("Yg"), I_b)])
            act(ap("ZTs", n0, n0 + 128), o, bias=ZO / 2 - 0.5, scale=0.5)
            send(SB - SC, ap("ZTc", n0, n0 + 128), ap("ZTs", n0, n0 + 128))
            send(-SC, ap("ZTh", n0, n0 + 128), ap("ZTs", n0, n0 + 128))
        o = ap(turn("#x"), 0, 128)
        group([(o, I_b, Zj), (o, I_b, ap("Yg"))])
        act(Zj, o, bias=ZO / 2 - 0.5, scale=0.5)
        if r + 1 < RO:
            act(ap("X", EXT, XW), Zj, bias=ZO - 1, scale=-1.0)
            quarters("j", r + 1, o, -0.125, ZO / 8 + 255.5)
            act(col("pt", 0), col("acc", 0), bias=143.75, scale=0.5)
            act(col("acc", 7), col("pt", 0), bias=col("acc", 0), scale=-2.0)
            act(beta("j", r + 1), col("acc", 7), bias=-288.0 * 256, scale=-256.0)
            act(col("eps", r + 1), col("acc", 7), bias=298.0 / 256, scale=1.0 / 256)
            send(SB - SC, ap("ANc", AW * (r + 1), AW * (r + 1) + 264), ap("ANj", AW * (r + 1), AW * (r + 1) + 264))
            judge_limits(r + 1)
        else:
            act(ap("zcl"), Zj, bias=-ZO)
            send(-SC, ap("Zy"), ap("zcl"))
            dma("Y", ap("ysect"), Xm, 4.5, [mark([i for i, o in enumerate(ops) if o["kind"] == "send" and o["round"] == r])])
            dma("Y", ap("yamt"), ap("Zy"), 2.0)

        stage[0] = "h%d" % r
        for u in CFG["home"]:
            b0, b1, way = u
            first[0] = ahead(b0)
            src, o = ind(Xm, ap("Vuh", R + 16 * b0, R + 16 * b1)), ap("IH", 256 * b0, 256 * b1)
            if way == "T":
                tt(o, src, ap("THh", 256 * b0, 256 * b1), A.is_gt)
            elif way == "C":
                p = spread("h", r, u, True, True)
                act(ap("RAh", 256 * b0, 256 * b1), src, bias=over, scale=-1.0)
                tt(o, p, ap("RAh", 256 * b0, 256 * b1), A.is_gt)
            else:
                step(o, summed("h", r, u, "Vuh"), -128.0)
        first[0] = 0
        if r + 1 < RO:
            limits("c", r + 1, CFG["cut"])
        for c, (b0, b1) in enumerate(CJ):
            a, b = 16 * b0, 16 * b1
            old, vf, bk, e = ap("Tfh", R + a, R + b), ap("Vf", a, b), turn("#w%d" % c), 2 * (b - a)
            first[0] = len(CJ) - 1 - c
            ts(vf, ap("Vuh", R + a, R + b), -HALF, A.add)
            group([(ap(bk, 0, e, 2), I_b, old), (ap(bk, 0, e, 2), ap("nIb"), vf)])
            mm(ap(bk, 1, e, 2), I_b, vf)
            o = ap(turn("#o%d" % c), a, b)
            group([(o, I_b, ap("c384", a, b)), (o, ap("n35"), ap("fmh", R + a, R + b))] +
                  [(o, sel(k), ap("IH", 16 * a + k, 16 * b, 16)) for k in range(16)] + [(o, ap("I8"), ap("aph", 136 * r + 8 + a, 136 * r + 8 + b))])
            step(ap("up", 2 * a + 1, 2 * b, 2), o, beta("h", r))
            scan(ap("tt", 2 * a, 2 * b), ap("up", 2 * a, 2 * b), ap(bk, 0, e), 0.0, A.mult, A.add)
            new = ap("tt", 2 * a + 1, 2 * b, 2)
            if r + 1 < RO:
                u_ = ap("Tuh", R + 128 + a, R + 128 + b)
                ts(u_, new, HALF, A.add)
                send(SB, ap("Tuc", R + 128 + a, R + 128 + b), u_)
                act(ap("Tfh", R + 128 + a, R + 128 + b), new)
                if CFG["cp"] and b1 in (CFG["ch"], 8):
                    a = 16 * CFG["ch"] * (b1 == 8)
                    halved(SB, ap("Tfc", R + 128 + a, R + 128 + b), "c", R + 128 + a, R + 128 + b)
            else:
                act(ap("To", a, b), new, bias=HALF)
                dma("S" if c == len(CJ) - 1 else "Y", ap("ytraj", a, b), ap("To", a, b), 2.0)
        first[0] = 0
        if r + 1 < RO:
            if not CFG["cp"]:
                halved(SB, ap("Tfc", R + 128, R + 256), "c", R + 128, R + 256)
            send(SC, ap("Tuj", R + 128, R + 256), ap("Tuh", R + 128, R + 256))
            halved(SC, ap("Tfj", slice(4 * r + 4, 4 * r + 8), ALL), "j", R + 128, R + 256)
            cp(ind(Xw, ap("osh")), ap("ts"))
    return ops


def gap(ops, d, i):
    a, b = ops[d], ops[i]
    if d in b["free"]:
        return a["cost"]
    return a["cost"] + a["lat"] + (b["same"] if a["eng"] == b["eng"] and not a["lat"] else b["hop"])


def order(ops):
    n = len(ops)
    users = [[] for _ in range(n)]
    for i, o in enumerate(ops):
        for d in o["deps"]:
            users[d].append(i)
    hop = lambda d, i: gap(ops, d, i) - ops[d]["cost"] - ops[d]["lat"]
    way = [0.0] * n
    for i in range(n - 1, -1, -1):
        way[i] = max([ops[i]["cost"] + ops[i]["lat"]] + [way[u] + gap(ops, i, u) for u in users[i]])
    way = [w + CFG["first"] * o["first"] for o, w in zip(ops, way)]
    left = [len(o["deps"]) for o in ops]
    ready, end, free = [0.0] * n, [0.0] * n, {}
    pool = {}
    for i in range(n):
        if not left[i]:
            pool.setdefault(ops[i]["eng"], []).append(i)
    seq = []
    while len(seq) < n:
        best = None
        for e, cand in pool.items():
            if cand:
                t = max(free.get(e, 0.0), min(ready[i] for i in cand))
                i = max((i for i in cand if ready[i] <= t + LOOK), key=lambda i: (way[i], -i))
                soon = [j for j in cand if t + LOOK < ready[j] < t + ops[i]["cost"]]
                if soon:
                    j = max(soon, key=lambda j: way[j])
                    if max(ready[j] + way[j], ready[j] + ops[j]["cost"] + way[i]) < max(t + way[i], t + ops[i]["cost"] + way[j]):
                        i, t = j, ready[j]
                if best is None or t < best[0]:
                    best = (t, e, i)
        t, e, i = best
        t = max(t, ready[i])
        pool[e].remove(i)
        free[e] = t + ops[i]["cost"]
        end[i] = free[e] + ops[i]["lat"]
        seq.append((i, t))
        for u in users[i]:
            ready[u] = max(ready[u], end[i] + hop(i, u))
            left[u] -= 1
            if not left[u]:
                pool.setdefault(ops[u]["eng"], []).append(u)
    return seq, max(end)


def squeeze(ops, seq, turns, late=False, seed=0):
    n = len(ops)
    cost, lat, eng = [o["cost"] for o in ops], [o["lat"] for o in ops], [o["eng"] for o in ops]
    hop = lambda d, i: gap(ops, d, i) - cost[d] - lat[d]
    fwd = [[(d, cost[d] + lat[d] + hop(d, i)) for d in o["deps"]] for i, o in enumerate(ops)]
    bwd = [[] for _ in range(n)]
    for i, o in enumerate(ops):
        for d in o["deps"]:
            bwd[d].append((i, cost[i] + lat[d] + hop(d, i)))

    def pack(rank, before, least):
        left = [len(b) for b in before]
        after = [[] for _ in range(n)]
        for i, b in enumerate(before):
            for d, _ in b:
                after[d].append(i)
        free = sorted((-rank[i], -i) for i in range(n) if not left[i])
        at, busy = [0.0] * n, {e: [] for e in eng}
        while free:
            i = -free.pop()[1]
            t = least[i]
            for d, w in before[i]:
                if at[d] + w > t:
                    t = at[d] + w
            b = busy[eng[i]]
            k = len(b)
            while k and b[k - 1][1] > t:
                k -= 1
            while k < len(b) and b[k][0] < t + cost[i] - 1e-9:
                t = max(t, b[k][1])
                k += 1
            b.insert(k, (t, t + cost[i]))
            at[i] = t
            for u in after[i]:
                left[u] -= 1
                if not left[u]:
                    x_, k = (-rank[u], -u), len(free)
                    while k and free[k - 1] > x_:
                        k -= 1
                    free.insert(k, x_)
        return at

    x, at, best, keep = 777 + seed, [0.0] * n, 1e9, None
    for i, t in seq:
        at[i] = t
    keys = sorted(set(o["key"] for o in ops))
    for it in range(turns):
        nudge = {}
        for k in keys:
            x = (x * 6364136223846793005 + 1442695040888963407) % (1 << 64)
            nudge[k] = NUDGE * ((x >> 33) % 1000 / 1000 - 0.5) if (x >> 20) % 8 == 0 else 0.0
        back = pack([-(at[i] + cost[i]) + nudge[ops[i]["key"]] for i in range(n)], bwd, lat)
        now = pack([-(back[i] + cost[i]) for i in range(n)], fwd, [0.0] * n)
        t = max(now[i] + cost[i] + lat[i] for i in range(n))
        if t < best + SLACK:
            at = now
        if t < best:
            best, keep = t, now
    if late:
        back = pack([-(keep[i] + cost[i]) for i in range(n)], bwd, lat)
        back = [best - back[i] - cost[i] for i in range(n)]
        least, opener = [0.0] * n, {}
        for i, o in enumerate(ops):
            for name in o["turns"]:
                if opener.setdefault(name, i) not in (i, None):
                    least[opener[name]] = back[i] - cost[opener[name]] - hop(opener[name], i) - EARLY
                    opener[name] = None
        keep = pack([max(back[i], least[i]) for i in range(n)], fwd, least)
    return sorted(((i, keep[i]) for i in range(n)), key=lambda p: (p[1], p[0])), best


def bind(ops, seq):
    at = dict(seq)
    users, after = {}, [set() for _ in ops]
    for i, o in enumerate(ops):
        for d in o["deps"]:
            after[d].add(i)
    for i, _ in seq:
        for name in ops[i]["turns"]:
            users.setdefault(name, []).append(i)
    pieces = lambda o: [x for a in [o["args"]] + o.get("more", []) for x in a if isinstance(x, tuple) and is_psum(x)]
    held, where = {"B%d" % k: (-1.0 - k, []) for k in range(8)}, {}
    for name, us in users.items():
        cols = [x[1][1] for i in us for x in pieces(ops[i]) if x[0] == name]
        narrow = name[0] == "%" or all(ops[i]["kind"] != "tensor_tensor_scan" for i in us) and all(
            c.step is None and c.start % 16 == c.stop % 16 == 0 and c.stop <= 256 for c in cols)
        banks = ["B7"] if name[0] == "%" else [b for b in held if b != "B7" or narrow]
        below, todo = set(us), list(us)
        while todo:
            for i in after[todo.pop()] - below:
                below.add(i)
                todo.append(i)
        b = min((b for b in banks if not below & set(held[b][1])), key=lambda b: (held[b][0] > at[us[0]], b != "B7", held[b][0]))
        ops[us[0]]["deps"] |= set(held[b][1])
        for i in held[b][1]:
            after[i].add(us[0])
        ops[us[0]]["free"] |= set(i for i in held[b][1] if ops[i]["eng"] == "P")
        held[b], where[name] = (max(at[i] + ops[i]["cost"] for i in us) + COST["hop"], us), b

    def moved(x):
        if not (isinstance(x, tuple) and is_psum(x)):
            return x
        if where[x[0]] == "B7" and x[0][0] == "#":
            return ("B7", (x[1][0], slice(x[1][1].start // 16, x[1][1].stop // 16), slice(0, 16)))
        return (where[x[0]], x[1])

    for o in ops:
        o["args"] = tuple(moved(x) for x in o["args"])
        o["more"] = [tuple(moved(x) for x in a) for a in o.get("more", [])]


def replay(ops, seq, costs):
    start, free = {}, {}
    for i, _ in seq:
        o = ops[i]
        costs[i]["free"] = o["free"]
        start[i] = max([free.get(o["eng"], 0.0)] + [start[d] + gap(costs, d, i) for d in o["deps"]])
        free[o["eng"]] = start[i] + costs[i]["cost"]
    return max(start[i] + costs[i]["cost"] + costs[i]["lat"] for i in start)


def schedule(turns, tries):
    base, others = dict(COST), []
    for m in SPREAD:
        COST.update(m)
        others.append(plan())
        COST.update(base)
        for o in others[-1]:
            if o["kind"] == "send":
                o["lat"] += m.get("odd", 0.0) * (sum(map(ord, o["key"])) * (7 + len(others)) % 11 / 10 - 0.3)
    ops = plan()
    seq, best = squeeze(ops, order(ops)[0], turns)[0], None
    for k in range(tries):
        mine = plan()
        late = squeeze(ops, seq, turns // 8, True, k)[0]
        bind(mine, late)
        late = squeeze(mine, late, turns // 4, False, k)[0]
        t = sum(replay(mine, late, p) / replay(ops, seq, p) for p in others)
        if best is None or t < best[0]:
            best = (t, mine, late)
    _, mine, late = best
    for p in others:
        for o, m in zip(p, mine):
            o["deps"], o["free"] = m["deps"], m["free"]
    late = anneal(others, late, MOVES, alike=False)[0]
    return mine, late, replay(mine, late, ops)


def anneal(plans, seq, steps, heat=0.15, seed=4321, alike=True):
    ops = plans[0]
    n = len(ops)
    eng = [o["eng"] for o in ops]
    names = sorted(set(eng))
    en = [names.index(e) for e in eng]
    deps = [sorted(o["deps"]) for o in ops]
    costs = [[o["cost"] for o in p] for p in plans]
    tails = [[o["cost"] + o["lat"] for o in p] for p in plans]
    waits = [[[(d, gap(p, d, i)) for d in deps[i]] for i in range(n)] for p in plans]
    at = [0.0] * n
    for i, t in seq:
        at[i] = t
    key = [o["unit"] if alike else (o["unit"], o["round"]) for o in ops]
    mid = {}
    for i, o in enumerate(ops):
        mid.setdefault(o["unit"], {}).setdefault(o["round"], at[i])
    gaps = [m[1] - m[0] for m in mid.values() if 0 in m and 1 in m]
    period = sorted(gaps)[len(gaps) // 2] if alike else 0.0
    place = {}
    for i, o in enumerate(ops):
        r = 1 if alike and 1 in mid[o["unit"]] else o["round"]
        place.setdefault(key[i], mid[o["unit"]][r] - period * r)
    key, place, off = list(range(n)), {i: t + 1e-6 * p for p, (i, t) in enumerate(seq)}, [0.0] * n

    def times():
        v = [0.0] * n
        for i, _ in seq:
            x = place[key[i]] + off[i]
            for d in deps[i]:
                if v[d] >= x:
                    x = v[d] + 1e-7
            v[i] = x
        line = sorted(range(n), key=lambda i: v[i])
        total, held = 0.0, []
        for cost, tail, wait in zip(costs, tails, waits):
            start, by, free, prev = [0.0] * n, [-1] * n, [0.0] * len(names), [-1] * len(names)
            end, last = 0.0, -1
            for i in line:
                e = en[i]
                t, b = free[e], -2 - prev[e]
                for d, w in wait[i]:
                    if start[d] + w > t:
                        t, b = start[d] + w, d
                start[i], by[i] = t, b
                free[e], prev[e] = t + cost[i], i
                if t + tail[i] > end:
                    end, last = t + tail[i], i
            total += end
            while last != -1:
                b = by[last]
                if b < -1:
                    b = -2 - b
                    if key[b] != key[last]:
                        held.append((b, last))
                last = b
        return total / len(plans), held, v, start

    x = [seed]

    def draw():
        x[0] = (x[0] * 6364136223846793005 + 1442695040888963407) % (1 << 64)
        return (x[0] >> 33) / float(1 << 31)

    cur, held, v, start = times()
    best, keep = cur, v
    for it in range(steps):
        if held and draw() < 0.7:
            a, b = held[int(draw() * len(held))]
            k, to = (key[b], v[a] - off[b] - draw() ** 2) if draw() < 0.5 else (key[a], v[b] - off[a] + draw() ** 2)
        else:
            k = key[int(draw() * n)]
            to = place[k] + 2 * (draw() - 0.5)
        old = place[k]
        place[k] = to
        t, h, w, s = times()
        if t <= cur + heat * (1 - it / steps) * draw():
            cur, held, v = t, h, w
            if t < best:
                best, keep = t, w
        else:
            place[k] = old
    return sorted(((i, keep[i]) for i in range(n)), key=lambda p: (p[1], p[0])), best


CACHE = {}


def rank_program(g, core, T, topo):
    rank = T.rank_of(core)
    if rank is None:
        return
    if not CACHE:
        CACHE["ops"], CACHE["seq"], _ = schedule(STEPS, TRIES)
    ops, seq = CACHE["ops"], CACHE["seq"]
    queue = {"V": g.vector, "S": g.scalar, "P": g.tensor, "G": g, "Y": g.sync}

    def res(x):
        if not isinstance(x, tuple):
            return x
        if x[0] == "*":
            return res(x[1]).indirect(res(x[2]))
        return T[x[0]][x[1]]

    place, waits, seen, knew = {i: p for p, (i, _) in enumerate(seq)}, {}, {e: {} for e in queue}, {}
    for i, _ in seq:
        mine, waits[i] = seen[ops[i]["eng"]], []
        for d in sorted(ops[i]["deps"] - ops[i]["free"], key=lambda d: -place[d]):
            s = d if ops[d]["kind"] in ("dma", "send", "mark") else ops[d]["eng"]
            if mine.get(s, -1) < place[d]:
                waits[i].append(d)
                mine[s] = place[d]
                if ops[d]["kind"] not in ("send", "mark"):
                    mine.update((k, v) for k, v in knew[d].items() if mine.get(k, -1) < v)
        knew[i] = dict(mine)
    told = set(d for w in waits.values() for d in w)

    token, count = {}, {"V": 0, "S": 0, "P": 0, "G": 0}
    nd, nm, sent, marks = 0, 0, 0, 0
    for i, _ in seq:
        o = ops[i]
        e, q, a = o["eng"], queue[o["eng"]], o["args"]
        for d in waits[i]:
            q.wait_ge(T.sem[token[d][0][0]], token[d][0][1])
        k = o["kind"]
        if k == "dma":
            token[i] = [("d%d" % nd, 16)]
            q.dma_start(res(a[0]), res(a[1])).then_inc(T.sem["d%d" % nd], 16)
            nd += 1
        elif k == "mark":
            marks += 1
            g.sem_inc(T.sem.mark, 1)
            token[i] = [("mark", marks)]
        elif k == "send":
            dst, src = T.cores[(rank + a[0]) % N], T.cores[(rank - a[0]) % N]
            rid, pid, _ = topo.addr(dst)
            g.remote_dma(res(a[1]), res(a[2]), T.sem["m%d" % nm], T.sem.sent, pid, rid, topo.mask(core, dst))
            token[i] = [("m%d" % nm, len(topo.engines(src, core)))]
            sent += len(topo.engines(core, dst))
            nm += 1
        else:
            r = [res(x) for x in a]
            if k == "activation":
                ins = q.activation(r[0], r[1], r[2], bias=r[3], scale=r[4], accum_out=r[5])
            elif k == "matmul":
                ins = q.matmul(*r)
                for m in o["more"]:
                    ins = q.matmul(*[res(x) for x in m])
            elif k == "iota":
                ins = q.iota(*r, allow_small_or_imprecise_dtypes=SCRATCH[a[0][0]][2] != i32)
            elif k == "tensor_copy":
                ins = q.tensor_copy(*r)
            elif k == "tensor_tensor":
                ins = q.tensor_tensor(*r)
            elif k == "tensor_scalar":
                ins = q.tensor_scalar(*r)
            elif k == "tensor_tensor_scan":
                ins = q.tensor_tensor_scan(*r)
            elif k == "transpose":
                ins = q.transpose(*r)
            else:
                ins = q.memset(*r)
            if i in told:
                count[e] += 1
                ins.then_inc(T.sem[e], 1)
                token[i] = [(e, count[e])]
    for e, v in count.items():
        if v:
            g.wait_ge(T.sem[e], v)
    g.wait_ge(T.sem.sent, sent)
    for i, o in enumerate(ops):
        if o["kind"] in ("dma", "send"):
            g.wait_ge(T.sem[token[i][0][0]], token[i][0][1])
